import numpy as np
import ml_dtypes


def mxq(x, axis, fmt="e4m3"):
    dtype, down = {"e4m3": (ml_dtypes.float8_e4m3fn, 7), "e5m2": (ml_dtypes.float8_e5m2, 14)}[fmt]
    v = np.moveaxis(np.asarray(x, np.float32).astype(ml_dtypes.bfloat16).astype(np.float64), axis, -1)
    blocks = v.reshape(v.shape[:-1] + (-1, 32))
    amax = np.abs(blocks).max(-1, keepdims=True)
    byte = np.maximum(np.where(amax > 0, np.frexp(amax)[1] - 1 + 127, 0) - down, 1)
    scale = np.exp2(byte - 127.0)
    codes = (blocks / scale).astype(np.float32).astype(dtype).astype(np.float64)
    return np.moveaxis((codes * scale).reshape(v.shape), -1, axis)


WIDE = False


def mx_kscale(k):
    if not WIDE:
        return np.ones(k)
    levels = np.array([10, -10, 5, -5, 0])
    if k % 512:
        return np.exp2(np.random.permutation(np.resize(levels, k // 32))).repeat(32)
    a = np.empty((k // 512, 16))
    for p in range(k // 512):
        a[p, :8] = np.random.permutation(np.resize(levels, 8))
        for g in range(8):
            far = levels[np.abs(levels - a[p, g]) >= 10]
            a[p, g + 8] = far[np.random.randint(len(far))]
    return np.exp2(a.ravel()).repeat(32)


def f64(x):
    return np.asarray(x).astype(np.float64)


def striped(idx):
    return np.tile(idx.reshape(-1, 16).T, (8, 1)).astype(np.uint16)


def unstriped(offs):
    return offs[:16].T.reshape(-1).astype(np.int64)


def relu(v):
    return np.maximum(v, 0.0)


K, T, E, C, H, N = 1536, 1024, 2, 256, 512, 128


def by_expert(wq, xq):
    return np.concatenate([wq[e].T @ xq[:, e * C:(e + 1) * C] for e in range(E)], axis=1)


def setup_inputs():
    n = np.random.standard_normal
    s = mx_kscale(K)[:, None]
    u = mx_kscale(H)
    return {
        "xT": (n((K, T)) * s).astype(np.float32),
        "w1": (n((E, K, H)) / np.sqrt(K) / s[None]).astype(np.float32),
        "w3": (n((E, K, H)) / np.sqrt(K) / s[None] * u[None, None, :]).astype(np.float32),
        "w2": (n((E, H, N)) / np.sqrt(H) / u[None, :, None]).astype(np.float32),
        "gate": np.tile(np.random.uniform(0.2, 1.0, E * C), (N, 1)).astype(np.float32),
        "offs": striped(np.random.permutation(T)[:E * C]),
    }


def reference(xT, w1, w3, w2, gate, offs):
    idx = unstriped(offs)
    xq = mxq(f64(xT)[:, idx], 0, "e4m3")
    h = relu(by_expert(mxq(f64(w1), 1, "e4m3"), xq))
    h = h * by_expert(mxq(f64(w3), 1, "e4m3"), xq)
    y = by_expert(mxq(f64(w2), 1, "e4m3"), mxq(h, 0, "e4m3"))
    out = np.zeros((N, T))
    out[:, idx] = f64(gate) * y
    return out

@@ -1,0 +1,188 @@
+from contextlib import ExitStack
+
+import concourse.mybir as mybir
+
+K, T, E, C, H, N = 1536, 1024, 2, 256, 512, 128
+FLOPS = 2 * E * C * (2 * K * H + H * N)
+
+F32 = mybir.dt.float32
+BF16 = mybir.dt.bfloat16
+U32 = mybir.dt.uint32
+U16 = mybir.dt.uint16
+U8 = mybir.dt.uint8
+FP8X4 = mybir.dt.float8_e4m3fn_x4
+MULT = mybir.AluOpType.mult
+RELU = mybir.ActivationFunctionType.Relu
+
+P = 128
+J = 4
+PASS = P * J
+PASSES = K // PASS
+SLOTS = E * C
+HALF_T = T // 2
+QUAD = 4
+
+X_CUT = 512
+L_CUT = 24
+W_CUT = 20
+CHUNKS = [(m, g) for g in range(PASSES) for m in range(2)]
+LAST = (E - 1, 1, PASSES - 1)
+PARTS = (1, 2)
+
+
+def tile_routed_moe_kernel(tc, xT, w1, w3, w2, gate, offs, out):
+    nc = tc.nc
+    xT_view = xT.rearrange("(g p j) n -> g p j n", p=P, j=J)
+    w_views = [w.rearrange("e (g p j) n -> e g p j n", p=P, j=J) for w in (w1, w3)]
+    w2_view = w2.rearrange("e (v t r) n -> e r v t n", t=QUAD, r=QUAD)
+
+    def token_source(ap):
+        return ap.rearrange("p j (c i) -> p c j i", i=QUAD)
+
+    def token_target(ap):
+        return ap.rearrange("p (c i j) -> p c j i", i=QUAD, j=J)
+
+    def weight_source(ap):
+        return ap.rearrange("p j (v t r) -> p t v j r", t=QUAD, r=QUAD)
+
+    def weight_target(ap):
+        return ap.rearrange("p (t v r j) -> p t v j r", t=QUAD, r=QUAD, j=J)
+
+    with ExitStack() as ctx:
+        keep = ctx.enter_context(tc.tile_pool(name="keep", bufs=1))
+        raws = ctx.enter_context(tc.tile_pool(name="raws", bufs=7))
+        stage = ctx.enter_context(tc.tile_pool(name="stage", bufs=3))
+        small = ctx.enter_context(tc.tile_pool(name="small", bufs=2))
+        psum = ctx.enter_context(tc.psum_pool(name="psum", bufs=8))
+
+        offsets = keep.tile([P, SLOTS // 16], U16, name="offsets")
+        window = keep.tile([P, T], F32, name="window")
+        nc.vector.memset(window[:], 0.0)
+
+        x_raw = {}
+        w_raw = {}
+        w2_raw = {}
+        gates = {}
+        for g in range(PASSES):
+            x_raw[g] = raws.tile([P, J, T], F32, name="x_raw", bufs=3)
+            nc.sync.dma_start(out=x_raw[g][:], in_=xT_view[g])
+            if g == 0:
+                nc.sync.dma_start(offsets[:], offs)
+        def load_w2(e):
+            w2_raw[e] = keep.tile([P, J, N], F32, name=f"w2_raw{e}")
+            for r in range(QUAD):
+                nc.sync.dma_start(out=w2_raw[e][r:P:QUAD], in_=w2_view[e, r])
+
+        def load_gate(e):
+            gates[e] = keep.tile([P, C], F32, name=f"gates{e}")
+            nc.sync.dma_start(out=gates[e][:], in_=gate[:, e * C : (e + 1) * C])
+
+        for e in range(E):
+            for i in range(len(CHUNKS)):
+                m, g = CHUNKS[i]
+                if (e, i) == (1, 1):
+                    load_w2(0)
+                if (e, i) == (1, 3):
+                    load_gate(0)
+                if (e, m, g) == LAST:
+                    for q in range(2):
+                        tile = raws.tile([P, J, H // 2], F32, name="raw_half", bufs=2)
+                        nc.sync.dma_start(out=tile[:], in_=w_views[m][e, g, :, :, q * H // 2 : (q + 1) * H // 2])
+                        w_raw[e, m, g, q] = tile
+                else:
+                    tile = raws.tile([P, J, H], F32, name="raw")
+                    nc.sync.dma_start(out=tile[:], in_=w_views[m][e, g])
+                    w_raw[e, m, g] = tile
+        load_w2(E - 1)
+        load_gate(E - 1)
+
+        x_words = {}
+        s_words = {}
+        x_bytes = keep.tile([P, T], U8, name="x_bytes", align_bytes=64)
+        s_bytes = keep.tile([P, SLOTS], U8, name="s_bytes", align_bytes=64)
+        for g in range(PASSES):
+            x_words[g] = keep.tile([P, T], U32, name=f"x_words{g}", align_bytes=64)
+            s_words[g] = keep.tile([P, SLOTS], U32, name=f"s_words{g}", align_bytes=64)
+            grouped = stage.tile([P, T * J], BF16, name="grouped", align_bytes=64, bufs=2)
+            target = token_target(grouped[:])
+            source = token_source(x_raw[g][:])
+            nc.scalar.copy(target[:, : X_CUT // QUAD], source[:, : X_CUT // QUAD])
+            nc.vector.tensor_copy(target[:, X_CUT // QUAD :], source[:, X_CUT // QUAD :])
+            for half in range(2):
+                cols = slice(half * HALF_T, (half + 1) * HALF_T)
+                nc.vector.quantize_mx(
+                    out=x_words[g][:, cols].bitcast(FP8X4),
+                    scales=x_bytes[4 * g :, cols],
+                    in_=grouped[:, J * cols.start : J * cols.stop],
+                )
+            nc.vector.tensor_copy(s_words[g][:], x_words[g][:].indirect(offsets[:]))
+        nc.vector.tensor_copy(s_bytes[:], x_bytes[:].indirect(offsets[:]))
+
+        for e in range(E):
+            banks = {}
+            gated = small.tile([P, 4, C], F32, name="gated")
+            for m, g in CHUNKS:
+                words = keep.tile([P, H], U32, name=f"w_words{e}{m}{g}", align_bytes=64)
+                scales = keep.tile([P, H], U8, name=f"w_bytes{e}{m}{g}", align_bytes=64)
+                grouped = stage.tile([P, H * J], BF16, name="w_grouped", align_bytes=64, bufs=5)
+                target = weight_target(grouped[:])
+                if (e, m, g) == LAST:
+                    pieces = [(w_raw[e, m, g, q], 16 * q, 16 * q + L_CUT // 4, 16 * (q + 1)) for q in range(2)]
+                else:
+                    pieces = [(w_raw[e, m, g], 0, W_CUT, 32)]
+                for raw, v0, v1, v2 in pieces:
+                    source = weight_source(raw[:])
+                    nc.scalar.copy(target[:, :, v0:v1], source[:, :, : v1 - v0])
+                    nc.vector.tensor_copy(target[:, :, v1:v2], source[:, :, v1 - v0 :])
+                nc.vector.quantize_mx(out=words[:].bitcast(FP8X4), scales=scales[:], in_=grouped[:])
+                for t in range(4):
+                    cols = slice(128 * t, 128 * (t + 1))
+                    if g == 0:
+                        banks[m, t] = psum.tile([P, C], F32, name="bank")
+                    nc.tensor.matmul_mx(
+                        out=banks[m, t][:],
+                        lhsT=words[:, cols].bitcast(FP8X4),
+                        lhsT_scale=scales[:, cols],
+                        rhs=s_words[g][:, e * C : (e + 1) * C].bitcast(FP8X4),
+                        rhs_scale=s_bytes[4 * g :, e * C : (e + 1) * C],
+                        start=(g == 0),
+                        stop=(g == PASSES - 1),
+                    )
+                    if m == 0 and g == PASSES - 1:
+                        nc.scalar.activation(gated[:, t, :], banks[m, t][:], RELU)
+
+            w2_grouped = small.tile([P, N * J], BF16, name="w2_grouped", align_bytes=64)
+            w2_words = small.tile([P, N], U32, name="w2_words", align_bytes=64)
+            w2_bytes = small.tile([P, N], U8, name="w2_bytes", align_bytes=64)
+            nc.scalar.copy(token_target(w2_grouped[:]), token_source(w2_raw[e][:]))
+            nc.vector.quantize_mx(out=w2_words[:].bitcast(FP8X4), scales=w2_bytes[:], in_=w2_grouped[:])
+
+            product = small.tile([P, 4, C], BF16, name="product")
+            for t in range(4):
+                nc.vector.tensor_tensor(product[:, t, :], banks[1, t][:], gated[:, t, :], MULT)
+            size = C // PARTS[e]
+            for b in range(PARTS[e]):
+                part = slice(b * size, (b + 1) * size)
+                h = small.tile([P, size * J], BF16, name="h", align_bytes=64)
+                interleave = nc.vector.tensor_copy if b == 0 else nc.scalar.copy
+                interleave(token_target(h[:]), token_source(product[:, :, part]))
+                h_words = small.tile([P, size], U32, name="h_words", align_bytes=64)
+                h_bytes = small.tile([P, size], U8, name="h_bytes", align_bytes=64)
+                nc.vector.quantize_mx(out=h_words[:].bitcast(FP8X4), scales=h_bytes[:], in_=h[:])
+                y_bank = psum.tile([P, size], F32, name="bank")
+                nc.tensor.matmul_mx(
+                    out=y_bank[:],
+                    lhsT=w2_words[:].bitcast(FP8X4),
+                    lhsT_scale=w2_bytes[:],
+                    rhs=h_words[:].bitcast(FP8X4),
+                    rhs_scale=h_bytes[:],
+                    start=True,
+                    stop=True,
+                )
+                y = small.tile([P, size], F32, name="y")
+                nc.scalar.copy(y[:], y_bank[:])
+                first = (e * C + part.start) // 16
+                nc.vector.tensor_tensor(
+                    window[:].indirect(offsets[:, first : first + size // 16]), y[:], gates[e][:, part], MULT
+                )
+        nc.sync.dma_start(out=out, in_=window[:])

@@ -1,6 +1,7 @@
 from contextlib import ExitStack
 
 import concourse.mybir as mybir
+from concourse.masks import make_identity
 
 K, T, E, C, H, N = 1536, 1024, 2, 256, 512, 128
 FLOPS = 2 * E * C * (2 * K * H + H * N)
@@ -21,80 +22,98 @@ PASSES = K // PASS
 SLOTS = E * C
 HALF_T = T // 2
 QUAD = 4
+GROUPS = C // P
 
 X_CUT = 512
+W_CUT = 36
 L_CUT = 24
-W_CUT = 20
-CHUNKS = [(m, g) for g in range(PASSES) for m in range(2)]
+A_CUT = 44
+B_CUT = 28
+R_CUT = 44
+Q_CUT = 32
 LAST = (E - 1, 1, PASSES - 1)
-PARTS = (1, 2)
+WHOLE = ((0, H),)
+LAST_LOADS = ((0, 256), (256, 512))
+LAST_BANKS = ((0, 256), (256, 512))
 
 
 def tile_routed_moe_kernel(tc, xT, w1, w3, w2, gate, offs, out):
     nc = tc.nc
     xT_view = xT.rearrange("(g p j) n -> g p j n", p=P, j=J)
     w_views = [w.rearrange("e (g p j) n -> e g p j n", p=P, j=J) for w in (w1, w3)]
-    w2_view = w2.rearrange("e (v t r) n -> e r v t n", t=QUAD, r=QUAD)
+    w2_view = w2.rearrange("e (p j) n -> e p j n", j=J)
 
-    def token_source(ap):
+    def rows(ap):
         return ap.rearrange("p j (c i) -> p c j i", i=QUAD)
 
-    def token_target(ap):
+    def side_by_side(ap):
         return ap.rearrange("p (c i j) -> p c j i", i=QUAD, j=J)
 
-    def weight_source(ap):
-        return ap.rearrange("p j (v t r) -> p t v j r", t=QUAD, r=QUAD)
+    def by_word(ap):
+        return ap.rearrange("s (w u b) -> s u w b", u=2, b=2)
 
-    def weight_target(ap):
-        return ap.rearrange("p (t v r j) -> p t v j r", t=QUAD, r=QUAD, j=J)
+    def word_major(ap):
+        return ap.rearrange("s (u w b) -> s u w b", u=2, b=2)
+
+    def round_and_interleave(grouped, raw, cut):
+        target = side_by_side(grouped)
+        source = rows(raw)
+        nc.scalar.copy(target[:, : cut // QUAD], source[:, : cut // QUAD])
+        nc.vector.tensor_copy(target[:, cut // QUAD :], source[:, cut // QUAD :])
 
     with ExitStack() as ctx:
         keep = ctx.enter_context(tc.tile_pool(name="keep", bufs=1))
-        raws = ctx.enter_context(tc.tile_pool(name="raws", bufs=7))
-        stage = ctx.enter_context(tc.tile_pool(name="stage", bufs=3))
+        stage = ctx.enter_context(tc.tile_pool(name="stage", bufs=4))
         small = ctx.enter_context(tc.tile_pool(name="small", bufs=2))
         psum = ctx.enter_context(tc.psum_pool(name="psum", bufs=8))
 
         offsets = keep.tile([P, SLOTS // 16], U16, name="offsets")
         window = keep.tile([P, T], F32, name="window")
+        identity = keep.tile([P, P], F32, name="identity")
         nc.vector.memset(window[:], 0.0)
+        make_identity(nc, identity[:])
 
         x_raw = {}
         w_raw = {}
         w2_raw = {}
         gates = {}
-        for g in range(PASSES):
-            x_raw[g] = raws.tile([P, J, T], F32, name="x_raw", bufs=3)
-            nc.sync.dma_start(out=x_raw[g][:], in_=xT_view[g])
-            if g == 0:
-                nc.sync.dma_start(offsets[:], offs)
+
         def load_w2(e):
             w2_raw[e] = keep.tile([P, J, N], F32, name=f"w2_raw{e}")
-            for r in range(QUAD):
-                nc.sync.dma_start(out=w2_raw[e][r:P:QUAD], in_=w2_view[e, r])
+            nc.sync.dma_start(out=w2_raw[e][:], in_=w2_view[e])
 
-        def load_gate(e):
-            gates[e] = keep.tile([P, C], F32, name=f"gates{e}")
-            nc.sync.dma_start(out=gates[e][:], in_=gate[:, e * C : (e + 1) * C])
+        def load_gate(first, last):
+            tile = keep.tile([P, (last - first) * P], F32, name=f"gates{first}")
+            nc.sync.dma_start(out=tile[:], in_=gate[:, first * P : last * P])
+            for n in range(first, last):
+                gates[n // GROUPS, n % GROUPS] = (tile, first * P)
 
-        for e in range(E):
-            for i in range(len(CHUNKS)):
-                m, g = CHUNKS[i]
-                if (e, i) == (1, 1):
-                    load_w2(0)
-                if (e, i) == (1, 3):
-                    load_gate(0)
-                if (e, m, g) == LAST:
-                    for q in range(2):
-                        tile = raws.tile([P, J, H // 2], F32, name="raw_half", bufs=2)
-                        nc.sync.dma_start(out=tile[:], in_=w_views[m][e, g, :, :, q * H // 2 : (q + 1) * H // 2])
-                        w_raw[e, m, g, q] = tile
-                else:
-                    tile = raws.tile([P, J, H], F32, name="raw")
-                    nc.sync.dma_start(out=tile[:], in_=w_views[m][e, g])
-                    w_raw[e, m, g] = tile
-        load_w2(E - 1)
-        load_gate(E - 1)
+        def load_tokens(g):
+            x_raw[g] = keep.tile([P, J, T], F32, name=f"x_raw{g}")
+            nc.sync.dma_start(out=x_raw[g][:], in_=xT_view[g])
+
+        def load_chunk(e, m, g):
+            for first, last in LAST_LOADS if (e, m, g) == LAST else WHOLE:
+                tile = keep.tile([P, J, last - first], F32, name=f"w_raw{e}{m}{g}_{first}")
+                nc.sync.dma_start(out=tile[:], in_=w_views[m][e, g, :, :, first:last])
+                w_raw[e, m, g, first] = tile
+
+        load_w2(0)
+        load_tokens(0)
+        nc.sync.dma_start(offsets[:], offs)
+        load_tokens(1)
+        load_tokens(2)
+        for m in range(2):
+            for g in range(PASSES):
+                load_chunk(0, m, g)
+        load_chunk(1, 0, 0)
+        load_chunk(1, 0, 1)
+        load_gate(0, 2)
+        load_chunk(1, 0, 2)
+        for g in range(PASSES):
+            load_chunk(1, 1, g)
+        load_w2(1)
+        load_gate(2, 4)
 
         x_words = {}
         s_words = {}
@@ -104,10 +123,7 @@ def tile_routed_moe_kernel(tc, xT, w1, w3, w2, gate, offs, out):
             x_words[g] = keep.tile([P, T], U32, name=f"x_words{g}", align_bytes=64)
             s_words[g] = keep.tile([P, SLOTS], U32, name=f"s_words{g}", align_bytes=64)
             grouped = stage.tile([P, T * J], BF16, name="grouped", align_bytes=64, bufs=2)
-            target = token_target(grouped[:])
-            source = token_source(x_raw[g][:])
-            nc.scalar.copy(target[:, : X_CUT // QUAD], source[:, : X_CUT // QUAD])
-            nc.vector.tensor_copy(target[:, X_CUT // QUAD :], source[:, X_CUT // QUAD :])
+            round_and_interleave(grouped[:], x_raw[g][:], X_CUT)
             for half in range(2):
                 cols = slice(half * HALF_T, (half + 1) * HALF_T)
                 nc.vector.quantize_mx(
@@ -115,74 +131,149 @@ def tile_routed_moe_kernel(tc, xT, w1, w3, w2, gate, offs, out):
                     scales=x_bytes[4 * g :, cols],
                     in_=grouped[:, J * cols.start : J * cols.stop],
                 )
+            if g == PASSES - 1:
+                nc.vector.tensor_copy(s_bytes[:], x_bytes[:].indirect(offsets[:]))
             nc.vector.tensor_copy(s_words[g][:], x_words[g][:].indirect(offsets[:]))
-        nc.vector.tensor_copy(s_bytes[:], x_bytes[:].indirect(offsets[:]))
 
-        for e in range(E):
-            banks = {}
-            gated = small.tile([P, 4, C], F32, name="gated")
-            for m, g in CHUNKS:
-                words = keep.tile([P, H], U32, name=f"w_words{e}{m}{g}", align_bytes=64)
-                scales = keep.tile([P, H], U8, name=f"w_bytes{e}{m}{g}", align_bytes=64)
-                grouped = stage.tile([P, H * J], BF16, name="w_grouped", align_bytes=64, bufs=5)
-                target = weight_target(grouped[:])
-                if (e, m, g) == LAST:
-                    pieces = [(w_raw[e, m, g, q], 16 * q, 16 * q + L_CUT // 4, 16 * (q + 1)) for q in range(2)]
-                else:
-                    pieces = [(w_raw[e, m, g], 0, W_CUT, 32)]
-                for raw, v0, v1, v2 in pieces:
-                    source = weight_source(raw[:])
-                    nc.scalar.copy(target[:, :, v0:v1], source[:, :, : v1 - v0])
-                    nc.vector.tensor_copy(target[:, :, v1:v2], source[:, :, v1 - v0 :])
-                nc.vector.quantize_mx(out=words[:].bitcast(FP8X4), scales=scales[:], in_=grouped[:])
-                for t in range(4):
-                    cols = slice(128 * t, 128 * (t + 1))
-                    if g == 0:
-                        banks[m, t] = psum.tile([P, C], F32, name="bank")
-                    nc.tensor.matmul_mx(
-                        out=banks[m, t][:],
-                        lhsT=words[:, cols].bitcast(FP8X4),
-                        lhsT_scale=scales[:, cols],
-                        rhs=s_words[g][:, e * C : (e + 1) * C].bitcast(FP8X4),
-                        rhs_scale=s_bytes[4 * g :, e * C : (e + 1) * C],
-                        start=(g == 0),
-                        stop=(g == PASSES - 1),
+        banks = {}
+        gated = {}
+        hidden = {}
+        w2_codes = {}
+        h_grouped = {}
+        h_codes = {}
+        y = {}
+
+        def first_layer(e, m, g, share):
+            ranges = LAST_BANKS if (e, m) == LAST[:2] else WHOLE
+            for first, last in LAST_LOADS if (e, m, g) == LAST else WHOLE:
+                width = last - first
+                grouped = stage.tile([P, width * J], BF16, name="w_grouped", tag="staging", align_bytes=64, bufs=5)
+                round_and_interleave(grouped[:], w_raw[e, m, g, first][:], width * share // 64 // 8 * 8)
+                inside = [r for r in ranges if first <= r[0] < last]
+                for c0, c1 in inside if (e, m, g) == LAST else WHOLE:
+                    words = stage.tile([P, c1 - c0], U32, name="w_words", tag="codes", align_bytes=64, bufs=5)
+                    scales = stage.tile([P, c1 - c0], U8, name="w_bytes", align_bytes=64)
+                    nc.vector.quantize_mx(
+                        out=words[:].bitcast(FP8X4),
+                        scales=scales[:],
+                        in_=grouped[:, J * (c0 - first) : J * (c1 - first)],
                     )
-                    if m == 0 and g == PASSES - 1:
-                        nc.scalar.activation(gated[:, t, :], banks[m, t][:], RELU)
+                    for b0, b1 in [r for r in ranges if c0 <= r[0] < c1]:
+                        cols = slice(b0 - c0, b1 - c0)
+                        for s in range(GROUPS):
+                            slots = slice(e * C + s * P, e * C + (s + 1) * P)
+                            if g == 0:
+                                banks[e, m, b0, s] = psum.tile([P, b1 - b0], F32, name="bank")
+                            nc.tensor.matmul_mx(
+                                out=banks[e, m, b0, s][:],
+                                lhsT=s_words[g][:, slots].bitcast(FP8X4),
+                                lhsT_scale=s_bytes[4 * g :, slots],
+                                rhs=words[:, cols].bitcast(FP8X4),
+                                rhs_scale=scales[:, cols],
+                                start=(g == 0),
+                                stop=(g == PASSES - 1),
+                            )
 
-            w2_grouped = small.tile([P, N * J], BF16, name="w2_grouped", align_bytes=64)
-            w2_words = small.tile([P, N], U32, name="w2_words", align_bytes=64)
-            w2_bytes = small.tile([P, N], U8, name="w2_bytes", align_bytes=64)
-            nc.scalar.copy(token_target(w2_grouped[:]), token_source(w2_raw[e][:]))
-            nc.vector.quantize_mx(out=w2_words[:].bitcast(FP8X4), scales=w2_bytes[:], in_=w2_grouped[:])
+        def rectify(e):
+            gated[e] = stage.tile([P, GROUPS, H], F32, name="gated", tag="staging", align_bytes=64, bufs=5)
+            for s in range(GROUPS):
+                nc.scalar.activation(word_major(gated[e][:, s, :]), by_word(banks[e, 0, 0, s][:]), RELU)
 
-            product = small.tile([P, 4, C], BF16, name="product")
-            for t in range(4):
-                nc.vector.tensor_tensor(product[:, t, :], banks[1, t][:], gated[:, t, :], MULT)
-            size = C // PARTS[e]
-            for b in range(PARTS[e]):
-                part = slice(b * size, (b + 1) * size)
-                h = small.tile([P, size * J], BF16, name="h", align_bytes=64)
-                interleave = nc.vector.tensor_copy if b == 0 else nc.scalar.copy
-                interleave(token_target(h[:]), token_source(product[:, :, part]))
-                h_words = small.tile([P, size], U32, name="h_words", align_bytes=64)
-                h_bytes = small.tile([P, size], U8, name="h_bytes", align_bytes=64)
-                nc.vector.quantize_mx(out=h_words[:].bitcast(FP8X4), scales=h_bytes[:], in_=h[:])
-                y_bank = psum.tile([P, size], F32, name="bank")
-                nc.tensor.matmul_mx(
-                    out=y_bank[:],
-                    lhsT=w2_words[:].bitcast(FP8X4),
-                    lhsT_scale=w2_bytes[:],
-                    rhs=h_words[:].bitcast(FP8X4),
-                    rhs_scale=h_bytes[:],
-                    start=True,
-                    stop=True,
-                )
-                y = small.tile([P, size], F32, name="y")
-                nc.scalar.copy(y[:], y_bank[:])
-                first = (e * C + part.start) // 16
-                nc.vector.tensor_tensor(
-                    window[:].indirect(offsets[:, first : first + size // 16]), y[:], gates[e][:, part], MULT
-                )
+        def multiply(e):
+            hidden[e] = stage.tile([P, GROUPS, H], BF16, name="hidden", tag="codes", align_bytes=64, bufs=5)
+            for b0, b1 in LAST_BANKS if e == E - 1 else WHOLE:
+                part = slice(b0 // J, b1 // J)
+                for s in range(GROUPS):
+                    nc.vector.tensor_tensor(
+                        word_major(hidden[e][:, s, :])[:, :, part],
+                        by_word(banks[e, 1, b0, s][:]),
+                        word_major(gated[e][:, s, :])[:, :, part],
+                        MULT,
+                    )
+
+        def quantise_w2(e):
+            grouped = small.tile([P, N * J], BF16, name="w2_grouped", align_bytes=64)
+            words = small.tile([P, N], U32, name="w2_words", align_bytes=64)
+            scales = small.tile([P, N], U8, name="w2_bytes", align_bytes=64)
+            nc.scalar.copy(side_by_side(grouped[:]), rows(w2_raw[e][:]))
+            nc.vector.quantize_mx(out=words[:].bitcast(FP8X4), scales=scales[:], in_=grouped[:])
+            w2_codes[e] = (words, scales)
+
+        def turn_hidden(e, groups):
+            turned = psum.tile([P, len(groups), 2, P], F32, name="bank")
+            for a, s in enumerate(groups):
+                pairs = hidden[e][:, s, :].bitcast(F32)
+                for u in range(2):
+                    nc.tensor.transpose(turned[:, a, u, :], pairs[:, u * P : (u + 1) * P], identity[:])
+            h = small.tile([P, len(groups) * P * J], BF16, name="h", align_bytes=64)
+            nc.scalar.copy(
+                h[:].bitcast(F32).rearrange("p (s n u) -> p s n u", s=len(groups), u=2),
+                turned[:].rearrange("p s u n -> p s n u"),
+            )
+            h_grouped[e, groups] = h
+
+        def quantise_hidden(e, groups):
+            words = small.tile([P, len(groups) * P], U32, name="h_words", align_bytes=64, bufs=3)
+            scales = small.tile([P, len(groups) * P], U8, name="h_bytes", align_bytes=64, bufs=3)
+            nc.vector.quantize_mx(out=words[:].bitcast(FP8X4), scales=scales[:], in_=h_grouped[e, groups][:])
+            h_codes[e, groups] = (words, scales)
+
+        def second_layer(e, groups, source):
+            words, scales = h_codes[e, source]
+            cols = slice((groups[0] - source[0]) * P, (groups[-1] + 1 - source[0]) * P)
+            bank = psum.tile([P, len(groups) * P], F32, name="bank")
+            nc.tensor.matmul_mx(
+                out=bank[:],
+                lhsT=w2_codes[e][0][:].bitcast(FP8X4),
+                lhsT_scale=w2_codes[e][1][:],
+                rhs=words[:, cols].bitcast(FP8X4),
+                rhs_scale=scales[:, cols],
+                start=True,
+                stop=True,
+            )
+            y[e, groups] = small.tile([P, len(groups) * P], F32, name="y", bufs=4)
+            nc.scalar.copy(y[e, groups][:], bank[:])
+
+        def put_back(e, groups):
+            first = e * C + groups[0] * P
+            last = first + len(groups) * P
+            entries = offsets[:, first // 16 : last // 16]
+            gate_tile, gate_first = gates[e, groups[0]]
+            nc.vector.tensor_tensor(
+                window[:].indirect(entries),
+                y[e, groups][:],
+                gate_tile[:, first - gate_first : last - gate_first],
+                MULT,
+            )
+
+        both = (0, 1)
+        quantise_w2(0)
+        for g in range(PASSES):
+            first_layer(0, 0, g, A_CUT)
+        first_layer(0, 1, 0, B_CUT)
+        rectify(0)
+        first_layer(0, 1, 1, B_CUT)
+        first_layer(0, 1, 2, B_CUT)
+        first_layer(1, 0, 0, W_CUT)
+        multiply(0)
+        turn_hidden(0, both)
+        first_layer(1, 0, 1, W_CUT)
+        quantise_hidden(0, both)
+        second_layer(0, both, both)
+        first_layer(1, 0, 2, W_CUT)
+        put_back(0, both)
+        first_layer(1, 1, 0, R_CUT)
+        rectify(1)
+        first_layer(1, 1, 1, Q_CUT)
+        first_layer(1, 1, 2, L_CUT)
+        multiply(1)
+        quantise_w2(1)
+        for s in range(GROUPS):
+            turn_hidden(1, (s,))
+        for s in range(GROUPS):
+            quantise_hidden(1, (s,))
+        for s in range(GROUPS):
+            second_layer(1, (s,), (s,))
+        for s in range(GROUPS):
+            put_back(1, (s,))
         nc.sync.dma_start(out=out, in_=window[:])

@@ -24,12 +24,12 @@ HALF_T = T // 2
 QUAD = 4
 GROUPS = C // P
 
-X_CUT = 512
-W_CUT = 36
-L_CUT = 24
+STAGING = 9
+W_CUT = 32
+L_CUT = 28
 A_CUT = 44
-B_CUT = 28
-R_CUT = 44
+B_CUT = 32
+R_CUT = 32
 Q_CUT = 32
 LAST = (E - 1, 1, PASSES - 1)
 WHOLE = ((0, H),)
@@ -66,6 +66,9 @@ def tile_routed_moe_kernel(tc, xT, w1, w3, w2, gate, offs, out):
         stage = ctx.enter_context(tc.tile_pool(name="stage", bufs=4))
         small = ctx.enter_context(tc.tile_pool(name="small", bufs=2))
         psum = ctx.enter_context(tc.psum_pool(name="psum", bufs=8))
+
+        def staging(shape, dtype, name):
+            return stage.tile(shape, dtype, name=name, tag="staging", align_bytes=64, bufs=STAGING)
 
         offsets = keep.tile([P, SLOTS // 16], U16, name="offsets")
         window = keep.tile([P, T], F32, name="window")
@@ -107,13 +110,13 @@ def tile_routed_moe_kernel(tc, xT, w1, w3, w2, gate, offs, out):
             for g in range(PASSES):
                 load_chunk(0, m, g)
         load_chunk(1, 0, 0)
+        load_gate(0, 1)
         load_chunk(1, 0, 1)
-        load_gate(0, 2)
         load_chunk(1, 0, 2)
         for g in range(PASSES):
             load_chunk(1, 1, g)
         load_w2(1)
-        load_gate(2, 4)
+        load_gate(1, 4)
 
         x_words = {}
         s_words = {}
@@ -122,20 +125,21 @@ def tile_routed_moe_kernel(tc, xT, w1, w3, w2, gate, offs, out):
         for g in range(PASSES):
             x_words[g] = keep.tile([P, T], U32, name=f"x_words{g}", align_bytes=64)
             s_words[g] = keep.tile([P, SLOTS], U32, name=f"s_words{g}", align_bytes=64)
-            grouped = stage.tile([P, T * J], BF16, name="grouped", align_bytes=64, bufs=2)
-            round_and_interleave(grouped[:], x_raw[g][:], X_CUT)
-            for half in range(2):
+            for half, copy in enumerate((nc.vector.tensor_copy, nc.scalar.copy)):
                 cols = slice(half * HALF_T, (half + 1) * HALF_T)
+                grouped = staging([P, HALF_T * J], BF16, "x_grouped")
+                copy(side_by_side(grouped[:]), rows(x_raw[g][:, :, cols]))
                 nc.vector.quantize_mx(
                     out=x_words[g][:, cols].bitcast(FP8X4),
                     scales=x_bytes[4 * g :, cols],
-                    in_=grouped[:, J * cols.start : J * cols.stop],
+                    in_=grouped[:],
                 )
             if g == PASSES - 1:
                 nc.vector.tensor_copy(s_bytes[:], x_bytes[:].indirect(offsets[:]))
             nc.vector.tensor_copy(s_words[g][:], x_words[g][:].indirect(offsets[:]))
 
         banks = {}
+        w_grouped = {}
         gated = {}
         hidden = {}
         w2_codes = {}
@@ -143,39 +147,38 @@ def tile_routed_moe_kernel(tc, xT, w1, w3, w2, gate, offs, out):
         h_codes = {}
         y = {}
 
-        def first_layer(e, m, g, share):
-            ranges = LAST_BANKS if (e, m) == LAST[:2] else WHOLE
-            for first, last in LAST_LOADS if (e, m, g) == LAST else WHOLE:
-                width = last - first
-                grouped = stage.tile([P, width * J], BF16, name="w_grouped", tag="staging", align_bytes=64, bufs=5)
-                round_and_interleave(grouped[:], w_raw[e, m, g, first][:], width * share // 64 // 8 * 8)
-                inside = [r for r in ranges if first <= r[0] < last]
-                for c0, c1 in inside if (e, m, g) == LAST else WHOLE:
-                    words = stage.tile([P, c1 - c0], U32, name="w_words", tag="codes", align_bytes=64, bufs=5)
-                    scales = stage.tile([P, c1 - c0], U8, name="w_bytes", align_bytes=64)
-                    nc.vector.quantize_mx(
-                        out=words[:].bitcast(FP8X4),
-                        scales=scales[:],
-                        in_=grouped[:, J * (c0 - first) : J * (c1 - first)],
+        def interleave(e, m, g, share, first=0):
+            raw = w_raw[e, m, g, first]
+            width = raw[:].shape[2]
+            w_grouped[e, m, g, first] = staging([P, width * J], BF16, "w_grouped")
+            round_and_interleave(w_grouped[e, m, g, first][:], raw[:], width * share // 64 // 8 * 8)
+
+        def first_layer(e, m, g, first=0):
+            grouped = w_grouped[e, m, g, first]
+            width = grouped[:].shape[1] // J
+            words = stage.tile([P, width], U32, name="w_words", tag="codes", align_bytes=64, bufs=5)
+            scales = stage.tile([P, width], U8, name="w_bytes", align_bytes=64)
+            nc.vector.quantize_mx(out=words[:].bitcast(FP8X4), scales=scales[:], in_=grouped[:])
+            for b0, b1 in LAST_BANKS if (e, m) == LAST[:2] else WHOLE:
+                if not first <= b0 < first + width:
+                    continue
+                cols = slice(b0 - first, b1 - first)
+                for s in range(GROUPS):
+                    slots = slice(e * C + s * P, e * C + (s + 1) * P)
+                    if g == 0:
+                        banks[e, m, b0, s] = psum.tile([P, b1 - b0], F32, name="sums", bufs=6)
+                    nc.tensor.matmul_mx(
+                        out=banks[e, m, b0, s][:],
+                        lhsT=s_words[g][:, slots].bitcast(FP8X4),
+                        lhsT_scale=s_bytes[4 * g :, slots],
+                        rhs=words[:, cols].bitcast(FP8X4),
+                        rhs_scale=scales[:, cols],
+                        start=(g == 0),
+                        stop=(g == PASSES - 1),
                     )
-                    for b0, b1 in [r for r in ranges if c0 <= r[0] < c1]:
-                        cols = slice(b0 - c0, b1 - c0)
-                        for s in range(GROUPS):
-                            slots = slice(e * C + s * P, e * C + (s + 1) * P)
-                            if g == 0:
-                                banks[e, m, b0, s] = psum.tile([P, b1 - b0], F32, name="bank")
-                            nc.tensor.matmul_mx(
-                                out=banks[e, m, b0, s][:],
-                                lhsT=s_words[g][:, slots].bitcast(FP8X4),
-                                lhsT_scale=s_bytes[4 * g :, slots],
-                                rhs=words[:, cols].bitcast(FP8X4),
-                                rhs_scale=scales[:, cols],
-                                start=(g == 0),
-                                stop=(g == PASSES - 1),
-                            )
 
         def rectify(e):
-            gated[e] = stage.tile([P, GROUPS, H], F32, name="gated", tag="staging", align_bytes=64, bufs=5)
+            gated[e] = staging([P, GROUPS, H], F32, "gated")
             for s in range(GROUPS):
                 nc.scalar.activation(word_major(gated[e][:, s, :]), by_word(banks[e, 0, 0, s][:]), RELU)
 
@@ -200,12 +203,12 @@ def tile_routed_moe_kernel(tc, xT, w1, w3, w2, gate, offs, out):
             w2_codes[e] = (words, scales)
 
         def turn_hidden(e, groups):
-            turned = psum.tile([P, len(groups), 2, P], F32, name="bank")
+            turned = psum.tile([P, len(groups), 2, P], F32, name="short", bufs=2)
             for a, s in enumerate(groups):
                 pairs = hidden[e][:, s, :].bitcast(F32)
                 for u in range(2):
                     nc.tensor.transpose(turned[:, a, u, :], pairs[:, u * P : (u + 1) * P], identity[:])
-            h = small.tile([P, len(groups) * P * J], BF16, name="h", align_bytes=64)
+            h = staging([P, len(groups) * P * J], BF16, "h")
             nc.scalar.copy(
                 h[:].bitcast(F32).rearrange("p (s n u) -> p s n u", s=len(groups), u=2),
                 turned[:].rearrange("p s u n -> p s n u"),
@@ -218,10 +221,10 @@ def tile_routed_moe_kernel(tc, xT, w1, w3, w2, gate, offs, out):
             nc.vector.quantize_mx(out=words[:].bitcast(FP8X4), scales=scales[:], in_=h_grouped[e, groups][:])
             h_codes[e, groups] = (words, scales)
 
-        def second_layer(e, groups, source):
+        def second_layer(e, groups, source, target):
             words, scales = h_codes[e, source]
             cols = slice((groups[0] - source[0]) * P, (groups[-1] + 1 - source[0]) * P)
-            bank = psum.tile([P, len(groups) * P], F32, name="bank")
+            bank = psum.tile([P, len(groups) * P], F32, name="short", bufs=2)
             nc.tensor.matmul_mx(
                 out=bank[:],
                 lhsT=w2_codes[e][0][:].bitcast(FP8X4),
@@ -231,17 +234,18 @@ def tile_routed_moe_kernel(tc, xT, w1, w3, w2, gate, offs, out):
                 start=True,
                 stop=True,
             )
-            y[e, groups] = small.tile([P, len(groups) * P], F32, name="y", bufs=4)
-            nc.scalar.copy(y[e, groups][:], bank[:])
+            if (e, target) not in y:
+                y[e, target] = staging([P, len(target) * P], F32, "y")
+            nc.scalar.copy(y[e, target][:, (groups[0] - target[0]) * P : (groups[-1] + 1 - target[0]) * P], bank[:])
 
-        def put_back(e, groups):
+        def put_back(e, groups, source):
             first = e * C + groups[0] * P
             last = first + len(groups) * P
             entries = offsets[:, first // 16 : last // 16]
             gate_tile, gate_first = gates[e, groups[0]]
             nc.vector.tensor_tensor(
                 window[:].indirect(entries),
-                y[e, groups][:],
+                y[e, source][:, (groups[0] - source[0]) * P : (groups[-1] + 1 - source[0]) * P],
                 gate_tile[:, first - gate_first : last - gate_first],
                 MULT,
             )
@@ -249,31 +253,43 @@ def tile_routed_moe_kernel(tc, xT, w1, w3, w2, gate, offs, out):
         both = (0, 1)
         quantise_w2(0)
         for g in range(PASSES):
-            first_layer(0, 0, g, A_CUT)
-        first_layer(0, 1, 0, B_CUT)
+            interleave(0, 0, g, A_CUT)
+            first_layer(0, 0, g)
+        interleave(0, 1, 0, B_CUT)
+        first_layer(0, 1, 0)
         rectify(0)
-        first_layer(0, 1, 1, B_CUT)
-        first_layer(0, 1, 2, B_CUT)
-        first_layer(1, 0, 0, W_CUT)
+        interleave(0, 1, 1, B_CUT)
+        first_layer(0, 1, 1)
+        interleave(0, 1, 2, B_CUT)
+        first_layer(0, 1, 2)
+        interleave(1, 0, 0, W_CUT)
         multiply(0)
+        first_layer(1, 0, 0)
+        interleave(1, 0, 1, W_CUT)
         turn_hidden(0, both)
-        first_layer(1, 0, 1, W_CUT)
+        first_layer(1, 0, 1)
         quantise_hidden(0, both)
-        second_layer(0, both, both)
-        first_layer(1, 0, 2, W_CUT)
-        put_back(0, both)
-        first_layer(1, 1, 0, R_CUT)
+        interleave(1, 0, 2, W_CUT)
+        second_layer(0, both, both, both)
+        first_layer(1, 0, 2)
+        put_back(0, (0,), both)
+        interleave(1, 1, 0, R_CUT)
+        first_layer(1, 1, 0)
         rectify(1)
-        first_layer(1, 1, 1, Q_CUT)
-        first_layer(1, 1, 2, L_CUT)
+        interleave(1, 1, 1, Q_CUT)
+        interleave(1, 1, 2, L_CUT, 0)
+        first_layer(1, 1, 1)
+        first_layer(1, 1, 2, 0)
+        interleave(1, 1, 2, L_CUT, 256)
+        first_layer(1, 1, 2, 256)
         multiply(1)
         quantise_w2(1)
+        put_back(0, (1,), both)
         for s in range(GROUPS):
             turn_hidden(1, (s,))
         for s in range(GROUPS):
             quantise_hidden(1, (s,))
         for s in range(GROUPS):
-            second_layer(1, (s,), (s,))
-        for s in range(GROUPS):
-            put_back(1, (s,))
+            second_layer(1, (s,), (s,), both)
+        put_back(1, both, both)
         nc.sync.dma_start(out=out, in_=window[:])

@@ -26,11 +26,12 @@ GROUPS = C // P
 
 STAGING = 9
 W_CUT = 32
-L_CUT = 28
+L_CUT = 40
 A_CUT = 44
 B_CUT = 32
-R_CUT = 32
-Q_CUT = 32
+R_CUT = 24
+Q_CUT = 24
+M_CUT = 24
 LAST = (E - 1, 1, PASSES - 1)
 WHOLE = ((0, H),)
 LAST_LOADS = ((0, 256), (256, 512))
@@ -58,8 +59,10 @@ def tile_routed_moe_kernel(tc, xT, w1, w3, w2, gate, offs, out):
     def round_and_interleave(grouped, raw, cut):
         target = side_by_side(grouped)
         source = rows(raw)
-        nc.scalar.copy(target[:, : cut // QUAD], source[:, : cut // QUAD])
-        nc.vector.tensor_copy(target[:, cut // QUAD :], source[:, cut // QUAD :])
+        if cut > 0:
+            nc.scalar.copy(target[:, : cut // QUAD], source[:, : cut // QUAD])
+        if cut // QUAD < source.shape[1]:
+            nc.vector.tensor_copy(target[:, cut // QUAD :], source[:, cut // QUAD :])
 
     with ExitStack() as ctx:
         keep = ctx.enter_context(tc.tile_pool(name="keep", bufs=1))
@@ -95,11 +98,10 @@ def tile_routed_moe_kernel(tc, xT, w1, w3, w2, gate, offs, out):
             x_raw[g] = keep.tile([P, J, T], F32, name=f"x_raw{g}")
             nc.sync.dma_start(out=x_raw[g][:], in_=xT_view[g])
 
-        def load_chunk(e, m, g):
-            for first, last in LAST_LOADS if (e, m, g) == LAST else WHOLE:
-                tile = keep.tile([P, J, last - first], F32, name=f"w_raw{e}{m}{g}_{first}")
-                nc.sync.dma_start(out=tile[:], in_=w_views[m][e, g, :, :, first:last])
-                w_raw[e, m, g, first] = tile
+        def load_chunk(e, m, g, first=0, last=H):
+            tile = keep.tile([P, J, last - first], F32, name=f"w_raw{e}{m}{g}_{first}")
+            nc.sync.dma_start(out=tile[:], in_=w_views[m][e, g, :, :, first:last])
+            w_raw[e, m, g, first] = tile
 
         load_w2(0)
         load_tokens(0)
@@ -110,11 +112,13 @@ def tile_routed_moe_kernel(tc, xT, w1, w3, w2, gate, offs, out):
             for g in range(PASSES):
                 load_chunk(0, m, g)
         load_chunk(1, 0, 0)
-        load_gate(0, 1)
         load_chunk(1, 0, 1)
         load_chunk(1, 0, 2)
-        for g in range(PASSES):
-            load_chunk(1, 1, g)
+        load_chunk(1, 1, 0)
+        load_gate(0, 1)
+        load_chunk(1, 1, 1, 0, 512)
+        load_chunk(1, 1, 2, 0, 256)
+        load_chunk(1, 1, 2, 256, 512)
         load_w2(1)
         load_gate(1, 4)
 
@@ -147,11 +151,12 @@ def tile_routed_moe_kernel(tc, xT, w1, w3, w2, gate, offs, out):
         h_codes = {}
         y = {}
 
-        def interleave(e, m, g, share, first=0):
-            raw = w_raw[e, m, g, first]
-            width = raw[:].shape[2]
+        def interleave(e, m, g, share, first=0, last=H):
+            start = max(key[3] for key in w_raw if key[:3] == (e, m, g) and key[3] <= first)
+            raw = w_raw[e, m, g, start][:, :, first - start : last - start]
+            width = last - first
             w_grouped[e, m, g, first] = staging([P, width * J], BF16, "w_grouped")
-            round_and_interleave(w_grouped[e, m, g, first][:], raw[:], width * share // 64 // 8 * 8)
+            round_and_interleave(w_grouped[e, m, g, first][:], raw, width * share // 64 // 8 * 8)
 
         def first_layer(e, m, g, first=0):
             grouped = w_grouped[e, m, g, first]
@@ -182,9 +187,10 @@ def tile_routed_moe_kernel(tc, xT, w1, w3, w2, gate, offs, out):
             for s in range(GROUPS):
                 nc.scalar.activation(word_major(gated[e][:, s, :]), by_word(banks[e, 0, 0, s][:]), RELU)
 
-        def multiply(e):
-            hidden[e] = stage.tile([P, GROUPS, H], BF16, name="hidden", tag="codes", align_bytes=64, bufs=5)
-            for b0, b1 in LAST_BANKS if e == E - 1 else WHOLE:
+        def multiply(e, ranges):
+            if e not in hidden:
+                hidden[e] = stage.tile([P, GROUPS, H], BF16, name="hidden", tag="codes", align_bytes=64, bufs=5)
+            for b0, b1 in ranges:
                 part = slice(b0 // J, b1 // J)
                 for s in range(GROUPS):
                     nc.vector.tensor_tensor(
@@ -263,7 +269,7 @@ def tile_routed_moe_kernel(tc, xT, w1, w3, w2, gate, offs, out):
         interleave(0, 1, 2, B_CUT)
         first_layer(0, 1, 2)
         interleave(1, 0, 0, W_CUT)
-        multiply(0)
+        multiply(0, WHOLE)
         first_layer(1, 0, 0)
         interleave(1, 0, 1, W_CUT)
         turn_hidden(0, both)
@@ -272,17 +278,17 @@ def tile_routed_moe_kernel(tc, xT, w1, w3, w2, gate, offs, out):
         interleave(1, 0, 2, W_CUT)
         second_layer(0, both, both, both)
         first_layer(1, 0, 2)
-        put_back(0, (0,), both)
         interleave(1, 1, 0, R_CUT)
+        put_back(0, (0,), both)
         first_layer(1, 1, 0)
         rectify(1)
         interleave(1, 1, 1, Q_CUT)
-        interleave(1, 1, 2, L_CUT, 0)
+        interleave(1, 1, 2, L_CUT, 0, 256)
         first_layer(1, 1, 1)
         first_layer(1, 1, 2, 0)
-        interleave(1, 1, 2, L_CUT, 256)
+        interleave(1, 1, 2, M_CUT, 256, 512)
         first_layer(1, 1, 2, 256)
-        multiply(1)
+        multiply(1, LAST_BANKS)
         quantise_w2(1)
         put_back(0, (1,), both)
         for s in range(GROUPS):

@@ -17,63 +17,62 @@ RELU = mybir.ActivationFunctionType.Relu
 
 P = 128
 J = 4
-PASS = P * J
-PASSES = K // PASS
+PASSES = K // (P * J)
 SLOTS = E * C
-HALF_T = T // 2
-QUAD = 4
 GROUPS = C // P
+RUN = 4
+LIST_COLUMN = 16
+W1, W3 = 0, 1
 
-STAGING = 9
-W_CUT = 32
-L_CUT = 40
-A_CUT = 44
-B_CUT = 32
-R_CUT = 24
-Q_CUT = 24
-M_CUT = 24
-LAST = (E - 1, 1, PASSES - 1)
-WHOLE = ((0, H),)
-LAST_LOADS = ((0, 256), (256, 512))
-LAST_BANKS = ((0, 256), (256, 512))
+ALL_COLUMNS = (0, H)
+COLUMN_HALVES = ((0, H // 2), (H // 2, H))
+
+SHARE_BESIDE_GATHERS = 44
+SHARE_BESIDE_RELU = 24
+SHARE_EVEN = 32
+SHARE_FIRST_HALF = 40
+
+STAGING_BUFS = 9
+CODES_BUFS = 5
+SUM_BANKS = 6
+SHORT_BANKS = 2
+H_CODE_BUFS = 3
 
 
 def tile_routed_moe_kernel(tc, xT, w1, w3, w2, gate, offs, out):
     nc = tc.nc
     xT_view = xT.rearrange("(g p j) n -> g p j n", p=P, j=J)
-    w_views = [w.rearrange("e (g p j) n -> e g p j n", p=P, j=J) for w in (w1, w3)]
+    w_views = [w.rearrange("e (g p j) n -> e p g j n", p=P, j=J) for w in (w1, w3)]
     w2_view = w2.rearrange("e (p j) n -> e p j n", j=J)
 
-    def rows(ap):
-        return ap.rearrange("p j (c i) -> p c j i", i=QUAD)
+    def loaded_order(ap):
+        return ap.rearrange("p j (c r) -> p c j r", r=RUN)
 
-    def side_by_side(ap):
-        return ap.rearrange("p (c i j) -> p c j i", i=QUAD, j=J)
+    def interleaved_order(ap):
+        return ap.rearrange("p (c r j) -> p c j r", r=RUN, j=J)
 
-    def by_word(ap):
+    def sums_by_word(ap):
         return ap.rearrange("s (w u b) -> s u w b", u=2, b=2)
 
-    def word_major(ap):
+    def stored_by_word(ap):
         return ap.rearrange("s (u w b) -> s u w b", u=2, b=2)
-
-    def round_and_interleave(grouped, raw, cut):
-        target = side_by_side(grouped)
-        source = rows(raw)
-        if cut > 0:
-            nc.scalar.copy(target[:, : cut // QUAD], source[:, : cut // QUAD])
-        if cut // QUAD < source.shape[1]:
-            nc.vector.tensor_copy(target[:, cut // QUAD :], source[:, cut // QUAD :])
 
     with ExitStack() as ctx:
         keep = ctx.enter_context(tc.tile_pool(name="keep", bufs=1))
         stage = ctx.enter_context(tc.tile_pool(name="stage", bufs=4))
-        small = ctx.enter_context(tc.tile_pool(name="small", bufs=2))
-        psum = ctx.enter_context(tc.psum_pool(name="psum", bufs=8))
+        small = ctx.enter_context(tc.tile_pool(name="small", bufs=E))
+        psum = ctx.enter_context(tc.psum_pool(name="psum", bufs=SUM_BANKS + SHORT_BANKS))
 
         def staging(shape, dtype, name):
-            return stage.tile(shape, dtype, name=name, tag="staging", align_bytes=64, bufs=STAGING)
+            return stage.tile(shape, dtype, name=name, tag="staging", align_bytes=64, bufs=STAGING_BUFS)
 
-        offsets = keep.tile([P, SLOTS // 16], U16, name="offsets")
+        def codes_ring(shape, dtype, name):
+            return stage.tile(shape, dtype, name=name, tag="codes", align_bytes=64, bufs=CODES_BUFS)
+
+        def h_ring(shape, dtype, name):
+            return small.tile(shape, dtype, name=name, tag="h_words", align_bytes=64, bufs=H_CODE_BUFS)
+
+        offsets = keep.tile([P, SLOTS // LIST_COLUMN], U16, name="offsets")
         window = keep.tile([P, T], F32, name="window")
         identity = keep.tile([P, P], F32, name="identity")
         nc.vector.memset(window[:], 0.0)
@@ -82,220 +81,207 @@ def tile_routed_moe_kernel(tc, xT, w1, w3, w2, gate, offs, out):
         x_raw = {}
         w_raw = {}
         w2_raw = {}
-        gates = {}
 
-        def load_w2(e):
-            w2_raw[e] = keep.tile([P, J, N], F32, name=f"w2_raw{e}")
-            nc.sync.dma_start(out=w2_raw[e][:], in_=w2_view[e])
+        def load_passes(e, m, first, last):
+            tile = keep.tile([P, last - first, J, H], F32, name=f"w_raw{e}{m}{first}")
+            nc.sync.dma_start(out=tile[:], in_=w_views[m][e, :, first:last])
+            for g in range(first, last):
+                w_raw[e, m, g, ALL_COLUMNS] = tile[:, g - first]
 
-        def load_gate(first, last):
-            tile = keep.tile([P, (last - first) * P], F32, name=f"gates{first}")
-            nc.sync.dma_start(out=tile[:], in_=gate[:, first * P : last * P])
-            for n in range(first, last):
-                gates[n // GROUPS, n % GROUPS] = (tile, first * P)
-
-        def load_tokens(g):
+        for g in range(PASSES):
             x_raw[g] = keep.tile([P, J, T], F32, name=f"x_raw{g}")
             nc.sync.dma_start(out=x_raw[g][:], in_=xT_view[g])
-
-        def load_chunk(e, m, g, first=0, last=H):
-            tile = keep.tile([P, J, last - first], F32, name=f"w_raw{e}{m}{g}_{first}")
-            nc.sync.dma_start(out=tile[:], in_=w_views[m][e, g, :, :, first:last])
-            w_raw[e, m, g, first] = tile
-
-        load_w2(0)
-        load_tokens(0)
-        nc.sync.dma_start(offsets[:], offs)
-        load_tokens(1)
-        load_tokens(2)
-        for m in range(2):
-            for g in range(PASSES):
-                load_chunk(0, m, g)
-        load_chunk(1, 0, 0)
-        load_chunk(1, 0, 1)
-        load_chunk(1, 0, 2)
-        load_chunk(1, 1, 0)
-        load_gate(0, 1)
-        load_chunk(1, 1, 1, 0, 512)
-        load_chunk(1, 1, 2, 0, 256)
-        load_chunk(1, 1, 2, 256, 512)
-        load_w2(1)
-        load_gate(1, 4)
-
-        x_words = {}
-        s_words = {}
-        x_bytes = keep.tile([P, T], U8, name="x_bytes", align_bytes=64)
-        s_bytes = keep.tile([P, SLOTS], U8, name="s_bytes", align_bytes=64)
+            if g == 0:
+                nc.sync.dma_start(offsets[:], offs)
+        for m in (W1, W3):
+            load_passes(0, m, 0, PASSES - 1)
+            load_passes(0, m, PASSES - 1, PASSES)
         for g in range(PASSES):
-            x_words[g] = keep.tile([P, T], U32, name=f"x_words{g}", align_bytes=64)
-            s_words[g] = keep.tile([P, SLOTS], U32, name=f"s_words{g}", align_bytes=64)
+            load_passes(1, W1, g, g + 1)
+        for g in range(PASSES - 1):
+            load_passes(1, W3, g, g + 1)
+        for first, last in COLUMN_HALVES:
+            tile = keep.tile([P, J, last - first], F32, name=f"w_half{first}")
+            nc.sync.dma_start(out=tile[:], in_=w_views[W3][1, :, PASSES - 1, :, first:last])
+            w_raw[1, W3, PASSES - 1, (first, last)] = tile[:]
+        for e in range(E):
+            w2_raw[e] = keep.tile([P, J, N], F32, name=f"w2_raw{e}")
+            nc.sync.dma_start(out=w2_raw[e][:], in_=w2_view[e])
+        gates = keep.tile([P, SLOTS], F32, name="gates")
+        nc.sync.dma_start(out=gates[:], in_=gate)
+
+        slot_words = {}
+        token_bytes = keep.tile([P, T], U8, name="token_bytes", align_bytes=64)
+        slot_bytes = keep.tile([P, SLOTS], U8, name="slot_bytes", align_bytes=64)
+        for g in range(PASSES):
+            token_words = keep.tile([P, T], U32, name=f"token_words{g}", align_bytes=64)
+            slot_words[g] = keep.tile([P, SLOTS], U32, name=f"slot_words{g}", align_bytes=64)
             for half, copy in enumerate((nc.vector.tensor_copy, nc.scalar.copy)):
-                cols = slice(half * HALF_T, (half + 1) * HALF_T)
-                grouped = staging([P, HALF_T * J], BF16, "x_grouped")
-                copy(side_by_side(grouped[:]), rows(x_raw[g][:, :, cols]))
+                tokens = slice(half * T // 2, (half + 1) * T // 2)
+                interleaved = staging([P, T // 2 * J], BF16, "x_interleaved")
+                copy(interleaved_order(interleaved[:]), loaded_order(x_raw[g][:, :, tokens]))
                 nc.vector.quantize_mx(
-                    out=x_words[g][:, cols].bitcast(FP8X4),
-                    scales=x_bytes[4 * g :, cols],
-                    in_=grouped[:],
+                    out=token_words[:, tokens].bitcast(FP8X4),
+                    scales=token_bytes[4 * g :, tokens],
+                    in_=interleaved[:],
                 )
             if g == PASSES - 1:
-                nc.vector.tensor_copy(s_bytes[:], x_bytes[:].indirect(offsets[:]))
-            nc.vector.tensor_copy(s_words[g][:], x_words[g][:].indirect(offsets[:]))
+                nc.vector.tensor_copy(slot_bytes[:], token_bytes[:].indirect(offsets[:]))
+            nc.vector.tensor_copy(slot_words[g][:], token_words[:].indirect(offsets[:]))
 
-        banks = {}
-        w_grouped = {}
-        gated = {}
+        w_interleaved = {}
+        sums = {}
+        rectified = {}
         hidden = {}
-        w2_codes = {}
-        h_grouped = {}
+        h_interleaved = {}
         h_codes = {}
-        y = {}
+        w2_codes = {}
 
-        def interleave(e, m, g, share, first=0, last=H):
-            start = max(key[3] for key in w_raw if key[:3] == (e, m, g) and key[3] <= first)
-            raw = w_raw[e, m, g, start][:, :, first - start : last - start]
-            width = last - first
-            w_grouped[e, m, g, first] = staging([P, width * J], BF16, "w_grouped")
-            round_and_interleave(w_grouped[e, m, g, first][:], raw, width * share // 64 // 8 * 8)
+        def sum_ranges(e, m):
+            return COLUMN_HALVES if (e, m) == (1, W3) else (ALL_COLUMNS,)
 
-        def first_layer(e, m, g, first=0):
-            grouped = w_grouped[e, m, g, first]
-            width = grouped[:].shape[1] // J
-            words = stage.tile([P, width], U32, name="w_words", tag="codes", align_bytes=64, bufs=5)
+        def interleave(e, m, g, share, columns=ALL_COLUMNS):
+            width = columns[1] - columns[0]
+            tile = staging([P, width * J], BF16, "w_interleaved")
+            target = interleaved_order(tile[:])
+            source = loaded_order(w_raw[e, m, g, columns])
+            cut = width * share // 64 // RUN
+            nc.scalar.copy(target[:, :cut], source[:, :cut])
+            nc.vector.tensor_copy(target[:, cut:], source[:, cut:])
+            w_interleaved[e, m, g, columns] = tile
+
+        def first_layer(e, m, g, columns=ALL_COLUMNS):
+            width = columns[1] - columns[0]
+            words = codes_ring([P, width], U32, "w_words")
             scales = stage.tile([P, width], U8, name="w_bytes", align_bytes=64)
-            nc.vector.quantize_mx(out=words[:].bitcast(FP8X4), scales=scales[:], in_=grouped[:])
-            for b0, b1 in LAST_BANKS if (e, m) == LAST[:2] else WHOLE:
-                if not first <= b0 < first + width:
-                    continue
-                cols = slice(b0 - first, b1 - first)
-                for s in range(GROUPS):
-                    slots = slice(e * C + s * P, e * C + (s + 1) * P)
-                    if g == 0:
-                        banks[e, m, b0, s] = psum.tile([P, b1 - b0], F32, name="sums", bufs=6)
-                    nc.tensor.matmul_mx(
-                        out=banks[e, m, b0, s][:],
-                        lhsT=s_words[g][:, slots].bitcast(FP8X4),
-                        lhsT_scale=s_bytes[4 * g :, slots],
-                        rhs=words[:, cols].bitcast(FP8X4),
-                        rhs_scale=scales[:, cols],
-                        start=(g == 0),
-                        stop=(g == PASSES - 1),
-                    )
+            nc.vector.quantize_mx(
+                out=words[:].bitcast(FP8X4), scales=scales[:], in_=w_interleaved[e, m, g, columns][:]
+            )
+            for first, last in sum_ranges(e, m):
+                if columns[0] <= first < columns[1]:
+                    moving = slice(first - columns[0], last - columns[0])
+                    for s in range(GROUPS):
+                        slots = slice(e * C + s * P, e * C + (s + 1) * P)
+                        if g == 0:
+                            sums[e, m, first, s] = psum.tile([P, last - first], F32, name="sums", bufs=SUM_BANKS)
+                        nc.tensor.matmul_mx(
+                            out=sums[e, m, first, s][:],
+                            lhsT=slot_words[g][:, slots].bitcast(FP8X4),
+                            lhsT_scale=slot_bytes[4 * g :, slots],
+                            rhs=words[:, moving].bitcast(FP8X4),
+                            rhs_scale=scales[:, moving],
+                            start=(g == 0),
+                            stop=(g == PASSES - 1),
+                        )
 
         def rectify(e):
-            gated[e] = staging([P, GROUPS, H], F32, "gated")
+            rectified[e] = staging([P, GROUPS, H], F32, "rectified")
             for s in range(GROUPS):
-                nc.scalar.activation(word_major(gated[e][:, s, :]), by_word(banks[e, 0, 0, s][:]), RELU)
+                nc.scalar.activation(stored_by_word(rectified[e][:, s, :]), sums_by_word(sums[e, W1, 0, s][:]), RELU)
 
-        def multiply(e, ranges):
-            if e not in hidden:
-                hidden[e] = stage.tile([P, GROUPS, H], BF16, name="hidden", tag="codes", align_bytes=64, bufs=5)
-            for b0, b1 in ranges:
-                part = slice(b0 // J, b1 // J)
+        def multiply(e):
+            hidden[e] = codes_ring([P, GROUPS, H], BF16, "hidden")
+            for first, last in sum_ranges(e, W3):
+                words = slice(first // J, last // J)
                 for s in range(GROUPS):
                     nc.vector.tensor_tensor(
-                        word_major(hidden[e][:, s, :])[:, :, part],
-                        by_word(banks[e, 1, b0, s][:]),
-                        word_major(gated[e][:, s, :])[:, :, part],
+                        stored_by_word(hidden[e][:, s, :])[:, :, words],
+                        sums_by_word(sums[e, W3, first, s][:]),
+                        stored_by_word(rectified[e][:, s, :])[:, :, words],
                         MULT,
                     )
 
-        def quantise_w2(e):
-            grouped = small.tile([P, N * J], BF16, name="w2_grouped", align_bytes=64)
-            words = small.tile([P, N], U32, name="w2_words", align_bytes=64)
-            scales = small.tile([P, N], U8, name="w2_bytes", align_bytes=64)
-            nc.scalar.copy(side_by_side(grouped[:]), rows(w2_raw[e][:]))
-            nc.vector.quantize_mx(out=words[:].bitcast(FP8X4), scales=scales[:], in_=grouped[:])
-            w2_codes[e] = (words, scales)
-
         def turn_hidden(e, groups):
-            turned = psum.tile([P, len(groups), 2, P], F32, name="short", bufs=2)
+            turned = psum.tile([P, len(groups), 2, P], F32, name="short", bufs=SHORT_BANKS)
             for a, s in enumerate(groups):
                 pairs = hidden[e][:, s, :].bitcast(F32)
                 for u in range(2):
                     nc.tensor.transpose(turned[:, a, u, :], pairs[:, u * P : (u + 1) * P], identity[:])
-            h = staging([P, len(groups) * P * J], BF16, "h")
+            tile = staging([P, len(groups) * P * J], BF16, "h_interleaved")
             nc.scalar.copy(
-                h[:].bitcast(F32).rearrange("p (s n u) -> p s n u", s=len(groups), u=2),
-                turned[:].rearrange("p s u n -> p s n u"),
+                tile[:].bitcast(F32).rearrange("p (a n u) -> p a n u", a=len(groups), u=2),
+                turned[:].rearrange("p a u n -> p a n u"),
             )
-            h_grouped[e, groups] = h
+            h_interleaved[e, groups] = tile
 
         def quantise_hidden(e, groups):
-            words = small.tile([P, len(groups) * P], U32, name="h_words", align_bytes=64, bufs=3)
-            scales = small.tile([P, len(groups) * P], U8, name="h_bytes", align_bytes=64, bufs=3)
-            nc.vector.quantize_mx(out=words[:].bitcast(FP8X4), scales=scales[:], in_=h_grouped[e, groups][:])
+            words = h_ring([P, len(groups) * P], U32, "h_words")
+            scales = small.tile([P, len(groups) * P], U8, name="h_bytes", align_bytes=64, bufs=H_CODE_BUFS)
+            nc.vector.quantize_mx(out=words[:].bitcast(FP8X4), scales=scales[:], in_=h_interleaved[e, groups][:])
             h_codes[e, groups] = (words, scales)
 
-        def second_layer(e, groups, source, target):
-            words, scales = h_codes[e, source]
-            cols = slice((groups[0] - source[0]) * P, (groups[-1] + 1 - source[0]) * P)
-            bank = psum.tile([P, len(groups) * P], F32, name="short", bufs=2)
+        def quantise_w2(e):
+            interleaved = small.tile([P, N * J], BF16, name="w2_interleaved", align_bytes=64)
+            words = small.tile([P, N], U32, name="w2_words", align_bytes=64)
+            scales = small.tile([P, N], U8, name="w2_bytes", align_bytes=64)
+            nc.scalar.copy(interleaved_order(interleaved[:]), loaded_order(w2_raw[e][:]))
+            nc.vector.quantize_mx(out=words[:].bitcast(FP8X4), scales=scales[:], in_=interleaved[:])
+            w2_codes[e] = (words, scales)
+
+        def second_layer(e, groups, bank):
             nc.tensor.matmul_mx(
                 out=bank[:],
                 lhsT=w2_codes[e][0][:].bitcast(FP8X4),
                 lhsT_scale=w2_codes[e][1][:],
-                rhs=words[:, cols].bitcast(FP8X4),
-                rhs_scale=scales[:, cols],
+                rhs=h_codes[e, groups][0][:].bitcast(FP8X4),
+                rhs_scale=h_codes[e, groups][1][:],
                 start=True,
                 stop=True,
             )
-            if (e, target) not in y:
-                y[e, target] = staging([P, len(target) * P], F32, "y")
-            nc.scalar.copy(y[e, target][:, (groups[0] - target[0]) * P : (groups[-1] + 1 - target[0]) * P], bank[:])
 
-        def put_back(e, groups, source):
-            first = e * C + groups[0] * P
-            last = first + len(groups) * P
-            entries = offsets[:, first // 16 : last // 16]
-            gate_tile, gate_first = gates[e, groups[0]]
-            nc.vector.tensor_tensor(
-                window[:].indirect(entries),
-                y[e, source][:, (groups[0] - source[0]) * P : (groups[-1] + 1 - source[0]) * P],
-                gate_tile[:, first - gate_first : last - gate_first],
-                MULT,
-            )
+        def put_back(y, first, last):
+            entries = offsets[:, first // LIST_COLUMN : last // LIST_COLUMN]
+            nc.vector.tensor_tensor(window[:].indirect(entries), y[:], gates[:, first:last], MULT)
 
-        both = (0, 1)
-        quantise_w2(0)
+        both = tuple(range(GROUPS))
         for g in range(PASSES):
-            interleave(0, 0, g, A_CUT)
-            first_layer(0, 0, g)
-        interleave(0, 1, 0, B_CUT)
-        first_layer(0, 1, 0)
-        rectify(0)
-        interleave(0, 1, 1, B_CUT)
-        first_layer(0, 1, 1)
-        interleave(0, 1, 2, B_CUT)
-        first_layer(0, 1, 2)
-        interleave(1, 0, 0, W_CUT)
-        multiply(0, WHOLE)
-        first_layer(1, 0, 0)
-        interleave(1, 0, 1, W_CUT)
+            interleave(0, W1, g, SHARE_BESIDE_GATHERS)
+            first_layer(0, W1, g)
+        for g in range(PASSES):
+            interleave(0, W3, g, SHARE_BESIDE_RELU)
+            first_layer(0, W3, g)
+            if g == 0:
+                rectify(0)
+
+        interleave(1, W1, 0, SHARE_EVEN)
+        multiply(0)
+        first_layer(1, W1, 0)
+        interleave(1, W1, 1, SHARE_EVEN)
         turn_hidden(0, both)
-        first_layer(1, 0, 1)
+        first_layer(1, W1, 1)
         quantise_hidden(0, both)
-        interleave(1, 0, 2, W_CUT)
-        second_layer(0, both, both, both)
-        first_layer(1, 0, 2)
-        interleave(1, 1, 0, R_CUT)
-        put_back(0, (0,), both)
-        first_layer(1, 1, 0)
+        interleave(1, W1, 2, SHARE_EVEN)
+        first_layer(1, W1, 2)
+
+        interleave(1, W3, 0, SHARE_BESIDE_RELU)
+        first_layer(1, W3, 0)
         rectify(1)
-        interleave(1, 1, 1, Q_CUT)
-        interleave(1, 1, 2, L_CUT, 0, 256)
-        first_layer(1, 1, 1)
-        first_layer(1, 1, 2, 0)
-        interleave(1, 1, 2, M_CUT, 256, 512)
-        first_layer(1, 1, 2, 256)
-        multiply(1, LAST_BANKS)
+        interleave(1, W3, 1, SHARE_BESIDE_RELU)
+        interleave(1, W3, 2, SHARE_FIRST_HALF, COLUMN_HALVES[0])
+        first_layer(1, W3, 1)
+        first_layer(1, W3, 2, COLUMN_HALVES[0])
+        interleave(1, W3, 2, SHARE_BESIDE_RELU, COLUMN_HALVES[1])
+        first_layer(1, W3, 2, COLUMN_HALVES[1])
+
+        quantise_w2(0)
+        first_bank = psum.tile([P, C], F32, name="sums", bufs=SUM_BANKS)
+        second_layer(0, both, first_bank)
+        multiply(1)
+        y_early = staging([P, P], F32, "y_early")
+        nc.scalar.copy(y_early[:], first_bank[:, :P])
         quantise_w2(1)
-        put_back(0, (1,), both)
+        put_back(y_early, 0, P)
         for s in range(GROUPS):
             turn_hidden(1, (s,))
+        quantise_hidden(1, (0,))
+        y_late = h_ring([P, P], F32, "y_late")
+        nc.scalar.copy(y_late[:], first_bank[:, P:])
+        quantise_hidden(1, (1,))
+        put_back(y_late, P, C)
+        y_last = staging([P, C], F32, "y_last")
         for s in range(GROUPS):
-            quantise_hidden(1, (s,))
-        for s in range(GROUPS):
-            second_layer(1, (s,), (s,), both)
-        put_back(1, both, both)
+            bank = psum.tile([P, P], F32, name="short", bufs=SHORT_BANKS)
+            second_layer(1, (s,), bank)
+            nc.scalar.copy(y_last[:, s * P : (s + 1) * P], bank[:])
+        put_back(y_last, C, SLOTS)
         nc.sync.dma_start(out=out, in_=window[:])

@@ -29,8 +29,9 @@ COLUMN_HALVES = ((0, H // 2), (H // 2, H))
 
 SHARE_BESIDE_GATHERS = 44
 SHARE_BESIDE_RELU = 24
-SHARE_EVEN = 32
-SHARE_FIRST_HALF = 40
+SHARE_EVEN = 38
+SHARE_LAST_HALF = 38
+SHARE_FIRST_HALF = 48
 
 STAGING_BUFS = 9
 CODES_BUFS = 5
@@ -238,7 +239,7 @@ def tile_routed_moe_kernel(tc, xT, w1, w3, w2, gate, offs, out):
             interleave(0, W1, g, SHARE_BESIDE_GATHERS)
             first_layer(0, W1, g)
         for g in range(PASSES):
-            interleave(0, W3, g, SHARE_BESIDE_RELU)
+            interleave(0, W3, g, 32)
             first_layer(0, W3, g)
             if g == 0:
                 rectify(0)
@@ -260,7 +261,7 @@ def tile_routed_moe_kernel(tc, xT, w1, w3, w2, gate, offs, out):
         interleave(1, W3, 2, SHARE_FIRST_HALF, COLUMN_HALVES[0])
         first_layer(1, W3, 1)
         first_layer(1, W3, 2, COLUMN_HALVES[0])
-        interleave(1, W3, 2, SHARE_BESIDE_RELU, COLUMN_HALVES[1])
+        interleave(1, W3, 2, SHARE_LAST_HALF, COLUMN_HALVES[1])
         first_layer(1, W3, 2, COLUMN_HALVES[1])
 
         quantise_w2(0)

@@ -1,7 +1,6 @@
 from contextlib import ExitStack
 
 import concourse.mybir as mybir
-from concourse.masks import make_identity
 
 K, T, E, C, H, N = 1536, 1024, 2, 256, 512, 128
 FLOPS = 2 * E * C * (2 * K * H + H * N)
@@ -27,17 +26,10 @@ W1, W3 = 0, 1
 ALL_COLUMNS = (0, H)
 COLUMN_HALVES = ((0, H // 2), (H // 2, H))
 
-SHARE_BESIDE_GATHERS = 44
-SHARE_BESIDE_RELU = 24
-SHARE_EVEN = 38
-SHARE_LAST_HALF = 38
-SHARE_FIRST_HALF = 48
-
 STAGING_BUFS = 9
 CODES_BUFS = 5
 SUM_BANKS = 6
-SHORT_BANKS = 2
-H_CODE_BUFS = 3
+Y_BANKS = 2
 
 
 def tile_routed_moe_kernel(tc, xT, w1, w3, w2, gate, offs, out):
@@ -52,36 +44,35 @@ def tile_routed_moe_kernel(tc, xT, w1, w3, w2, gate, offs, out):
     def interleaved_order(ap):
         return ap.rearrange("p (c r j) -> p c j r", r=RUN, j=J)
 
-    def sums_by_word(ap):
-        return ap.rearrange("s (w u b) -> s u w b", u=2, b=2)
+    def loaded_by_block(ap):
+        return ap.rearrange("p j (m t) -> p m j t", t=J)
 
-    def stored_by_word(ap):
-        return ap.rearrange("s (u w b) -> s u w b", u=2, b=2)
+    def interleaved_by_block(ap):
+        return ap.rearrange("p (t m j) -> p m j t", t=J, j=J)
+
+    def sums_by_slot(ap):
+        return ap.rearrange("p t n -> p n t")
+
+    def stored_by_slot(ap):
+        return ap.rearrange("p (n t) -> p n t", t=J)
 
     with ExitStack() as ctx:
         keep = ctx.enter_context(tc.tile_pool(name="keep", bufs=1))
         stage = ctx.enter_context(tc.tile_pool(name="stage", bufs=4))
         small = ctx.enter_context(tc.tile_pool(name="small", bufs=E))
-        psum = ctx.enter_context(tc.psum_pool(name="psum", bufs=SUM_BANKS + SHORT_BANKS))
+        psum = ctx.enter_context(tc.psum_pool(name="psum", bufs=SUM_BANKS + Y_BANKS))
 
         def staging(shape, dtype, name):
             return stage.tile(shape, dtype, name=name, tag="staging", align_bytes=64, bufs=STAGING_BUFS)
 
-        def codes_ring(shape, dtype, name):
-            return stage.tile(shape, dtype, name=name, tag="codes", align_bytes=64, bufs=CODES_BUFS)
-
-        def h_ring(shape, dtype, name):
-            return small.tile(shape, dtype, name=name, tag="h_words", align_bytes=64, bufs=H_CODE_BUFS)
-
         offsets = keep.tile([P, SLOTS // LIST_COLUMN], U16, name="offsets")
         window = keep.tile([P, T], F32, name="window")
-        identity = keep.tile([P, P], F32, name="identity")
         nc.vector.memset(window[:], 0.0)
-        make_identity(nc, identity[:])
 
         x_raw = {}
         w_raw = {}
         w2_raw = {}
+        gates = {}
 
         def load_passes(e, m, first, last):
             tile = keep.tile([P, last - first, J, H], F32, name=f"w_raw{e}{m}{first}")
@@ -89,27 +80,36 @@ def tile_routed_moe_kernel(tc, xT, w1, w3, w2, gate, offs, out):
             for g in range(first, last):
                 w_raw[e, m, g, ALL_COLUMNS] = tile[:, g - first]
 
+        def load_w2(e):
+            w2_raw[e] = keep.tile([P, J, N], F32, name=f"w2_raw{e}")
+            nc.sync.dma_start(out=w2_raw[e][:], in_=w2_view[e])
+
+        def load_gate(e):
+            gates[e] = keep.tile([P, C], F32, name=f"gates{e}")
+            nc.sync.dma_start(out=gates[e][:], in_=gate[:, e * C : (e + 1) * C])
+
         for g in range(PASSES):
             x_raw[g] = keep.tile([P, J, T], F32, name=f"x_raw{g}")
             nc.sync.dma_start(out=x_raw[g][:], in_=xT_view[g])
             if g == 0:
                 nc.sync.dma_start(offsets[:], offs)
-        for m in (W1, W3):
-            load_passes(0, m, 0, PASSES - 1)
-            load_passes(0, m, PASSES - 1, PASSES)
+        load_passes(0, W1, 0, PASSES - 1)
+        load_passes(0, W1, PASSES - 1, PASSES)
         for g in range(PASSES):
-            load_passes(1, W1, g, g + 1)
+            load_passes(0, W3, g, g + 1)
+        load_passes(1, W1, 0, 1)
+        load_w2(0)
+        load_passes(1, W1, 1, 2)
+        load_gate(0)
+        load_passes(1, W1, 2, 3)
         for g in range(PASSES - 1):
             load_passes(1, W3, g, g + 1)
         for first, last in COLUMN_HALVES:
             tile = keep.tile([P, J, last - first], F32, name=f"w_half{first}")
             nc.sync.dma_start(out=tile[:], in_=w_views[W3][1, :, PASSES - 1, :, first:last])
             w_raw[1, W3, PASSES - 1, (first, last)] = tile[:]
-        for e in range(E):
-            w2_raw[e] = keep.tile([P, J, N], F32, name=f"w2_raw{e}")
-            nc.sync.dma_start(out=w2_raw[e][:], in_=w2_view[e])
-        gates = keep.tile([P, SLOTS], F32, name="gates")
-        nc.sync.dma_start(out=gates[:], in_=gate)
+        load_w2(1)
+        load_gate(1)
 
         slot_words = {}
         token_bytes = keep.tile([P, T], U8, name="token_bytes", align_bytes=64)
@@ -131,85 +131,101 @@ def tile_routed_moe_kernel(tc, xT, w1, w3, w2, gate, offs, out):
             nc.vector.tensor_copy(slot_words[g][:], token_words[:].indirect(offsets[:]))
 
         w_interleaved = {}
+        w_codes = {}
         sums = {}
         rectified = {}
         hidden = {}
-        h_interleaved = {}
         h_codes = {}
         w2_codes = {}
 
-        def sum_ranges(e, m):
-            return COLUMN_HALVES if (e, m) == (1, W3) else (ALL_COLUMNS,)
-
-        def interleave(e, m, g, share, columns=ALL_COLUMNS):
-            width = columns[1] - columns[0]
-            tile = staging([P, width * J], BF16, "w_interleaved")
-            target = interleaved_order(tile[:])
-            source = loaded_order(w_raw[e, m, g, columns])
-            cut = width * share // 64 // RUN
-            nc.scalar.copy(target[:, :cut], source[:, :cut])
-            nc.vector.tensor_copy(target[:, cut:], source[:, cut:])
+        def round_on_vector(e, m, g, columns=ALL_COLUMNS):
+            tile = staging([P, (columns[1] - columns[0]) * J], BF16, "w_interleaved")
             w_interleaved[e, m, g, columns] = tile
+            target = interleaved_by_block(tile[:])
+            source = loaded_by_block(w_raw[e, m, g, columns])
+            nc.vector.tensor_copy(target[:, :, :, : J // 2], source[:, :, :, : J // 2])
 
-        def first_layer(e, m, g, columns=ALL_COLUMNS):
-            width = columns[1] - columns[0]
-            words = codes_ring([P, width], U32, "w_words")
-            scales = stage.tile([P, width], U8, name="w_bytes", align_bytes=64)
-            nc.vector.quantize_mx(
-                out=words[:].bitcast(FP8X4), scales=scales[:], in_=w_interleaved[e, m, g, columns][:]
-            )
-            for first, last in sum_ranges(e, m):
-                if columns[0] <= first < columns[1]:
-                    moving = slice(first - columns[0], last - columns[0])
-                    for s in range(GROUPS):
-                        slots = slice(e * C + s * P, e * C + (s + 1) * P)
-                        if g == 0:
-                            sums[e, m, first, s] = psum.tile([P, last - first], F32, name="sums", bufs=SUM_BANKS)
-                        nc.tensor.matmul_mx(
-                            out=sums[e, m, first, s][:],
-                            lhsT=slot_words[g][:, slots].bitcast(FP8X4),
-                            lhsT_scale=slot_bytes[4 * g :, slots],
-                            rhs=words[:, moving].bitcast(FP8X4),
-                            rhs_scale=scales[:, moving],
-                            start=(g == 0),
-                            stop=(g == PASSES - 1),
-                        )
+        def round_on_scalar(e, m, g, columns=ALL_COLUMNS):
+            target = interleaved_by_block(w_interleaved[e, m, g, columns][:])
+            source = loaded_by_block(w_raw[e, m, g, columns])
+            nc.scalar.copy(target[:, :, :, J // 2 :], source[:, :, :, J // 2 :])
+
+        def interleave(e, m, g, columns=ALL_COLUMNS):
+            round_on_vector(e, m, g, columns)
+            round_on_scalar(e, m, g, columns)
+
+        def interleave_on_scalar(e, m, g):
+            tile = staging([P, H * J], BF16, "w_interleaved")
+            w_interleaved[e, m, g, ALL_COLUMNS] = tile
+            nc.scalar.copy(interleaved_by_block(tile[:]), loaded_by_block(w_raw[e, m, g, ALL_COLUMNS]))
+
+        def quantise(e, m, g, columns=ALL_COLUMNS):
+            if columns[0] == 0:
+                words = stage.tile([P, H], U32, name="w_words", align_bytes=64, bufs=CODES_BUFS)
+                scales = stage.tile([P, H], U8, name="w_bytes", align_bytes=64, bufs=CODES_BUFS)
+                w_codes[e, m, g] = (words, scales)
+            words, scales = w_codes[e, m, g]
+            source = w_interleaved[e, m, g, columns]
+            if columns == ALL_COLUMNS:
+                nc.vector.quantize_mx(out=words[:].bitcast(FP8X4), scales=scales[:], in_=source[:])
+            else:
+                width = columns[1] - columns[0]
+                for t in (2, 3, 0, 1):
+                    place = slice(t * P + columns[0] // J, t * P + columns[1] // J)
+                    nc.vector.quantize_mx(
+                        out=words[:, place].bitcast(FP8X4),
+                        scales=scales[:, place],
+                        in_=source[:, t * width : (t + 1) * width],
+                    )
+
+        def first_layer(e, m, g):
+            words, scales = w_codes[e, m, g]
+            for s in range(GROUPS):
+                slots = slice(e * C + s * P, e * C + (s + 1) * P)
+                if g == 0:
+                    sums[e, m, s] = psum.tile([P, J, P], F32, name="sums", bufs=SUM_BANKS)
+                for turn, t in enumerate((2, 3, 0, 1)):
+                    block = slice(t * P, (t + 1) * P)
+                    nc.tensor.matmul_mx(
+                        out=sums[e, m, s][:, t, :],
+                        lhsT=words[:, block].bitcast(FP8X4),
+                        lhsT_scale=scales[:, block],
+                        rhs=slot_words[g][:, slots].bitcast(FP8X4),
+                        rhs_scale=slot_bytes[4 * g :, slots],
+                        start=(g == 0 and turn == 0),
+                        stop=(g == PASSES - 1 and turn == J - 1),
+                    )
+
+        def chunk(e, m, g):
+            quantise(e, m, g)
+            first_layer(e, m, g)
 
         def rectify(e):
             rectified[e] = staging([P, GROUPS, H], F32, "rectified")
             for s in range(GROUPS):
-                nc.scalar.activation(stored_by_word(rectified[e][:, s, :]), sums_by_word(sums[e, W1, 0, s][:]), RELU)
+                nc.scalar.activation(stored_by_slot(rectified[e][:, s, :]), sums_by_slot(sums[e, W1, s][:]), RELU)
 
         def multiply(e):
-            hidden[e] = codes_ring([P, GROUPS, H], BF16, "hidden")
-            for first, last in sum_ranges(e, W3):
-                words = slice(first // J, last // J)
-                for s in range(GROUPS):
-                    nc.vector.tensor_tensor(
-                        stored_by_word(hidden[e][:, s, :])[:, :, words],
-                        sums_by_word(sums[e, W3, first, s][:]),
-                        stored_by_word(rectified[e][:, s, :])[:, :, words],
-                        MULT,
-                    )
+            hidden[e] = small.tile([P, GROUPS * H], BF16, name="hidden", align_bytes=64)
+            for s in range(GROUPS):
+                nc.vector.tensor_tensor(
+                    stored_by_slot(hidden[e][:, s * H : (s + 1) * H]),
+                    sums_by_slot(sums[e, W3, s][:]),
+                    stored_by_slot(rectified[e][:, s, :]),
+                    MULT,
+                )
 
-        def turn_hidden(e, groups):
-            turned = psum.tile([P, len(groups), 2, P], F32, name="short", bufs=SHORT_BANKS)
-            for a, s in enumerate(groups):
-                pairs = hidden[e][:, s, :].bitcast(F32)
-                for u in range(2):
-                    nc.tensor.transpose(turned[:, a, u, :], pairs[:, u * P : (u + 1) * P], identity[:])
-            tile = staging([P, len(groups) * P * J], BF16, "h_interleaved")
-            nc.scalar.copy(
-                tile[:].bitcast(F32).rearrange("p (a n u) -> p a n u", a=len(groups), u=2),
-                turned[:].rearrange("p a u n -> p a n u"),
+        def quantise_hidden(e, first, last):
+            if first == 0:
+                words = small.tile([P, C], U32, name="h_words", align_bytes=64)
+                scales = small.tile([P, C], U8, name="h_bytes", align_bytes=64)
+                h_codes[e] = (words, scales)
+            words, scales = h_codes[e]
+            nc.vector.quantize_mx(
+                out=words[:, first:last].bitcast(FP8X4),
+                scales=scales[:, first:last],
+                in_=hidden[e][:, first * J : last * J],
             )
-            h_interleaved[e, groups] = tile
-
-        def quantise_hidden(e, groups):
-            words = h_ring([P, len(groups) * P], U32, "h_words")
-            scales = small.tile([P, len(groups) * P], U8, name="h_bytes", align_bytes=64, bufs=H_CODE_BUFS)
-            nc.vector.quantize_mx(out=words[:].bitcast(FP8X4), scales=scales[:], in_=h_interleaved[e, groups][:])
-            h_codes[e, groups] = (words, scales)
 
         def quantise_w2(e):
             interleaved = small.tile([P, N * J], BF16, name="w2_interleaved", align_bytes=64)
@@ -219,70 +235,63 @@ def tile_routed_moe_kernel(tc, xT, w1, w3, w2, gate, offs, out):
             nc.vector.quantize_mx(out=words[:].bitcast(FP8X4), scales=scales[:], in_=interleaved[:])
             w2_codes[e] = (words, scales)
 
-        def second_layer(e, groups, bank):
+        def second_layer(e, first, last):
+            bank = psum.tile([P, last - first], F32, name="y_bank", bufs=Y_BANKS)
             nc.tensor.matmul_mx(
                 out=bank[:],
                 lhsT=w2_codes[e][0][:].bitcast(FP8X4),
                 lhsT_scale=w2_codes[e][1][:],
-                rhs=h_codes[e, groups][0][:].bitcast(FP8X4),
-                rhs_scale=h_codes[e, groups][1][:],
+                rhs=h_codes[e][0][:, first:last].bitcast(FP8X4),
+                rhs_scale=h_codes[e][1][:, first:last],
                 start=True,
                 stop=True,
             )
+            return bank
 
-        def put_back(y, first, last):
-            entries = offsets[:, first // LIST_COLUMN : last // LIST_COLUMN]
-            nc.vector.tensor_tensor(window[:].indirect(entries), y[:], gates[:, first:last], MULT)
+        def put_back(e, y, first, last):
+            entries = offsets[:, (e * C + first) // LIST_COLUMN : (e * C + last) // LIST_COLUMN]
+            nc.vector.tensor_tensor(window[:].indirect(entries), y[:], gates[e][:, first:last], MULT)
 
-        both = tuple(range(GROUPS))
         for g in range(PASSES):
-            interleave(0, W1, g, SHARE_BESIDE_GATHERS)
-            first_layer(0, W1, g)
+            interleave(0, W1, g)
+            chunk(0, W1, g)
         for g in range(PASSES):
-            interleave(0, W3, g, 32)
-            first_layer(0, W3, g)
+            interleave(0, W3, g)
+            chunk(0, W3, g)
             if g == 0:
                 rectify(0)
 
-        interleave(1, W1, 0, SHARE_EVEN)
+        interleave_on_scalar(1, W1, 0)
         multiply(0)
-        first_layer(1, W1, 0)
-        interleave(1, W1, 1, SHARE_EVEN)
-        turn_hidden(0, both)
-        first_layer(1, W1, 1)
-        quantise_hidden(0, both)
-        interleave(1, W1, 2, SHARE_EVEN)
-        first_layer(1, W1, 2)
-
-        interleave(1, W3, 0, SHARE_BESIDE_RELU)
-        first_layer(1, W3, 0)
-        rectify(1)
-        interleave(1, W3, 1, SHARE_BESIDE_RELU)
-        interleave(1, W3, 2, SHARE_FIRST_HALF, COLUMN_HALVES[0])
-        first_layer(1, W3, 1)
-        first_layer(1, W3, 2, COLUMN_HALVES[0])
-        interleave(1, W3, 2, SHARE_LAST_HALF, COLUMN_HALVES[1])
-        first_layer(1, W3, 2, COLUMN_HALVES[1])
-
+        chunk(1, W1, 0)
+        quantise_hidden(0, 0, C)
         quantise_w2(0)
-        first_bank = psum.tile([P, C], F32, name="sums", bufs=SUM_BANKS)
-        second_layer(0, both, first_bank)
-        multiply(1)
-        y_early = staging([P, P], F32, "y_early")
-        nc.scalar.copy(y_early[:], first_bank[:, :P])
+        first_bank = second_layer(0, 0, C)
+        interleave(1, W1, 1)
+        chunk(1, W1, 1)
+        for s, (m, g) in enumerate(((W1, 2), (W3, 0))):
+            round_on_vector(1, m, g)
+            y = staging([P, P], F32, "y_first")
+            nc.scalar.copy(y[:], first_bank[:, s * P : (s + 1) * P])
+            round_on_scalar(1, m, g)
+            put_back(0, y, s * P, (s + 1) * P)
+            chunk(1, m, g)
+        interleave(1, W3, 1)
+        interleave(1, W3, 2, COLUMN_HALVES[0])
+        chunk(1, W3, 1)
+        quantise(1, W3, 2, COLUMN_HALVES[0])
+        interleave(1, W3, 2, COLUMN_HALVES[1])
+        quantise(1, W3, 2, COLUMN_HALVES[1])
+        first_layer(1, W3, 2)
         quantise_w2(1)
-        put_back(y_early, 0, P)
+        rectify(1)
+
+        multiply(1)
+        y_last = small.tile([P, C], F32, name="y_last")
         for s in range(GROUPS):
-            turn_hidden(1, (s,))
-        quantise_hidden(1, (0,))
-        y_late = h_ring([P, P], F32, "y_late")
-        nc.scalar.copy(y_late[:], first_bank[:, P:])
-        quantise_hidden(1, (1,))
-        put_back(y_late, P, C)
-        y_last = staging([P, C], F32, "y_last")
+            quantise_hidden(1, s * P, (s + 1) * P)
         for s in range(GROUPS):
-            bank = psum.tile([P, P], F32, name="short", bufs=SHORT_BANKS)
-            second_layer(1, (s,), bank)
+            bank = second_layer(1, s * P, (s + 1) * P)
             nc.scalar.copy(y_last[:, s * P : (s + 1) * P], bank[:])
-        put_back(y_last, C, SLOTS)
+        put_back(1, y_last, 0, C)
         nc.sync.dma_start(out=out, in_=window[:])

@@ -1,6 +1,7 @@
 from contextlib import ExitStack
 
 import concourse.mybir as mybir
+from concourse.masks import make_identity
 
 K, T, E, C, H, N = 1536, 1024, 2, 256, 512, 128
 FLOPS = 2 * E * C * (2 * K * H + H * N)
@@ -26,6 +27,10 @@ W1, W3 = 0, 1
 ALL_COLUMNS = (0, H)
 COLUMN_HALVES = ((0, H // 2), (H // 2, H))
 
+SHARE_BESIDE_GATHERS = 48
+SHARE_PLAIN = 36
+SHARE_BESIDE_RELU = 30
+
 STAGING_BUFS = 9
 CODES_BUFS = 5
 SUM_BANKS = 6
@@ -37,6 +42,7 @@ def tile_routed_moe_kernel(tc, xT, w1, w3, w2, gate, offs, out):
     xT_view = xT.rearrange("(g p j) n -> g p j n", p=P, j=J)
     w_views = [w.rearrange("e (g p j) n -> e p g j n", p=P, j=J) for w in (w1, w3)]
     w2_view = w2.rearrange("e (p j) n -> e p j n", j=J)
+    w2_by_block = w2.rearrange("e (m t l) n -> e l m t n", t=J, l=2)
 
     def loaded_order(ap):
         return ap.rearrange("p j (c r) -> p c j r", r=RUN)
@@ -45,16 +51,25 @@ def tile_routed_moe_kernel(tc, xT, w1, w3, w2, gate, offs, out):
         return ap.rearrange("p (c r j) -> p c j r", r=RUN, j=J)
 
     def loaded_by_block(ap):
-        return ap.rearrange("p j (m t) -> p m j t", t=J)
+        return ap.rearrange("p j (m t l) -> p m j t l", t=J, l=2)
 
     def interleaved_by_block(ap):
-        return ap.rearrange("p (t m j) -> p m j t", t=J, j=J)
+        return ap.rearrange("p (t m l j) -> p m j t l", t=J, l=2, j=J)
 
-    def sums_by_slot(ap):
-        return ap.rearrange("p t n -> p n t")
+    def sums_by_word(ap):
+        return ap.rearrange("s (w u b) -> s u w b", u=2, b=2)
 
-    def stored_by_slot(ap):
-        return ap.rearrange("p (n t) -> p n t", t=J)
+    def stored_by_word(ap):
+        return ap.rearrange("s (u w b) -> s u w b", u=2, b=2)
+
+    def sums_by_pair(ap):
+        return ap.rearrange("p t (c r) -> p c t r", r=2)
+
+    def stored_by_pair(ap):
+        return ap.rearrange("p (c t r) -> p c t r", t=J, r=2)
+
+    def interleaved_by_pair(ap):
+        return ap.rearrange("p (c r t) -> p c t r", t=J, r=2)
 
     with ExitStack() as ctx:
         keep = ctx.enter_context(tc.tile_pool(name="keep", bufs=1))
@@ -67,7 +82,9 @@ def tile_routed_moe_kernel(tc, xT, w1, w3, w2, gate, offs, out):
 
         offsets = keep.tile([P, SLOTS // LIST_COLUMN], U16, name="offsets")
         window = keep.tile([P, T], F32, name="window")
+        identity = keep.tile([P, P], F32, name="identity")
         nc.vector.memset(window[:], 0.0)
+        make_identity(nc, identity[:])
 
         x_raw = {}
         w_raw = {}
@@ -82,7 +99,11 @@ def tile_routed_moe_kernel(tc, xT, w1, w3, w2, gate, offs, out):
 
         def load_w2(e):
             w2_raw[e] = keep.tile([P, J, N], F32, name=f"w2_raw{e}")
-            nc.sync.dma_start(out=w2_raw[e][:], in_=w2_view[e])
+            if e == 0:
+                nc.sync.dma_start(out=w2_raw[e][:], in_=w2_view[e])
+            else:
+                for l in range(2):
+                    nc.sync.dma_start(out=w2_raw[e][l::2], in_=w2_by_block[e, l])
 
         def load_gate(e):
             gates[e] = keep.tile([P, C], F32, name=f"gates{e}")
@@ -138,26 +159,25 @@ def tile_routed_moe_kernel(tc, xT, w1, w3, w2, gate, offs, out):
         h_codes = {}
         w2_codes = {}
 
-        def round_on_vector(e, m, g, columns=ALL_COLUMNS):
+        def interleave_first(m, g, share):
+            tile = staging([P, H * J], BF16, "w_interleaved")
+            target = interleaved_order(tile[:])
+            source = loaded_order(w_raw[0, m, g, ALL_COLUMNS])
+            cut = H * share // 64 // RUN
+            nc.scalar.copy(target[:, :cut], source[:, :cut])
+            nc.vector.tensor_copy(target[:, cut:], source[:, cut:])
+            w_interleaved[0, m, g, ALL_COLUMNS] = tile
+
+        def interleave(e, m, g, columns=ALL_COLUMNS, copies=(nc.vector.tensor_copy, nc.scalar.copy)):
             tile = staging([P, (columns[1] - columns[0]) * J], BF16, "w_interleaved")
             w_interleaved[e, m, g, columns] = tile
             target = interleaved_by_block(tile[:])
             source = loaded_by_block(w_raw[e, m, g, columns])
-            nc.vector.tensor_copy(target[:, :, :, : J // 2], source[:, :, :, : J // 2])
-
-        def round_on_scalar(e, m, g, columns=ALL_COLUMNS):
-            target = interleaved_by_block(w_interleaved[e, m, g, columns][:])
-            source = loaded_by_block(w_raw[e, m, g, columns])
-            nc.scalar.copy(target[:, :, :, J // 2 :], source[:, :, :, J // 2 :])
-
-        def interleave(e, m, g, columns=ALL_COLUMNS):
-            round_on_vector(e, m, g, columns)
-            round_on_scalar(e, m, g, columns)
+            for pair, copy in enumerate(copies):
+                copy(target[:, :, :, 2 * pair : 2 * pair + 2], source[:, :, :, 2 * pair : 2 * pair + 2])
 
         def interleave_on_scalar(e, m, g):
-            tile = staging([P, H * J], BF16, "w_interleaved")
-            w_interleaved[e, m, g, ALL_COLUMNS] = tile
-            nc.scalar.copy(interleaved_by_block(tile[:]), loaded_by_block(w_raw[e, m, g, ALL_COLUMNS]))
+            interleave(e, m, g, ALL_COLUMNS, (nc.scalar.copy, nc.scalar.copy))
 
         def quantise(e, m, g, columns=ALL_COLUMNS):
             if columns[0] == 0:
@@ -196,22 +216,66 @@ def tile_routed_moe_kernel(tc, xT, w1, w3, w2, gate, offs, out):
                         stop=(g == PASSES - 1 and turn == J - 1),
                     )
 
+        def first_layer_by_slots(m, g):
+            words, scales = w_codes[0, m, g]
+            for s in range(GROUPS):
+                slots = slice(s * P, (s + 1) * P)
+                if g == 0:
+                    sums[0, m, s] = psum.tile([P, H], F32, name="sums", bufs=SUM_BANKS)
+                nc.tensor.matmul_mx(
+                    out=sums[0, m, s][:],
+                    lhsT=slot_words[g][:, slots].bitcast(FP8X4),
+                    lhsT_scale=slot_bytes[4 * g :, slots],
+                    rhs=words[:].bitcast(FP8X4),
+                    rhs_scale=scales[:],
+                    start=(g == 0),
+                    stop=(g == PASSES - 1),
+                )
+
         def chunk(e, m, g):
             quantise(e, m, g)
-            first_layer(e, m, g)
+            if e == 0:
+                first_layer_by_slots(m, g)
+            else:
+                first_layer(e, m, g)
 
         def rectify(e):
             rectified[e] = staging([P, GROUPS, H], F32, "rectified")
             for s in range(GROUPS):
-                nc.scalar.activation(stored_by_slot(rectified[e][:, s, :]), sums_by_slot(sums[e, W1, s][:]), RELU)
+                if e == 0:
+                    nc.scalar.activation(stored_by_word(rectified[e][:, s, :]), sums_by_word(sums[e, W1, s][:]), RELU)
+                else:
+                    nc.scalar.activation(stored_by_pair(rectified[e][:, s, :]), sums_by_pair(sums[e, W1, s][:]), RELU)
+
+        def multiply_by_slots():
+            hidden["rows"] = small.tile([P, GROUPS, H], BF16, name="hidden_rows", align_bytes=64, bufs=1)
+            for s in range(GROUPS):
+                nc.vector.tensor_tensor(
+                    stored_by_word(hidden["rows"][:, s, :]),
+                    sums_by_word(sums[0, W3, s][:]),
+                    stored_by_word(rectified[0][:, s, :]),
+                    MULT,
+                )
+
+        def turn_hidden():
+            turned = psum.tile([P, GROUPS, 2, P], F32, name="y_bank", bufs=Y_BANKS)
+            for s in range(GROUPS):
+                pairs = hidden["rows"][:, s, :].bitcast(F32)
+                for u in range(2):
+                    nc.tensor.transpose(turned[:, s, u, :], pairs[:, u * P : (u + 1) * P], identity[:])
+            hidden[0] = small.tile([P, GROUPS * H], BF16, name="hidden", align_bytes=64)
+            nc.scalar.copy(
+                hidden[0][:].bitcast(F32).rearrange("p (a n u) -> p a n u", a=GROUPS, u=2),
+                turned[:].rearrange("p a u n -> p a n u"),
+            )
 
         def multiply(e):
             hidden[e] = small.tile([P, GROUPS * H], BF16, name="hidden", align_bytes=64)
             for s in range(GROUPS):
                 nc.vector.tensor_tensor(
-                    stored_by_slot(hidden[e][:, s * H : (s + 1) * H]),
-                    sums_by_slot(sums[e, W3, s][:]),
-                    stored_by_slot(rectified[e][:, s, :]),
+                    interleaved_by_pair(hidden[e][:, s * H : (s + 1) * H]),
+                    sums_by_pair(sums[e, W3, s][:]),
+                    stored_by_pair(rectified[e][:, s, :]),
                     MULT,
                 )
 
@@ -253,29 +317,30 @@ def tile_routed_moe_kernel(tc, xT, w1, w3, w2, gate, offs, out):
             nc.vector.tensor_tensor(window[:].indirect(entries), y[:], gates[e][:, first:last], MULT)
 
         for g in range(PASSES):
-            interleave(0, W1, g)
+            interleave_first(W1, g, SHARE_BESIDE_GATHERS if g < PASSES - 1 else SHARE_PLAIN)
             chunk(0, W1, g)
         for g in range(PASSES):
-            interleave(0, W3, g)
+            interleave_first(W3, g, SHARE_BESIDE_RELU if g == 1 else SHARE_PLAIN)
             chunk(0, W3, g)
             if g == 0:
                 rectify(0)
 
         interleave_on_scalar(1, W1, 0)
-        multiply(0)
+        multiply_by_slots()
         chunk(1, W1, 0)
-        quantise_hidden(0, 0, C)
         quantise_w2(0)
-        first_bank = second_layer(0, 0, C)
+        turn_hidden()
         interleave(1, W1, 1)
+        quantise_hidden(0, 0, C)
+        first_bank = second_layer(0, 0, C)
         chunk(1, W1, 1)
-        for s, (m, g) in enumerate(((W1, 2), (W3, 0))):
-            round_on_vector(1, m, g)
-            y = staging([P, P], F32, "y_first")
-            nc.scalar.copy(y[:], first_bank[:, s * P : (s + 1) * P])
-            round_on_scalar(1, m, g)
-            put_back(0, y, s * P, (s + 1) * P)
-            chunk(1, m, g)
+        y_first = staging([P, C], F32, "y_first")
+        nc.scalar.copy(y_first[:], first_bank[:])
+        interleave_on_scalar(1, W1, 2)
+        put_back(0, y_first, 0, C)
+        chunk(1, W1, 2)
+        interleave(1, W3, 0)
+        chunk(1, W3, 0)
         interleave(1, W3, 1)
         interleave(1, W3, 2, COLUMN_HALVES[0])
         chunk(1, W3, 1)
@@ -283,10 +348,10 @@ def tile_routed_moe_kernel(tc, xT, w1, w3, w2, gate, offs, out):
         interleave(1, W3, 2, COLUMN_HALVES[1])
         quantise(1, W3, 2, COLUMN_HALVES[1])
         first_layer(1, W3, 2)
-        quantise_w2(1)
         rectify(1)
 
         multiply(1)
+        quantise_w2(1)
         y_last = small.tile([P, C], F32, name="y_last")
         for s in range(GROUPS):
             quantise_hidden(1, s * P, (s + 1) * P)

@@ -35,6 +35,7 @@ STAGING_BUFS = 9
 CODES_BUFS = 5
 SUM_BANKS = 6
 Y_BANKS = 2
+LAST_BUFS = 7
 
 
 def tile_routed_moe_kernel(tc, xT, w1, w3, w2, gate, offs, out):
@@ -42,7 +43,7 @@ def tile_routed_moe_kernel(tc, xT, w1, w3, w2, gate, offs, out):
     xT_view = xT.rearrange("(g p j) n -> g p j n", p=P, j=J)
     w_views = [w.rearrange("e (g p j) n -> e p g j n", p=P, j=J) for w in (w1, w3)]
     w2_view = w2.rearrange("e (p j) n -> e p j n", j=J)
-    w2_by_block = w2.rearrange("e (m t l) n -> e l m t n", t=J, l=2)
+    w2_by_block = w2.rearrange("e (m t l) n -> e l m t n", t=J, l=RUN)
 
     def loaded_order(ap):
         return ap.rearrange("p j (c r) -> p c j r", r=RUN)
@@ -51,10 +52,10 @@ def tile_routed_moe_kernel(tc, xT, w1, w3, w2, gate, offs, out):
         return ap.rearrange("p (c r j) -> p c j r", r=RUN, j=J)
 
     def loaded_by_block(ap):
-        return ap.rearrange("p j (m t l) -> p m j t l", t=J, l=2)
+        return ap.rearrange("p j (m t l) -> p t m j l", t=J, l=RUN)
 
     def interleaved_by_block(ap):
-        return ap.rearrange("p (t m l j) -> p m j t l", t=J, l=2, j=J)
+        return ap.rearrange("p (t m l j) -> p t m j l", t=J, l=RUN, j=J)
 
     def sums_by_word(ap):
         return ap.rearrange("s (w u b) -> s u w b", u=2, b=2)
@@ -102,8 +103,8 @@ def tile_routed_moe_kernel(tc, xT, w1, w3, w2, gate, offs, out):
             if e == 0:
                 nc.sync.dma_start(out=w2_raw[e][:], in_=w2_view[e])
             else:
-                for l in range(2):
-                    nc.sync.dma_start(out=w2_raw[e][l::2], in_=w2_by_block[e, l])
+                for l in range(RUN):
+                    nc.sync.dma_start(out=w2_raw[e][l::RUN], in_=w2_by_block[e, l])
 
         def load_gate(e):
             gates[e] = keep.tile([P, C], F32, name=f"gates{e}")
@@ -158,6 +159,7 @@ def tile_routed_moe_kernel(tc, xT, w1, w3, w2, gate, offs, out):
         hidden = {}
         h_codes = {}
         w2_codes = {}
+        w2_interleaved = {}
 
         def interleave_first(m, g, share):
             tile = staging([P, H * J], BF16, "w_interleaved")
@@ -174,7 +176,7 @@ def tile_routed_moe_kernel(tc, xT, w1, w3, w2, gate, offs, out):
             target = interleaved_by_block(tile[:])
             source = loaded_by_block(w_raw[e, m, g, columns])
             for pair, copy in enumerate(copies):
-                copy(target[:, :, :, 2 * pair : 2 * pair + 2], source[:, :, :, 2 * pair : 2 * pair + 2])
+                copy(target[:, 2 * pair : 2 * pair + 2], source[:, 2 * pair : 2 * pair + 2])
 
         def interleave_on_scalar(e, m, g):
             interleave(e, m, g, ALL_COLUMNS, (nc.scalar.copy, nc.scalar.copy))
@@ -190,7 +192,7 @@ def tile_routed_moe_kernel(tc, xT, w1, w3, w2, gate, offs, out):
                 nc.vector.quantize_mx(out=words[:].bitcast(FP8X4), scales=scales[:], in_=source[:])
             else:
                 width = columns[1] - columns[0]
-                for t in (2, 3, 0, 1):
+                for t in range(J):
                     place = slice(t * P + columns[0] // J, t * P + columns[1] // J)
                     nc.vector.quantize_mx(
                         out=words[:, place].bitcast(FP8X4),
@@ -204,7 +206,7 @@ def tile_routed_moe_kernel(tc, xT, w1, w3, w2, gate, offs, out):
                 slots = slice(e * C + s * P, e * C + (s + 1) * P)
                 if g == 0:
                     sums[e, m, s] = psum.tile([P, J, P], F32, name="sums", bufs=SUM_BANKS)
-                for turn, t in enumerate((2, 3, 0, 1)):
+                for t in range(J):
                     block = slice(t * P, (t + 1) * P)
                     nc.tensor.matmul_mx(
                         out=sums[e, m, s][:, t, :],
@@ -212,8 +214,8 @@ def tile_routed_moe_kernel(tc, xT, w1, w3, w2, gate, offs, out):
                         lhsT_scale=scales[:, block],
                         rhs=slot_words[g][:, slots].bitcast(FP8X4),
                         rhs_scale=slot_bytes[4 * g :, slots],
-                        start=(g == 0 and turn == 0),
-                        stop=(g == PASSES - 1 and turn == J - 1),
+                        start=(g == 0 and t == 0),
+                        stop=(g == PASSES - 1 and t == J - 1),
                     )
 
         def first_layer_by_slots(m, g):
@@ -239,13 +241,14 @@ def tile_routed_moe_kernel(tc, xT, w1, w3, w2, gate, offs, out):
             else:
                 first_layer(e, m, g)
 
-        def rectify(e):
-            rectified[e] = staging([P, GROUPS, H], F32, "rectified")
+        def rectify_first():
+            rectified[0] = staging([P, GROUPS, H], F32, "rectified")
             for s in range(GROUPS):
-                if e == 0:
-                    nc.scalar.activation(stored_by_word(rectified[e][:, s, :]), sums_by_word(sums[e, W1, s][:]), RELU)
-                else:
-                    nc.scalar.activation(stored_by_pair(rectified[e][:, s, :]), sums_by_pair(sums[e, W1, s][:]), RELU)
+                nc.scalar.activation(stored_by_word(rectified[0][:, s, :]), sums_by_word(sums[0, W1, s][:]), RELU)
+
+        def rectify_last(s):
+            rectified[1, s] = staging([P, H], F32, "rectified")
+            nc.scalar.activation(stored_by_pair(rectified[1, s][:]), sums_by_pair(sums[1, W1, s][:]), RELU)
 
         def multiply_by_slots():
             hidden["rows"] = small.tile([P, GROUPS, H], BF16, name="hidden_rows", align_bytes=64, bufs=1)
@@ -263,50 +266,47 @@ def tile_routed_moe_kernel(tc, xT, w1, w3, w2, gate, offs, out):
                 pairs = hidden["rows"][:, s, :].bitcast(F32)
                 for u in range(2):
                     nc.tensor.transpose(turned[:, s, u, :], pairs[:, u * P : (u + 1) * P], identity[:])
-            hidden[0] = small.tile([P, GROUPS * H], BF16, name="hidden", align_bytes=64)
+            hidden[0] = small.tile([P, GROUPS * H], BF16, name="hidden", align_bytes=64, bufs=1)
             nc.scalar.copy(
                 hidden[0][:].bitcast(F32).rearrange("p (a n u) -> p a n u", a=GROUPS, u=2),
                 turned[:].rearrange("p a u n -> p a n u"),
             )
 
-        def multiply(e):
-            hidden[e] = small.tile([P, GROUPS * H], BF16, name="hidden", align_bytes=64)
-            for s in range(GROUPS):
-                nc.vector.tensor_tensor(
-                    interleaved_by_pair(hidden[e][:, s * H : (s + 1) * H]),
-                    sums_by_pair(sums[e, W3, s][:]),
-                    stored_by_pair(rectified[e][:, s, :]),
-                    MULT,
-                )
+        def last_ring(shape, dtype, name):
+            return small.tile(shape, dtype, name=name, tag="last", align_bytes=64, bufs=LAST_BUFS)
 
-        def quantise_hidden(e, first, last):
-            if first == 0:
-                words = small.tile([P, C], U32, name="h_words", align_bytes=64)
-                scales = small.tile([P, C], U8, name="h_bytes", align_bytes=64)
-                h_codes[e] = (words, scales)
-            words, scales = h_codes[e]
-            nc.vector.quantize_mx(
-                out=words[:, first:last].bitcast(FP8X4),
-                scales=scales[:, first:last],
-                in_=hidden[e][:, first * J : last * J],
+        def multiply(s):
+            hidden[1, s] = last_ring([P, H], BF16, "hidden_last")
+            nc.vector.tensor_tensor(
+                interleaved_by_pair(hidden[1, s][:]),
+                sums_by_pair(sums[1, W3, s][:]),
+                stored_by_pair(rectified[1, s][:]),
+                MULT,
             )
 
-        def quantise_w2(e):
-            interleaved = small.tile([P, N * J], BF16, name="w2_interleaved", align_bytes=64)
-            words = small.tile([P, N], U32, name="w2_words", align_bytes=64)
+        def quantise_hidden(key, words):
+            scales = small.tile(list(words.shape), U8, name="h_bytes", align_bytes=64, bufs=1 + GROUPS)
+            nc.vector.quantize_mx(out=words[:].bitcast(FP8X4), scales=scales[:], in_=hidden[key][:])
+            h_codes[key] = (words, scales)
+
+        def round_w2(e):
+            w2_interleaved[e] = staging([P, N * J], BF16, "w2_interleaved")
+            nc.scalar.copy(interleaved_order(w2_interleaved[e][:]), loaded_order(w2_raw[e][:]))
+
+        def quantise_w2(e, words):
             scales = small.tile([P, N], U8, name="w2_bytes", align_bytes=64)
-            nc.scalar.copy(interleaved_order(interleaved[:]), loaded_order(w2_raw[e][:]))
-            nc.vector.quantize_mx(out=words[:].bitcast(FP8X4), scales=scales[:], in_=interleaved[:])
+            nc.vector.quantize_mx(out=words[:].bitcast(FP8X4), scales=scales[:], in_=w2_interleaved[e][:])
             w2_codes[e] = (words, scales)
 
-        def second_layer(e, first, last):
-            bank = psum.tile([P, last - first], F32, name="y_bank", bufs=Y_BANKS)
+        def second_layer(e, key):
+            words, scales = h_codes[key]
+            bank = psum.tile(list(words.shape), F32, name="y_bank", bufs=Y_BANKS)
             nc.tensor.matmul_mx(
                 out=bank[:],
                 lhsT=w2_codes[e][0][:].bitcast(FP8X4),
                 lhsT_scale=w2_codes[e][1][:],
-                rhs=h_codes[e][0][:, first:last].bitcast(FP8X4),
-                rhs_scale=h_codes[e][1][:, first:last],
+                rhs=words[:].bitcast(FP8X4),
+                rhs_scale=scales[:],
                 start=True,
                 stop=True,
             )
@@ -323,16 +323,17 @@ def tile_routed_moe_kernel(tc, xT, w1, w3, w2, gate, offs, out):
             interleave_first(W3, g, SHARE_BESIDE_RELU if g == 1 else SHARE_PLAIN)
             chunk(0, W3, g)
             if g == 0:
-                rectify(0)
+                rectify_first()
 
-        interleave_on_scalar(1, W1, 0)
+        interleave(1, W1, 0)
+        round_w2(0)
         multiply_by_slots()
         chunk(1, W1, 0)
-        quantise_w2(0)
         turn_hidden()
         interleave(1, W1, 1)
-        quantise_hidden(0, 0, C)
-        first_bank = second_layer(0, 0, C)
+        quantise_w2(0, keep.tile([P, N], U32, name="w2_words", align_bytes=64))
+        quantise_hidden(0, keep.tile([P, C], U32, name="h_words", align_bytes=64))
+        first_bank = second_layer(0, 0)
         chunk(1, W1, 1)
         y_first = staging([P, C], F32, "y_first")
         nc.scalar.copy(y_first[:], first_bank[:])
@@ -348,15 +349,18 @@ def tile_routed_moe_kernel(tc, xT, w1, w3, w2, gate, offs, out):
         interleave(1, W3, 2, COLUMN_HALVES[1])
         quantise(1, W3, 2, COLUMN_HALVES[1])
         first_layer(1, W3, 2)
-        rectify(1)
+        rectify_last(0)
+        round_w2(1)
+        rectify_last(1)
 
-        multiply(1)
-        quantise_w2(1)
-        y_last = small.tile([P, C], F32, name="y_last")
         for s in range(GROUPS):
-            quantise_hidden(1, s * P, (s + 1) * P)
+            multiply(s)
+            if s == 0:
+                quantise_w2(1, last_ring([P, N], U32, "w2_words_last"))
+            quantise_hidden((1, s), last_ring([P, P], U32, "h_words_last"))
         for s in range(GROUPS):
-            bank = second_layer(1, s * P, (s + 1) * P)
-            nc.scalar.copy(y_last[:, s * P : (s + 1) * P], bank[:])
-        put_back(1, y_last, 0, C)
+            bank = second_layer(1, (1, s))
+            y_last = last_ring([P, P], F32, "y_last")
+            nc.scalar.copy(y_last[:], bank[:])
+            put_back(1, y_last, s * P, (s + 1) * P)
         nc.sync.dma_start(out=out, in_=window[:])

@@ -23,19 +23,21 @@ GROUPS = C // P
 RUN = 4
 LIST_COLUMN = 16
 W1, W3 = 0, 1
+FIRST, LAST = 0, 1
 
 ALL_COLUMNS = (0, H)
 COLUMN_HALVES = ((0, H // 2), (H // 2, H))
+QUARTER_PAIRS = ((0, 2), (2, 4))
 
 SHARE_BESIDE_GATHERS = 48
 SHARE_PLAIN = 36
 SHARE_BESIDE_RELU = 30
 
 STAGING_BUFS = 9
+LAST_BUFS = 7
 CODES_BUFS = 5
 SUM_BANKS = 6
-Y_BANKS = 2
-LAST_BUFS = 7
+SHORT_BANKS = 2
 
 
 def tile_routed_moe_kernel(tc, xT, w1, w3, w2, gate, offs, out):
@@ -43,7 +45,7 @@ def tile_routed_moe_kernel(tc, xT, w1, w3, w2, gate, offs, out):
     xT_view = xT.rearrange("(g p j) n -> g p j n", p=P, j=J)
     w_views = [w.rearrange("e (g p j) n -> e p g j n", p=P, j=J) for w in (w1, w3)]
     w2_view = w2.rearrange("e (p j) n -> e p j n", j=J)
-    w2_by_block = w2.rearrange("e (m t l) n -> e l m t n", t=J, l=RUN)
+    w2_by_quarter = w2.rearrange("e (m t l) n -> e l m t n", t=J, l=RUN)
 
     def loaded_order(ap):
         return ap.rearrange("p j (c r) -> p c j r", r=RUN)
@@ -51,11 +53,11 @@ def tile_routed_moe_kernel(tc, xT, w1, w3, w2, gate, offs, out):
     def interleaved_order(ap):
         return ap.rearrange("p (c r j) -> p c j r", r=RUN, j=J)
 
-    def loaded_by_block(ap):
-        return ap.rearrange("p j (m t l) -> p t m j l", t=J, l=RUN)
+    def loaded_by_quarter(ap):
+        return ap.rearrange("p j (m t l) -> p m t j l", t=J, l=RUN)
 
-    def interleaved_by_block(ap):
-        return ap.rearrange("p (t m l j) -> p t m j l", t=J, l=RUN, j=J)
+    def interleaved_by_quarter(ap):
+        return ap.rearrange("p (t m l j) -> p m t j l", t=J, l=RUN, j=J)
 
     def sums_by_word(ap):
         return ap.rearrange("s (w u b) -> s u w b", u=2, b=2)
@@ -63,23 +65,29 @@ def tile_routed_moe_kernel(tc, xT, w1, w3, w2, gate, offs, out):
     def stored_by_word(ap):
         return ap.rearrange("s (u w b) -> s u w b", u=2, b=2)
 
-    def sums_by_pair(ap):
+    def sums_by_slot_pair(ap):
         return ap.rearrange("p t (c r) -> p c t r", r=2)
 
-    def stored_by_pair(ap):
+    def stored_by_slot_pair(ap):
         return ap.rearrange("p (c t r) -> p c t r", t=J, r=2)
 
-    def interleaved_by_pair(ap):
+    def interleaved_by_slot_pair(ap):
         return ap.rearrange("p (c r t) -> p c t r", t=J, r=2)
 
     with ExitStack() as ctx:
         keep = ctx.enter_context(tc.tile_pool(name="keep", bufs=1))
-        stage = ctx.enter_context(tc.tile_pool(name="stage", bufs=4))
+        stage = ctx.enter_context(tc.tile_pool(name="stage", bufs=CODES_BUFS))
         small = ctx.enter_context(tc.tile_pool(name="small", bufs=E))
-        psum = ctx.enter_context(tc.psum_pool(name="psum", bufs=SUM_BANKS + Y_BANKS))
+        psum = ctx.enter_context(tc.psum_pool(name="psum", bufs=SUM_BANKS + SHORT_BANKS))
 
         def staging(shape, dtype, name):
             return stage.tile(shape, dtype, name=name, tag="staging", align_bytes=64, bufs=STAGING_BUFS)
+
+        def last_ring(shape, dtype, name):
+            return small.tile(shape, dtype, name=name, tag="last", align_bytes=64, bufs=LAST_BUFS)
+
+        def short_bank(shape):
+            return psum.tile(shape, F32, name="short", bufs=SHORT_BANKS)
 
         offsets = keep.tile([P, SLOTS // LIST_COLUMN], U16, name="offsets")
         window = keep.tile([P, T], F32, name="window")
@@ -98,14 +106,6 @@ def tile_routed_moe_kernel(tc, xT, w1, w3, w2, gate, offs, out):
             for g in range(first, last):
                 w_raw[e, m, g, ALL_COLUMNS] = tile[:, g - first]
 
-        def load_w2(e):
-            w2_raw[e] = keep.tile([P, J, N], F32, name=f"w2_raw{e}")
-            if e == 0:
-                nc.sync.dma_start(out=w2_raw[e][:], in_=w2_view[e])
-            else:
-                for l in range(RUN):
-                    nc.sync.dma_start(out=w2_raw[e][l::RUN], in_=w2_by_block[e, l])
-
         def load_gate(e):
             gates[e] = keep.tile([P, C], F32, name=f"gates{e}")
             nc.sync.dma_start(out=gates[e][:], in_=gate[:, e * C : (e + 1) * C])
@@ -115,23 +115,26 @@ def tile_routed_moe_kernel(tc, xT, w1, w3, w2, gate, offs, out):
             nc.sync.dma_start(out=x_raw[g][:], in_=xT_view[g])
             if g == 0:
                 nc.sync.dma_start(offsets[:], offs)
-        load_passes(0, W1, 0, PASSES - 1)
-        load_passes(0, W1, PASSES - 1, PASSES)
+        load_passes(FIRST, W1, 0, PASSES - 1)
+        load_passes(FIRST, W1, PASSES - 1, PASSES)
         for g in range(PASSES):
-            load_passes(0, W3, g, g + 1)
-        load_passes(1, W1, 0, 1)
-        load_w2(0)
-        load_passes(1, W1, 1, 2)
-        load_gate(0)
-        load_passes(1, W1, 2, 3)
+            load_passes(FIRST, W3, g, g + 1)
+        load_passes(LAST, W1, 0, 1)
+        w2_raw[FIRST] = keep.tile([P, J, N], F32, name="w2_raw_first")
+        nc.sync.dma_start(out=w2_raw[FIRST][:], in_=w2_view[FIRST])
+        load_passes(LAST, W1, 1, 2)
+        load_gate(FIRST)
+        load_passes(LAST, W1, 2, 3)
         for g in range(PASSES - 1):
-            load_passes(1, W3, g, g + 1)
+            load_passes(LAST, W3, g, g + 1)
         for first, last in COLUMN_HALVES:
             tile = keep.tile([P, J, last - first], F32, name=f"w_half{first}")
-            nc.sync.dma_start(out=tile[:], in_=w_views[W3][1, :, PASSES - 1, :, first:last])
-            w_raw[1, W3, PASSES - 1, (first, last)] = tile[:]
-        load_w2(1)
-        load_gate(1)
+            nc.sync.dma_start(out=tile[:], in_=w_views[W3][LAST, :, PASSES - 1, :, first:last])
+            w_raw[LAST, W3, PASSES - 1, (first, last)] = tile[:]
+        w2_raw[LAST] = keep.tile([P, J, N], F32, name="w2_raw_last")
+        for l in range(RUN):
+            nc.sync.dma_start(out=w2_raw[LAST][l::RUN], in_=w2_by_quarter[LAST, l])
+        load_gate(LAST)
 
         slot_words = {}
         token_bytes = keep.tile([P, T], U8, name="token_bytes", align_bytes=64)
@@ -153,141 +156,21 @@ def tile_routed_moe_kernel(tc, xT, w1, w3, w2, gate, offs, out):
             nc.vector.tensor_copy(slot_words[g][:], token_words[:].indirect(offsets[:]))
 
         w_interleaved = {}
-        w_codes = {}
         sums = {}
-        rectified = {}
-        hidden = {}
-        h_codes = {}
-        w2_codes = {}
         w2_interleaved = {}
+        w2_codes = {}
 
-        def interleave_first(m, g, share):
-            tile = staging([P, H * J], BF16, "w_interleaved")
-            target = interleaved_order(tile[:])
-            source = loaded_order(w_raw[0, m, g, ALL_COLUMNS])
-            cut = H * share // 64 // RUN
-            nc.scalar.copy(target[:, :cut], source[:, :cut])
-            nc.vector.tensor_copy(target[:, cut:], source[:, cut:])
-            w_interleaved[0, m, g, ALL_COLUMNS] = tile
+        def quantise(words, scales, interleaved):
+            nc.vector.quantize_mx(out=words.bitcast(FP8X4), scales=scales, in_=interleaved)
 
-        def interleave(e, m, g, columns=ALL_COLUMNS, copies=(nc.vector.tensor_copy, nc.scalar.copy)):
-            tile = staging([P, (columns[1] - columns[0]) * J], BF16, "w_interleaved")
-            w_interleaved[e, m, g, columns] = tile
-            target = interleaved_by_block(tile[:])
-            source = loaded_by_block(w_raw[e, m, g, columns])
-            for pair, copy in enumerate(copies):
-                copy(target[:, 2 * pair : 2 * pair + 2], source[:, 2 * pair : 2 * pair + 2])
+        def weight_bytes():
+            return stage.tile([P, H], U8, name="w_bytes", align_bytes=64)
 
-        def interleave_on_scalar(e, m, g):
-            interleave(e, m, g, ALL_COLUMNS, (nc.scalar.copy, nc.scalar.copy))
-
-        def quantise(e, m, g, columns=ALL_COLUMNS):
-            if columns[0] == 0:
-                words = stage.tile([P, H], U32, name="w_words", align_bytes=64, bufs=CODES_BUFS)
-                scales = stage.tile([P, H], U8, name="w_bytes", align_bytes=64, bufs=CODES_BUFS)
-                w_codes[e, m, g] = (words, scales)
-            words, scales = w_codes[e, m, g]
-            source = w_interleaved[e, m, g, columns]
-            if columns == ALL_COLUMNS:
-                nc.vector.quantize_mx(out=words[:].bitcast(FP8X4), scales=scales[:], in_=source[:])
-            else:
-                width = columns[1] - columns[0]
-                for t in range(J):
-                    place = slice(t * P + columns[0] // J, t * P + columns[1] // J)
-                    nc.vector.quantize_mx(
-                        out=words[:, place].bitcast(FP8X4),
-                        scales=scales[:, place],
-                        in_=source[:, t * width : (t + 1) * width],
-                    )
-
-        def first_layer(e, m, g):
-            words, scales = w_codes[e, m, g]
-            for s in range(GROUPS):
-                slots = slice(e * C + s * P, e * C + (s + 1) * P)
-                if g == 0:
-                    sums[e, m, s] = psum.tile([P, J, P], F32, name="sums", bufs=SUM_BANKS)
-                for t in range(J):
-                    block = slice(t * P, (t + 1) * P)
-                    nc.tensor.matmul_mx(
-                        out=sums[e, m, s][:, t, :],
-                        lhsT=words[:, block].bitcast(FP8X4),
-                        lhsT_scale=scales[:, block],
-                        rhs=slot_words[g][:, slots].bitcast(FP8X4),
-                        rhs_scale=slot_bytes[4 * g :, slots],
-                        start=(g == 0 and t == 0),
-                        stop=(g == PASSES - 1 and t == J - 1),
-                    )
-
-        def first_layer_by_slots(m, g):
-            words, scales = w_codes[0, m, g]
-            for s in range(GROUPS):
-                slots = slice(s * P, (s + 1) * P)
-                if g == 0:
-                    sums[0, m, s] = psum.tile([P, H], F32, name="sums", bufs=SUM_BANKS)
-                nc.tensor.matmul_mx(
-                    out=sums[0, m, s][:],
-                    lhsT=slot_words[g][:, slots].bitcast(FP8X4),
-                    lhsT_scale=slot_bytes[4 * g :, slots],
-                    rhs=words[:].bitcast(FP8X4),
-                    rhs_scale=scales[:],
-                    start=(g == 0),
-                    stop=(g == PASSES - 1),
-                )
-
-        def chunk(e, m, g):
-            quantise(e, m, g)
-            if e == 0:
-                first_layer_by_slots(m, g)
-            else:
-                first_layer(e, m, g)
-
-        def rectify_first():
-            rectified[0] = staging([P, GROUPS, H], F32, "rectified")
-            for s in range(GROUPS):
-                nc.scalar.activation(stored_by_word(rectified[0][:, s, :]), sums_by_word(sums[0, W1, s][:]), RELU)
-
-        def rectify_last(s):
-            rectified[1, s] = staging([P, H], F32, "rectified")
-            nc.scalar.activation(stored_by_pair(rectified[1, s][:]), sums_by_pair(sums[1, W1, s][:]), RELU)
-
-        def multiply_by_slots():
-            hidden["rows"] = small.tile([P, GROUPS, H], BF16, name="hidden_rows", align_bytes=64, bufs=1)
-            for s in range(GROUPS):
-                nc.vector.tensor_tensor(
-                    stored_by_word(hidden["rows"][:, s, :]),
-                    sums_by_word(sums[0, W3, s][:]),
-                    stored_by_word(rectified[0][:, s, :]),
-                    MULT,
-                )
-
-        def turn_hidden():
-            turned = psum.tile([P, GROUPS, 2, P], F32, name="y_bank", bufs=Y_BANKS)
-            for s in range(GROUPS):
-                pairs = hidden["rows"][:, s, :].bitcast(F32)
-                for u in range(2):
-                    nc.tensor.transpose(turned[:, s, u, :], pairs[:, u * P : (u + 1) * P], identity[:])
-            hidden[0] = small.tile([P, GROUPS * H], BF16, name="hidden", align_bytes=64, bufs=1)
-            nc.scalar.copy(
-                hidden[0][:].bitcast(F32).rearrange("p (a n u) -> p a n u", a=GROUPS, u=2),
-                turned[:].rearrange("p a u n -> p a n u"),
-            )
-
-        def last_ring(shape, dtype, name):
-            return small.tile(shape, dtype, name=name, tag="last", align_bytes=64, bufs=LAST_BUFS)
-
-        def multiply(s):
-            hidden[1, s] = last_ring([P, H], BF16, "hidden_last")
-            nc.vector.tensor_tensor(
-                interleaved_by_pair(hidden[1, s][:]),
-                sums_by_pair(sums[1, W3, s][:]),
-                stored_by_pair(rectified[1, s][:]),
-                MULT,
-            )
-
-        def quantise_hidden(key, words):
-            scales = small.tile(list(words.shape), U8, name="h_bytes", align_bytes=64, bufs=1 + GROUPS)
-            nc.vector.quantize_mx(out=words[:].bitcast(FP8X4), scales=scales[:], in_=hidden[key][:])
-            h_codes[key] = (words, scales)
+        def quantise_chunk(e, m, g):
+            words = stage.tile([P, H], U32, name="w_words", align_bytes=64)
+            scales = weight_bytes()
+            quantise(words[:], scales[:], w_interleaved[e, m, g, ALL_COLUMNS][:])
+            return words, scales
 
         def round_w2(e):
             w2_interleaved[e] = staging([P, N * J], BF16, "w2_interleaved")
@@ -295,12 +178,16 @@ def tile_routed_moe_kernel(tc, xT, w1, w3, w2, gate, offs, out):
 
         def quantise_w2(e, words):
             scales = small.tile([P, N], U8, name="w2_bytes", align_bytes=64)
-            nc.vector.quantize_mx(out=words[:].bitcast(FP8X4), scales=scales[:], in_=w2_interleaved[e][:])
+            quantise(words[:], scales[:], w2_interleaved[e][:])
             w2_codes[e] = (words, scales)
 
-        def second_layer(e, key):
-            words, scales = h_codes[key]
-            bank = psum.tile(list(words.shape), F32, name="y_bank", bufs=Y_BANKS)
+        def quantise_hidden(words, interleaved):
+            scales = small.tile(list(words.shape), U8, name="h_bytes", align_bytes=64, bufs=1 + GROUPS)
+            quantise(words[:], scales[:], interleaved[:])
+            return words, scales
+
+        def second_layer(e, words, scales):
+            bank = short_bank(list(words.shape))
             nc.tensor.matmul_mx(
                 out=bank[:],
                 lhsT=w2_codes[e][0][:].bitcast(FP8X4),
@@ -316,51 +203,160 @@ def tile_routed_moe_kernel(tc, xT, w1, w3, w2, gate, offs, out):
             entries = offsets[:, (e * C + first) // LIST_COLUMN : (e * C + last) // LIST_COLUMN]
             nc.vector.tensor_tensor(window[:].indirect(entries), y[:], gates[e][:, first:last], MULT)
 
-        for g in range(PASSES):
-            interleave_first(W1, g, SHARE_BESIDE_GATHERS if g < PASSES - 1 else SHARE_PLAIN)
-            chunk(0, W1, g)
-        for g in range(PASSES):
-            interleave_first(W3, g, SHARE_BESIDE_RELU if g == 1 else SHARE_PLAIN)
-            chunk(0, W3, g)
-            if g == 0:
-                rectify_first()
+        def chunk_of_first(m, g, share):
+            tile = staging([P, H * J], BF16, "w_interleaved")
+            target = interleaved_order(tile[:])
+            source = loaded_order(w_raw[FIRST, m, g, ALL_COLUMNS])
+            cut = H * share // 64 // RUN
+            nc.scalar.copy(target[:, :cut], source[:, :cut])
+            nc.vector.tensor_copy(target[:, cut:], source[:, cut:])
+            w_interleaved[FIRST, m, g, ALL_COLUMNS] = tile
+            words, scales = quantise_chunk(FIRST, m, g)
+            for s in range(GROUPS):
+                slots = slice(s * P, (s + 1) * P)
+                if g == 0:
+                    sums[FIRST, m, s] = psum.tile([P, H], F32, name="sums", bufs=SUM_BANKS)
+                nc.tensor.matmul_mx(
+                    out=sums[FIRST, m, s][:],
+                    lhsT=slot_words[g][:, slots].bitcast(FP8X4),
+                    lhsT_scale=slot_bytes[4 * g :, slots],
+                    rhs=words[:].bitcast(FP8X4),
+                    rhs_scale=scales[:],
+                    start=(g == 0),
+                    stop=(g == PASSES - 1),
+                )
 
-        interleave(1, W1, 0)
-        round_w2(0)
-        multiply_by_slots()
-        chunk(1, W1, 0)
-        turn_hidden()
-        interleave(1, W1, 1)
-        quantise_w2(0, keep.tile([P, N], U32, name="w2_words", align_bytes=64))
-        quantise_hidden(0, keep.tile([P, C], U32, name="h_words", align_bytes=64))
-        first_bank = second_layer(0, 0)
-        chunk(1, W1, 1)
+        def rectify_first():
+            tile = staging([P, GROUPS, H], F32, "rectified")
+            for s in range(GROUPS):
+                nc.scalar.activation(stored_by_word(tile[:, s, :]), sums_by_word(sums[FIRST, W1, s][:]), RELU)
+            return tile
+
+        def multiply_first(rectified):
+            rows = small.tile([P, GROUPS, H], BF16, name="hidden_rows", align_bytes=64, bufs=1)
+            for s in range(GROUPS):
+                nc.vector.tensor_tensor(
+                    stored_by_word(rows[:, s, :]),
+                    sums_by_word(sums[FIRST, W3, s][:]),
+                    stored_by_word(rectified[:, s, :]),
+                    MULT,
+                )
+            return rows
+
+        def turn_hidden(rows):
+            tile = small.tile([P, GROUPS * H], BF16, name="hidden_first", align_bytes=64, bufs=1)
+            for s in range(GROUPS):
+                turned = short_bank([P, 2, P])
+                pairs = rows[:, s, :].bitcast(F32)
+                for u in range(2):
+                    nc.tensor.transpose(turned[:, u, :], pairs[:, u * P : (u + 1) * P], identity[:])
+                nc.scalar.copy(
+                    tile[:, s * H : (s + 1) * H].bitcast(F32).rearrange("p (n u) -> p n u", u=2),
+                    turned[:].rearrange("p u n -> p n u"),
+                )
+            return tile
+
+        def round_last(m, g, columns=ALL_COLUMNS, shared=True):
+            tile = staging([P, (columns[1] - columns[0]) * J], BF16, "w_interleaved")
+            w_interleaved[LAST, m, g, columns] = tile
+            target = interleaved_by_quarter(tile[:])
+            source = loaded_by_quarter(w_raw[LAST, m, g, columns])
+            if shared:
+                for (first, last), copy in zip(QUARTER_PAIRS, (nc.vector.tensor_copy, nc.scalar.copy)):
+                    copy(target[:, :, first:last], source[:, :, first:last])
+            else:
+                nc.scalar.copy(target, source)
+
+        def quantise_halves():
+            words = staging([P, H], U32, "w_words_last")
+            scales = weight_bytes()
+            for quarters in QUARTER_PAIRS:
+                for first, last in COLUMN_HALVES:
+                    source = w_interleaved[LAST, W3, PASSES - 1, (first, last)]
+                    width = last - first
+                    for t in range(*quarters):
+                        places = slice(t * P + first // J, t * P + last // J)
+                        quantise(words[:, places], scales[:, places], source[:, t * width : (t + 1) * width])
+            return words, scales
+
+        def first_layer_of_last(m, g, words, scales):
+            for s in range(GROUPS):
+                slots = slice(C + s * P, C + (s + 1) * P)
+                if g == 0:
+                    sums[LAST, m, s] = psum.tile([P, J, P], F32, name="sums", bufs=SUM_BANKS)
+                for t in range(J):
+                    quarter = slice(t * P, (t + 1) * P)
+                    nc.tensor.matmul_mx(
+                        out=sums[LAST, m, s][:, t, :],
+                        lhsT=words[:, quarter].bitcast(FP8X4),
+                        lhsT_scale=scales[:, quarter],
+                        rhs=slot_words[g][:, slots].bitcast(FP8X4),
+                        rhs_scale=slot_bytes[4 * g :, slots],
+                        start=(g == 0 and t == 0),
+                        stop=(g == PASSES - 1 and t == J - 1),
+                    )
+
+        def multiply_out_last(m, g):
+            first_layer_of_last(m, g, *quantise_chunk(LAST, m, g))
+
+        def rectify_last(s):
+            tile = staging([P, H], F32, "rectified")
+            nc.scalar.activation(stored_by_slot_pair(tile[:]), sums_by_slot_pair(sums[LAST, W1, s][:]), RELU)
+            return tile
+
+        def multiply_last(s, rectified):
+            tile = last_ring([P, H], BF16, "hidden_last")
+            nc.vector.tensor_tensor(
+                interleaved_by_slot_pair(tile[:]),
+                sums_by_slot_pair(sums[LAST, W3, s][:]),
+                stored_by_slot_pair(rectified[:]),
+                MULT,
+            )
+            return tile
+
+        for g in range(PASSES):
+            chunk_of_first(W1, g, SHARE_BESIDE_GATHERS if g < PASSES - 1 else SHARE_PLAIN)
+        chunk_of_first(W3, 0, SHARE_PLAIN)
+        rectified_first = rectify_first()
+        chunk_of_first(W3, 1, SHARE_BESIDE_RELU)
+        chunk_of_first(W3, 2, SHARE_PLAIN)
+
+        round_last(W1, 0)
+        round_w2(FIRST)
+        hidden_rows = multiply_first(rectified_first)
+        multiply_out_last(W1, 0)
+        hidden_first = turn_hidden(hidden_rows)
+        round_last(W1, 1)
+        quantise_w2(FIRST, keep.tile([P, N], U32, name="w2_words", align_bytes=64))
+        codes_first = quantise_hidden(keep.tile([P, C], U32, name="h_words", align_bytes=64), hidden_first)
+        bank_first = second_layer(FIRST, *codes_first)
+        multiply_out_last(W1, 1)
         y_first = staging([P, C], F32, "y_first")
-        nc.scalar.copy(y_first[:], first_bank[:])
-        interleave_on_scalar(1, W1, 2)
-        put_back(0, y_first, 0, C)
-        chunk(1, W1, 2)
-        interleave(1, W3, 0)
-        chunk(1, W3, 0)
-        interleave(1, W3, 1)
-        interleave(1, W3, 2, COLUMN_HALVES[0])
-        chunk(1, W3, 1)
-        quantise(1, W3, 2, COLUMN_HALVES[0])
-        interleave(1, W3, 2, COLUMN_HALVES[1])
-        quantise(1, W3, 2, COLUMN_HALVES[1])
-        first_layer(1, W3, 2)
-        rectify_last(0)
-        round_w2(1)
-        rectify_last(1)
+        nc.scalar.copy(y_first[:], bank_first[:])
+        round_last(W1, 2, shared=False)
+        put_back(FIRST, y_first, 0, C)
+        multiply_out_last(W1, 2)
 
+        round_last(W3, 0)
+        multiply_out_last(W3, 0)
+        round_last(W3, 1)
+        round_last(W3, 2, COLUMN_HALVES[0])
+        rectified_last = [rectify_last(0)]
+        multiply_out_last(W3, 1)
+        round_last(W3, 2, COLUMN_HALVES[1])
+        first_layer_of_last(W3, 2, *quantise_halves())
+        rectified_last.append(rectify_last(1))
+        round_w2(LAST)
+
+        codes_last = []
         for s in range(GROUPS):
-            multiply(s)
+            hidden_last = multiply_last(s, rectified_last[s])
             if s == 0:
-                quantise_w2(1, last_ring([P, N], U32, "w2_words_last"))
-            quantise_hidden((1, s), last_ring([P, P], U32, "h_words_last"))
+                quantise_w2(LAST, last_ring([P, N], U32, "w2_words_last"))
+            codes_last.append(quantise_hidden(last_ring([P, P], U32, "h_words_last"), hidden_last))
         for s in range(GROUPS):
-            bank = second_layer(1, (1, s))
+            bank_last = second_layer(LAST, *codes_last[s])
             y_last = last_ring([P, P], F32, "y_last")
-            nc.scalar.copy(y_last[:], bank[:])
-            put_back(1, y_last, s * P, (s + 1) * P)
+            nc.scalar.copy(y_last[:], bank_last[:])
+            put_back(LAST, y_last, s * P, (s + 1) * P)
         nc.sync.dma_start(out=out, in_=window[:])

@@ -14,6 +14,7 @@ U8 = mybir.dt.uint8
 FP8X4 = mybir.dt.float8_e4m3fn_x4
 MULT = mybir.AluOpType.mult
 RELU = mybir.ActivationFunctionType.Relu
+COPY = mybir.ActivationFunctionType.Copy
 
 P = 128
 J = 4
@@ -24,17 +25,15 @@ RUN = 4
 LIST_COLUMN = 16
 W1, W3 = 0, 1
 FIRST, LAST = 0, 1
-
 ALL_COLUMNS = (0, H)
 COLUMN_HALVES = ((0, H // 2), (H // 2, H))
 QUARTER_PAIRS = ((0, 2), (2, 4))
 
 SHARE_BESIDE_GATHERS = 48
-SHARE_PLAIN = 36
-SHARE_BESIDE_RELU = 30
+SHARE_PLAIN = 34
 
 STAGING_BUFS = 9
-LAST_BUFS = 7
+LAST_BUFS = 9
 CODES_BUFS = 5
 SUM_BANKS = 6
 SHORT_BANKS = 2
@@ -45,7 +44,7 @@ def tile_routed_moe_kernel(tc, xT, w1, w3, w2, gate, offs, out):
     xT_view = xT.rearrange("(g p j) n -> g p j n", p=P, j=J)
     w_views = [w.rearrange("e (g p j) n -> e p g j n", p=P, j=J) for w in (w1, w3)]
     w2_view = w2.rearrange("e (p j) n -> e p j n", j=J)
-    w2_by_quarter = w2.rearrange("e (m t l) n -> e l m t n", t=J, l=RUN)
+    w2_by_quarter = w2.rearrange("e (m u l v) n -> e l m u (v n)", u=2, l=2, v=2)
 
     def loaded_order(ap):
         return ap.rearrange("p j (c r) -> p c j r", r=RUN)
@@ -54,10 +53,10 @@ def tile_routed_moe_kernel(tc, xT, w1, w3, w2, gate, offs, out):
         return ap.rearrange("p (c r j) -> p c j r", r=RUN, j=J)
 
     def loaded_by_quarter(ap):
-        return ap.rearrange("p j (m t l) -> p m t j l", t=J, l=RUN)
+        return ap.rearrange("p j (m u l v) -> p u m j l v", u=2, l=2, v=2)
 
     def interleaved_by_quarter(ap):
-        return ap.rearrange("p (t m l j) -> p m t j l", t=J, l=RUN, j=J)
+        return ap.rearrange("p (u v m l j) -> p u m j l v", u=2, v=2, l=2, j=J)
 
     def sums_by_word(ap):
         return ap.rearrange("s (w u b) -> s u w b", u=2, b=2)
@@ -101,7 +100,10 @@ def tile_routed_moe_kernel(tc, xT, w1, w3, w2, gate, offs, out):
         gates = {}
 
         def load_passes(e, m, first, last):
-            tile = keep.tile([P, last - first, J, H], F32, name=f"w_raw{e}{m}{first}")
+            if (e, m) == (LAST, W3):
+                tile = stage.tile([P, last - first, J, H], F32, name="w_raw", tag="raw", bufs=PASSES)
+            else:
+                tile = keep.tile([P, last - first, J, H], F32, name=f"w_raw{e}{m}{first}")
             nc.sync.dma_start(out=tile[:], in_=w_views[m][e, :, first:last])
             for g in range(first, last):
                 w_raw[e, m, g, ALL_COLUMNS] = tile[:, g - first]
@@ -111,7 +113,7 @@ def tile_routed_moe_kernel(tc, xT, w1, w3, w2, gate, offs, out):
             nc.sync.dma_start(out=gates[e][:], in_=gate[:, e * C : (e + 1) * C])
 
         for g in range(PASSES):
-            x_raw[g] = keep.tile([P, J, T], F32, name=f"x_raw{g}")
+            x_raw[g] = stage.tile([P, J, T], F32, name="x_raw", tag="raw", bufs=PASSES)
             nc.sync.dma_start(out=x_raw[g][:], in_=xT_view[g])
             if g == 0:
                 nc.sync.dma_start(offsets[:], offs)
@@ -122,9 +124,8 @@ def tile_routed_moe_kernel(tc, xT, w1, w3, w2, gate, offs, out):
         load_passes(LAST, W1, 0, 1)
         w2_raw[FIRST] = keep.tile([P, J, N], F32, name="w2_raw_first")
         nc.sync.dma_start(out=w2_raw[FIRST][:], in_=w2_view[FIRST])
-        load_passes(LAST, W1, 1, 2)
-        load_gate(FIRST)
-        load_passes(LAST, W1, 2, 3)
+        for g in range(1, PASSES):
+            load_passes(LAST, W1, g, g + 1)
         for g in range(PASSES - 1):
             load_passes(LAST, W3, g, g + 1)
         for first, last in COLUMN_HALVES:
@@ -132,8 +133,10 @@ def tile_routed_moe_kernel(tc, xT, w1, w3, w2, gate, offs, out):
             nc.sync.dma_start(out=tile[:], in_=w_views[W3][LAST, :, PASSES - 1, :, first:last])
             w_raw[LAST, W3, PASSES - 1, (first, last)] = tile[:]
         w2_raw[LAST] = keep.tile([P, J, N], F32, name="w2_raw_last")
-        for l in range(RUN):
-            nc.sync.dma_start(out=w2_raw[LAST][l::RUN], in_=w2_by_quarter[LAST, l])
+        for l in range(2):
+            rows = w2_raw[LAST][l::2].rearrange("p (u v) n -> p u (v n)", v=2)
+            nc.sync.dma_start(out=rows, in_=w2_by_quarter[LAST, l])
+        load_gate(FIRST)
         load_gate(LAST)
 
         slot_words = {}
@@ -155,30 +158,25 @@ def tile_routed_moe_kernel(tc, xT, w1, w3, w2, gate, offs, out):
                 nc.vector.tensor_copy(slot_bytes[:], token_bytes[:].indirect(offsets[:]))
             nc.vector.tensor_copy(slot_words[g][:], token_words[:].indirect(offsets[:]))
 
-        w_interleaved = {}
         sums = {}
-        w2_interleaved = {}
         w2_codes = {}
 
         def quantise(words, scales, interleaved):
             nc.vector.quantize_mx(out=words.bitcast(FP8X4), scales=scales, in_=interleaved)
 
-        def weight_bytes():
-            return stage.tile([P, H], U8, name="w_bytes", align_bytes=64)
-
-        def quantise_chunk(e, m, g):
+        def chunk_codes():
             words = stage.tile([P, H], U32, name="w_words", align_bytes=64)
-            scales = weight_bytes()
-            quantise(words[:], scales[:], w_interleaved[e, m, g, ALL_COLUMNS][:])
+            scales = stage.tile([P, H], U8, name="w_bytes", align_bytes=64)
             return words, scales
 
-        def round_w2(e):
-            w2_interleaved[e] = staging([P, N * J], BF16, "w2_interleaved")
-            nc.scalar.copy(interleaved_order(w2_interleaved[e][:]), loaded_order(w2_raw[e][:]))
+        def round_w2(e, ring):
+            tile = ring([P, N * J], BF16, "w2_interleaved")
+            nc.scalar.copy(interleaved_order(tile[:]), loaded_order(w2_raw[e][:]))
+            return tile
 
-        def quantise_w2(e, words):
+        def quantise_w2(e, words, interleaved):
             scales = small.tile([P, N], U8, name="w2_bytes", align_bytes=64)
-            quantise(words[:], scales[:], w2_interleaved[e][:])
+            quantise(words[:], scales[:], interleaved[:])
             w2_codes[e] = (words, scales)
 
         def quantise_hidden(words, interleaved):
@@ -199,9 +197,11 @@ def tile_routed_moe_kernel(tc, xT, w1, w3, w2, gate, offs, out):
             )
             return bank
 
-        def put_back(e, y, first, last):
+        def put_back(e, bank, first, last):
+            weighed = last_ring([P, last - first], F32, "weighed")
+            nc.vector.tensor_tensor(weighed[:], bank[:], gates[e][:, first:last], MULT)
             entries = offsets[:, (e * C + first) // LIST_COLUMN : (e * C + last) // LIST_COLUMN]
-            nc.vector.tensor_tensor(window[:].indirect(entries), y[:], gates[e][:, first:last], MULT)
+            nc.scalar.activation(window[:].indirect(entries), weighed[:], COPY)
 
         def chunk_of_first(m, g, share):
             tile = staging([P, H * J], BF16, "w_interleaved")
@@ -210,8 +210,8 @@ def tile_routed_moe_kernel(tc, xT, w1, w3, w2, gate, offs, out):
             cut = H * share // 64 // RUN
             nc.scalar.copy(target[:, :cut], source[:, :cut])
             nc.vector.tensor_copy(target[:, cut:], source[:, cut:])
-            w_interleaved[FIRST, m, g, ALL_COLUMNS] = tile
-            words, scales = quantise_chunk(FIRST, m, g)
+            words, scales = chunk_codes()
+            quantise(words[:], scales[:], tile[:])
             for s in range(GROUPS):
                 slots = slice(s * P, (s + 1) * P)
                 if g == 0:
@@ -256,48 +256,49 @@ def tile_routed_moe_kernel(tc, xT, w1, w3, w2, gate, offs, out):
                 )
             return tile
 
-        def round_last(m, g, columns=ALL_COLUMNS, shared=True):
+        def round_last(m, g, columns):
             tile = staging([P, (columns[1] - columns[0]) * J], BF16, "w_interleaved")
-            w_interleaved[LAST, m, g, columns] = tile
             target = interleaved_by_quarter(tile[:])
             source = loaded_by_quarter(w_raw[LAST, m, g, columns])
-            if shared:
-                for (first, last), copy in zip(QUARTER_PAIRS, (nc.vector.tensor_copy, nc.scalar.copy)):
-                    copy(target[:, :, first:last], source[:, :, first:last])
-            else:
-                nc.scalar.copy(target, source)
+            for u, copy in enumerate((nc.vector.tensor_copy, nc.scalar.copy)):
+                copy(target[:, u], source[:, u])
+            return tile
 
-        def quantise_halves():
-            words = staging([P, H], U32, "w_words_last")
-            scales = weight_bytes()
-            for quarters in QUARTER_PAIRS:
-                for first, last in COLUMN_HALVES:
-                    source = w_interleaved[LAST, W3, PASSES - 1, (first, last)]
-                    width = last - first
-                    for t in range(*quarters):
-                        places = slice(t * P + first // J, t * P + last // J)
-                        quantise(words[:, places], scales[:, places], source[:, t * width : (t + 1) * width])
-            return words, scales
+        def quantise_pair(codes, pair, columns, interleaved):
+            words, scales = codes
+            first, last = columns
+            width = last - first
+            for n, t in enumerate(range(*pair)):
+                places = slice(n * P + first // J, n * P + last // J)
+                quantise(words[:, places], scales[:, places], interleaved[:, t * width : (t + 1) * width])
 
-        def first_layer_of_last(m, g, words, scales):
+        def pair_codes(words):
+            return words, stage.tile([P, 2 * P], U8, name="pair_bytes", align_bytes=64, bufs=2)
+
+        def first_layer_of_last(m, g, quarters):
             for s in range(GROUPS):
                 slots = slice(C + s * P, C + (s + 1) * P)
                 if g == 0:
                     sums[LAST, m, s] = psum.tile([P, J, P], F32, name="sums", bufs=SUM_BANKS)
                 for t in range(J):
-                    quarter = slice(t * P, (t + 1) * P)
                     nc.tensor.matmul_mx(
                         out=sums[LAST, m, s][:, t, :],
-                        lhsT=words[:, quarter].bitcast(FP8X4),
-                        lhsT_scale=scales[:, quarter],
+                        lhsT=quarters[t][0].bitcast(FP8X4),
+                        lhsT_scale=quarters[t][1],
                         rhs=slot_words[g][:, slots].bitcast(FP8X4),
                         rhs_scale=slot_bytes[4 * g :, slots],
                         start=(g == 0 and t == 0),
                         stop=(g == PASSES - 1 and t == J - 1),
                     )
 
-        def multiply_out_last(m, g):
-            first_layer_of_last(m, g, *quantise_chunk(LAST, m, g))
+        def quarters_of(words, scales):
+            return [(words[:, n : n + P], scales[:, n : n + P]) for n in range(0, words.shape[1], P)]
+
+        def chunk_of_last(m, g):
+            tile = round_last(m, g, ALL_COLUMNS)
+            words, scales = chunk_codes()
+            quantise(words[:], scales[:], tile[:])
+            first_layer_of_last(m, g, quarters_of(words, scales))
 
         def rectify_last(s):
             tile = staging([P, H], F32, "rectified")
@@ -318,45 +319,47 @@ def tile_routed_moe_kernel(tc, xT, w1, w3, w2, gate, offs, out):
             chunk_of_first(W1, g, SHARE_BESIDE_GATHERS if g < PASSES - 1 else SHARE_PLAIN)
         chunk_of_first(W3, 0, SHARE_PLAIN)
         rectified_first = rectify_first()
-        chunk_of_first(W3, 1, SHARE_BESIDE_RELU)
+        chunk_of_first(W3, 1, SHARE_PLAIN)
         chunk_of_first(W3, 2, SHARE_PLAIN)
 
-        round_last(W1, 0)
-        round_w2(FIRST)
+        chunk_of_last(W1, 0)
         hidden_rows = multiply_first(rectified_first)
-        multiply_out_last(W1, 0)
         hidden_first = turn_hidden(hidden_rows)
-        round_last(W1, 1)
-        quantise_w2(FIRST, keep.tile([P, N], U32, name="w2_words", align_bytes=64))
+        w2_first = round_w2(FIRST, staging)
+        chunk_of_last(W1, 1)
+        quantise_w2(FIRST, keep.tile([P, N], U32, name="w2_words", align_bytes=64), w2_first)
         codes_first = quantise_hidden(keep.tile([P, C], U32, name="h_words", align_bytes=64), hidden_first)
         bank_first = second_layer(FIRST, *codes_first)
-        multiply_out_last(W1, 1)
-        y_first = staging([P, C], F32, "y_first")
-        nc.scalar.copy(y_first[:], bank_first[:])
-        round_last(W1, 2, shared=False)
-        put_back(FIRST, y_first, 0, C)
-        multiply_out_last(W1, 2)
+        chunk_of_last(W1, 2)
 
-        round_last(W3, 0)
-        multiply_out_last(W3, 0)
-        round_last(W3, 1)
-        round_last(W3, 2, COLUMN_HALVES[0])
+        chunk_of_last(W3, 0)
         rectified_last = [rectify_last(0)]
-        multiply_out_last(W3, 1)
-        round_last(W3, 2, COLUMN_HALVES[1])
-        first_layer_of_last(W3, 2, *quantise_halves())
+        tile = round_last(W3, 1, ALL_COLUMNS)
+        words, scales = chunk_codes()
+        for first, last in QUARTER_PAIRS:
+            places = slice(first * P, last * P)
+            quantise(words[:, places], scales[:, places], tile[:, first * H : last * H])
+        first_layer_of_last(W3, 1, quarters_of(words, scales))
+        first_half = round_last(W3, PASSES - 1, COLUMN_HALVES[0])
+        vector_pair = pair_codes(stage.tile([P, 2 * P], U32, name="pair_words", align_bytes=64, bufs=1))
+        quantise_pair(vector_pair, QUARTER_PAIRS[0], COLUMN_HALVES[0], first_half)
         rectified_last.append(rectify_last(1))
-        round_w2(LAST)
+        last_half = round_last(W3, PASSES - 1, COLUMN_HALVES[1])
+        scalar_pair = pair_codes(staging([P, 2 * P], U32, "pair_words_held"))
+        quantise_pair(scalar_pair, QUARTER_PAIRS[1], COLUMN_HALVES[0], first_half)
+        quantise_pair(vector_pair, QUARTER_PAIRS[0], COLUMN_HALVES[1], last_half)
+        quantise_pair(scalar_pair, QUARTER_PAIRS[1], COLUMN_HALVES[1], last_half)
+        first_layer_of_last(W3, PASSES - 1, quarters_of(*vector_pair) + quarters_of(*scalar_pair))
+        w2_last = round_w2(LAST, last_ring)
+        put_back(FIRST, bank_first, 0, C)
 
-        codes_last = []
-        for s in range(GROUPS):
-            hidden_last = multiply_last(s, rectified_last[s])
-            if s == 0:
-                quantise_w2(LAST, last_ring([P, N], U32, "w2_words_last"))
-            codes_last.append(quantise_hidden(last_ring([P, P], U32, "h_words_last"), hidden_last))
-        for s in range(GROUPS):
-            bank_last = second_layer(LAST, *codes_last[s])
-            y_last = last_ring([P, P], F32, "y_last")
-            nc.scalar.copy(y_last[:], bank_last[:])
-            put_back(LAST, y_last, s * P, (s + 1) * P)
+        hidden = multiply_last(0, rectified_last[0])
+        quantise_w2(LAST, last_ring([P, N], U32, "w2_words_last"), w2_last)
+        codes = quantise_hidden(last_ring([P, P], U32, "h_words_last"), hidden)
+        bank = second_layer(LAST, *codes)
+        hidden = multiply_last(1, rectified_last[1])
+        put_back(LAST, bank, 0, P)
+        codes = quantise_hidden(last_ring([P, P], U32, "h_words_last"), hidden)
+        bank = second_layer(LAST, *codes)
+        put_back(LAST, bank, P, C)
         nc.sync.dma_start(out=out, in_=window[:])

@@ -26,14 +26,13 @@ LIST_COLUMN = 16
 W1, W3 = 0, 1
 FIRST, LAST = 0, 1
 ALL_COLUMNS = (0, H)
-COLUMN_HALVES = ((0, H // 2), (H // 2, H))
-QUARTER_PAIRS = ((0, 2), (2, 4))
+ROW_PAIRS = ((0, 2), (2, 4))
 
 SHARE_BESIDE_GATHERS = 48
 SHARE_PLAIN = 34
 
 STAGING_BUFS = 9
-LAST_BUFS = 9
+LAST_BUFS = 12
 CODES_BUFS = 5
 SUM_BANKS = 6
 SHORT_BANKS = 2
@@ -128,10 +127,11 @@ def tile_routed_moe_kernel(tc, xT, w1, w3, w2, gate, offs, out):
             load_passes(LAST, W1, g, g + 1)
         for g in range(PASSES - 1):
             load_passes(LAST, W3, g, g + 1)
-        for first, last in COLUMN_HALVES:
-            tile = keep.tile([P, J, last - first], F32, name=f"w_half{first}")
-            nc.sync.dma_start(out=tile[:], in_=w_views[W3][LAST, :, PASSES - 1, :, first:last])
-            w_raw[LAST, W3, PASSES - 1, (first, last)] = tile[:]
+        row_pairs = []
+        for first, last in ROW_PAIRS:
+            tile = keep.tile([P, last - first, H], F32, name=f"w_rows{first}")
+            nc.sync.dma_start(out=tile[:], in_=w_views[W3][LAST, :, PASSES - 1, first:last])
+            row_pairs.append(loaded_by_quarter(tile[:]))
         w2_raw[LAST] = keep.tile([P, J, N], F32, name="w2_raw_last")
         for l in range(2):
             rows = w2_raw[LAST][l::2].rearrange("p (u v) n -> p u (v n)", v=2)
@@ -264,32 +264,24 @@ def tile_routed_moe_kernel(tc, xT, w1, w3, w2, gate, offs, out):
                 copy(target[:, u], source[:, u])
             return tile
 
-        def quantise_pair(codes, pair, columns, interleaved):
-            words, scales = codes
-            first, last = columns
-            width = last - first
-            for n, t in enumerate(range(*pair)):
-                places = slice(n * P + first // J, n * P + last // J)
-                quantise(words[:, places], scales[:, places], interleaved[:, t * width : (t + 1) * width])
-
-        def pair_codes(words):
-            return words, stage.tile([P, 2 * P], U8, name="pair_bytes", align_bytes=64, bufs=2)
+        def pass_of_last(m, g, s, t, quarter, stop):
+            slots = slice(C + s * P, C + (s + 1) * P)
+            if g == 0 and t == 0:
+                sums[LAST, m, s] = psum.tile([P, J, P], F32, name="sums", bufs=SUM_BANKS)
+            nc.tensor.matmul_mx(
+                out=sums[LAST, m, s][:, t, :],
+                lhsT=quarter[0].bitcast(FP8X4),
+                lhsT_scale=quarter[1],
+                rhs=slot_words[g][:, slots].bitcast(FP8X4),
+                rhs_scale=slot_bytes[4 * g :, slots],
+                start=(g == 0 and t == 0),
+                stop=stop,
+            )
 
         def first_layer_of_last(m, g, quarters):
             for s in range(GROUPS):
-                slots = slice(C + s * P, C + (s + 1) * P)
-                if g == 0:
-                    sums[LAST, m, s] = psum.tile([P, J, P], F32, name="sums", bufs=SUM_BANKS)
                 for t in range(J):
-                    nc.tensor.matmul_mx(
-                        out=sums[LAST, m, s][:, t, :],
-                        lhsT=quarters[t][0].bitcast(FP8X4),
-                        lhsT_scale=quarters[t][1],
-                        rhs=slot_words[g][:, slots].bitcast(FP8X4),
-                        rhs_scale=slot_bytes[4 * g :, slots],
-                        start=(g == 0 and t == 0),
-                        stop=(g == PASSES - 1 and t == J - 1),
-                    )
+                    pass_of_last(m, g, s, t, quarters[t], g == PASSES - 1 and t == J - 1)
 
         def quarters_of(words, scales):
             return [(words[:, n : n + P], scales[:, n : n + P]) for n in range(0, words.shape[1], P)]
@@ -302,7 +294,12 @@ def tile_routed_moe_kernel(tc, xT, w1, w3, w2, gate, offs, out):
 
         def rectify_last(s):
             tile = staging([P, H], F32, "rectified")
-            nc.scalar.activation(stored_by_slot_pair(tile[:]), sums_by_slot_pair(sums[LAST, W1, s][:]), RELU)
+            target = stored_by_slot_pair(tile[:])
+            source = sums_by_slot_pair(sums[LAST, W1, s][:])
+            if s == 0:
+                nc.vector.tensor_scalar_max(target, source, 0.0)
+            else:
+                nc.scalar.activation(target, source, RELU)
             return tile
 
         def multiply_last(s, rectified):
@@ -332,24 +329,34 @@ def tile_routed_moe_kernel(tc, xT, w1, w3, w2, gate, offs, out):
         bank_first = second_layer(FIRST, *codes_first)
         chunk_of_last(W1, 2)
 
-        chunk_of_last(W3, 0)
-        rectified_last = [rectify_last(0)]
-        tile = round_last(W3, 1, ALL_COLUMNS)
+        tile = round_last(W3, 0, ALL_COLUMNS)
+        rectified_last = [rectify_last(s) for s in range(GROUPS)]
         words, scales = chunk_codes()
-        for first, last in QUARTER_PAIRS:
-            places = slice(first * P, last * P)
-            quantise(words[:, places], scales[:, places], tile[:, first * H : last * H])
+        quantise(words[:], scales[:], tile[:])
+        first_layer_of_last(W3, 0, quarters_of(words, scales))
+        before = round_last(W3, 1, ALL_COLUMNS)
+
+        tile = staging([P, H * J], BF16, "w_interleaved")
+        target = interleaved_by_quarter(tile[:])
+        early, late = (slice(*pair) for pair in ROW_PAIRS)
+        nc.vector.tensor_copy(target[:, 0, :, early], row_pairs[0][:, 0])
+        nc.scalar.copy(target[:, 1, :, early], row_pairs[0][:, 1])
+        words, scales = chunk_codes()
+        quantise(words[:], scales[:], before[:])
         first_layer_of_last(W3, 1, quarters_of(words, scales))
-        first_half = round_last(W3, PASSES - 1, COLUMN_HALVES[0])
-        vector_pair = pair_codes(stage.tile([P, 2 * P], U32, name="pair_words", align_bytes=64, bufs=1))
-        quantise_pair(vector_pair, QUARTER_PAIRS[0], COLUMN_HALVES[0], first_half)
-        rectified_last.append(rectify_last(1))
-        last_half = round_last(W3, PASSES - 1, COLUMN_HALVES[1])
-        scalar_pair = pair_codes(staging([P, 2 * P], U32, "pair_words_held"))
-        quantise_pair(scalar_pair, QUARTER_PAIRS[1], COLUMN_HALVES[0], first_half)
-        quantise_pair(vector_pair, QUARTER_PAIRS[0], COLUMN_HALVES[1], last_half)
-        quantise_pair(scalar_pair, QUARTER_PAIRS[1], COLUMN_HALVES[1], last_half)
-        first_layer_of_last(W3, PASSES - 1, quarters_of(*vector_pair) + quarters_of(*scalar_pair))
+        nc.vector.tensor_copy(target[:, 0, :, late], row_pairs[1][:, 0])
+        for v, copy in enumerate((nc.vector.tensor_copy, nc.scalar.copy)):
+            copy(target[:, 1, :, late, :, v], row_pairs[1][:, 1, :, :, :, v])
+        quarters = {}
+        for first, last in ((0, 2), (3, 4), (2, 3)):
+            words = last_ring([P, (last - first) * P], U32, "w_words_last")
+            scales = stage.tile([P, (last - first) * P], U8, name="w_bytes_last", align_bytes=64, bufs=3)
+            quantise(words[:], scales[:], tile[:, first * H : last * H])
+            for t, quarter in enumerate(quarters_of(words, scales), first):
+                quarters[t] = quarter
+        for s in range(GROUPS):
+            for t in quarters:
+                pass_of_last(W3, PASSES - 1, s, t, quarters[t], t == 2)
         w2_last = round_w2(LAST, last_ring)
         put_back(FIRST, bank_first, 0, C)
 

@@ -32,7 +32,7 @@ SHARE_BESIDE_GATHERS = 48
 SHARE_PLAIN = 34
 
 STAGING_BUFS = 9
-LAST_BUFS = 12
+LAST_BUFS = 16
 CODES_BUFS = 5
 SUM_BANKS = 6
 SHORT_BANKS = 2
@@ -132,11 +132,11 @@ def tile_routed_moe_kernel(tc, xT, w1, w3, w2, gate, offs, out):
             tile = keep.tile([P, last - first, H], F32, name=f"w_rows{first}")
             nc.sync.dma_start(out=tile[:], in_=w_views[W3][LAST, :, PASSES - 1, first:last])
             row_pairs.append(loaded_by_quarter(tile[:]))
+        load_gate(FIRST)
         w2_raw[LAST] = keep.tile([P, J, N], F32, name="w2_raw_last")
         for l in range(2):
             rows = w2_raw[LAST][l::2].rearrange("p (u v) n -> p u (v n)", v=2)
             nc.sync.dma_start(out=rows, in_=w2_by_quarter[LAST, l])
-        load_gate(FIRST)
         load_gate(LAST)
 
         slot_words = {}
@@ -169,9 +169,9 @@ def tile_routed_moe_kernel(tc, xT, w1, w3, w2, gate, offs, out):
             scales = stage.tile([P, H], U8, name="w_bytes", align_bytes=64)
             return words, scales
 
-        def round_w2(e, ring):
+        def round_w2(e, ring, copy):
             tile = ring([P, N * J], BF16, "w2_interleaved")
-            nc.scalar.copy(interleaved_order(tile[:]), loaded_order(w2_raw[e][:]))
+            copy(interleaved_order(tile[:]), loaded_order(w2_raw[e][:]))
             return tile
 
         def quantise_w2(e, words, interleaved):
@@ -180,14 +180,13 @@ def tile_routed_moe_kernel(tc, xT, w1, w3, w2, gate, offs, out):
             w2_codes[e] = (words, scales)
 
         def quantise_hidden(words, interleaved):
-            scales = small.tile(list(words.shape), U8, name="h_bytes", align_bytes=64, bufs=1 + GROUPS)
+            scales = small.tile(list(words.shape), U8, name="h_bytes", align_bytes=64, bufs=2 + GROUPS)
             quantise(words[:], scales[:], interleaved[:])
             return words, scales
 
-        def second_layer(e, words, scales):
-            bank = short_bank(list(words.shape))
+        def second_layer(e, y, words, scales):
             nc.tensor.matmul_mx(
-                out=bank[:],
+                out=y,
                 lhsT=w2_codes[e][0][:].bitcast(FP8X4),
                 lhsT_scale=w2_codes[e][1][:],
                 rhs=words[:].bitcast(FP8X4),
@@ -195,11 +194,10 @@ def tile_routed_moe_kernel(tc, xT, w1, w3, w2, gate, offs, out):
                 start=True,
                 stop=True,
             )
-            return bank
 
-        def put_back(e, bank, first, last):
+        def put_back(e, y, first, last):
             weighed = last_ring([P, last - first], F32, "weighed")
-            nc.vector.tensor_tensor(weighed[:], bank[:], gates[e][:, first:last], MULT)
+            nc.vector.tensor_tensor(weighed[:], y, gates[e][:, first:last], MULT)
             entries = offsets[:, (e * C + first) // LIST_COLUMN : (e * C + last) // LIST_COLUMN]
             nc.scalar.activation(window[:].indirect(entries), weighed[:], COPY)
 
@@ -302,12 +300,12 @@ def tile_routed_moe_kernel(tc, xT, w1, w3, w2, gate, offs, out):
                 nc.scalar.activation(target, source, RELU)
             return tile
 
-        def multiply_last(s, rectified):
-            tile = last_ring([P, H], BF16, "hidden_last")
+        def multiply_last(s, rectified, first, last):
+            tile = last_ring([P, (last - first) * J], BF16, "hidden_last")
             nc.vector.tensor_tensor(
                 interleaved_by_slot_pair(tile[:]),
-                sums_by_slot_pair(sums[LAST, W3, s][:]),
-                stored_by_slot_pair(rectified[:]),
+                sums_by_slot_pair(sums[LAST, W3, s][:, :, first:last]),
+                stored_by_slot_pair(rectified[:, first * J : last * J]),
                 MULT,
             )
             return tile
@@ -322,11 +320,12 @@ def tile_routed_moe_kernel(tc, xT, w1, w3, w2, gate, offs, out):
         chunk_of_last(W1, 0)
         hidden_rows = multiply_first(rectified_first)
         hidden_first = turn_hidden(hidden_rows)
-        w2_first = round_w2(FIRST, staging)
+        w2_first = round_w2(FIRST, staging, nc.scalar.copy)
         chunk_of_last(W1, 1)
         quantise_w2(FIRST, keep.tile([P, N], U32, name="w2_words", align_bytes=64), w2_first)
         codes_first = quantise_hidden(keep.tile([P, C], U32, name="h_words", align_bytes=64), hidden_first)
-        bank_first = second_layer(FIRST, *codes_first)
+        bank_first = short_bank([P, C])
+        second_layer(FIRST, bank_first[:], *codes_first)
         chunk_of_last(W1, 2)
 
         tile = round_last(W3, 0, ALL_COLUMNS)
@@ -345,10 +344,11 @@ def tile_routed_moe_kernel(tc, xT, w1, w3, w2, gate, offs, out):
         quantise(words[:], scales[:], before[:])
         first_layer_of_last(W3, 1, quarters_of(words, scales))
         nc.vector.tensor_copy(target[:, 0, :, late], row_pairs[1][:, 0])
-        for v, copy in enumerate((nc.vector.tensor_copy, nc.scalar.copy)):
-            copy(target[:, 1, :, late, :, v], row_pairs[1][:, 1, :, :, :, v])
+        for v in range(2):
+            nc.scalar.copy(target[:, 1, :, late, :, v], row_pairs[1][:, 1, :, :, :, v])
+        put_back(FIRST, bank_first[:, :P], 0, P)
         quarters = {}
-        for first, last in ((0, 2), (3, 4), (2, 3)):
+        for first, last in ((0, 2), (2, 3), (3, 4)):
             words = last_ring([P, (last - first) * P], U32, "w_words_last")
             scales = stage.tile([P, (last - first) * P], U8, name="w_bytes_last", align_bytes=64, bufs=3)
             quantise(words[:], scales[:], tile[:, first * H : last * H])
@@ -356,17 +356,22 @@ def tile_routed_moe_kernel(tc, xT, w1, w3, w2, gate, offs, out):
                 quarters[t] = quarter
         for s in range(GROUPS):
             for t in quarters:
-                pass_of_last(W3, PASSES - 1, s, t, quarters[t], t == 2)
-        w2_last = round_w2(LAST, last_ring)
-        put_back(FIRST, bank_first, 0, C)
+                pass_of_last(W3, PASSES - 1, s, t, quarters[t], t == J - 1)
+        put_back(FIRST, bank_first[:, P:], P, C)
+        w2_last = round_w2(LAST, last_ring, nc.vector.tensor_copy)
 
-        hidden = multiply_last(0, rectified_last[0])
+        early = multiply_last(0, rectified_last[0], 0, P // 2)
+        late = multiply_last(0, rectified_last[0], P // 2, P)
+        codes_early = quantise_hidden(last_ring([P, P // 2], U32, "h_words_last"), early)
         quantise_w2(LAST, last_ring([P, N], U32, "w2_words_last"), w2_last)
+        codes_late = quantise_hidden(last_ring([P, P // 2], U32, "h_words_last"), late)
+        bank = short_bank([P, P])
+        second_layer(LAST, bank[:, : P // 2], *codes_early)
+        second_layer(LAST, bank[:, P // 2 :], *codes_late)
+        hidden = multiply_last(1, rectified_last[1], 0, P)
+        put_back(LAST, bank[:], 0, P)
         codes = quantise_hidden(last_ring([P, P], U32, "h_words_last"), hidden)
-        bank = second_layer(LAST, *codes)
-        hidden = multiply_last(1, rectified_last[1])
-        put_back(LAST, bank, 0, P)
-        codes = quantise_hidden(last_ring([P, P], U32, "h_words_last"), hidden)
-        bank = second_layer(LAST, *codes)
-        put_back(LAST, bank, P, C)
+        bank = short_bank([P, P])
+        second_layer(LAST, bank[:], *codes)
+        put_back(LAST, bank[:], P, C)
         nc.sync.dma_start(out=out, in_=window[:])

@@ -132,11 +132,11 @@ def tile_routed_moe_kernel(tc, xT, w1, w3, w2, gate, offs, out):
             tile = keep.tile([P, last - first, H], F32, name=f"w_rows{first}")
             nc.sync.dma_start(out=tile[:], in_=w_views[W3][LAST, :, PASSES - 1, first:last])
             row_pairs.append(loaded_by_quarter(tile[:]))
-        load_gate(FIRST)
         w2_raw[LAST] = keep.tile([P, J, N], F32, name="w2_raw_last")
         for l in range(2):
             rows = w2_raw[LAST][l::2].rearrange("p (u v) n -> p u (v n)", v=2)
             nc.sync.dma_start(out=rows, in_=w2_by_quarter[LAST, l])
+        load_gate(FIRST)
         load_gate(LAST)
 
         slot_words = {}
@@ -343,22 +343,24 @@ def tile_routed_moe_kernel(tc, xT, w1, w3, w2, gate, offs, out):
         words, scales = chunk_codes()
         quantise(words[:], scales[:], before[:])
         first_layer_of_last(W3, 1, quarters_of(words, scales))
-        nc.vector.tensor_copy(target[:, 0, :, late], row_pairs[1][:, 0])
+        middle = target.shape[2] // 2
         for v in range(2):
-            nc.scalar.copy(target[:, 1, :, late, :, v], row_pairs[1][:, 1, :, :, :, v])
-        put_back(FIRST, bank_first[:, :P], 0, P)
+            nc.vector.tensor_copy(target[:, 0, :, late, :, v], row_pairs[1][:, 0, :, :, :, v])
+        nc.scalar.copy(target[:, 1, :, late, :, 0], row_pairs[1][:, 1, :, :, :, 0])
+        nc.vector.tensor_copy(target[:, 1, :middle, late, :, 1], row_pairs[1][:, 1, :middle, :, :, 1])
+        nc.scalar.copy(target[:, 1, middle:, late, :, 1], row_pairs[1][:, 1, middle:, :, :, 1])
         quarters = {}
-        for first, last in ((0, 2), (2, 3), (3, 4)):
+        for first, last in ((0, 1), (1, 2), (2, 3), (3, 4)):
             words = last_ring([P, (last - first) * P], U32, "w_words_last")
-            scales = stage.tile([P, (last - first) * P], U8, name="w_bytes_last", align_bytes=64, bufs=3)
+            scales = stage.tile([P, (last - first) * P], U8, name="w_bytes_last", align_bytes=64, bufs=4)
             quantise(words[:], scales[:], tile[:, first * H : last * H])
             for t, quarter in enumerate(quarters_of(words, scales), first):
                 quarters[t] = quarter
         for s in range(GROUPS):
             for t in quarters:
                 pass_of_last(W3, PASSES - 1, s, t, quarters[t], t == J - 1)
-        put_back(FIRST, bank_first[:, P:], P, C)
-        w2_last = round_w2(LAST, last_ring, nc.vector.tensor_copy)
+        w2_last = round_w2(LAST, last_ring, nc.scalar.copy)
+        put_back(FIRST, bank_first[:], 0, C)
 
         early = multiply_last(0, rectified_last[0], 0, P // 2)
         late = multiply_last(0, rectified_last[0], P // 2, P)

@@ -1,7 +1,6 @@
 from contextlib import ExitStack
 
 import concourse.mybir as mybir
-from concourse.masks import make_identity
 
 K, T, E, C, H, N = 1536, 1024, 2, 256, 512, 128
 FLOPS = 2 * E * C * (2 * K * H + H * N)
@@ -25,11 +24,7 @@ RUN = 4
 LIST_COLUMN = 16
 W1, W3 = 0, 1
 FIRST, LAST = 0, 1
-ALL_COLUMNS = (0, H)
 ROW_PAIRS = ((0, 2), (2, 4))
-
-SHARE_BESIDE_GATHERS = 48
-SHARE_PLAIN = 34
 
 STAGING_BUFS = 9
 LAST_BUFS = 16
@@ -41,8 +36,7 @@ SHORT_BANKS = 2
 def tile_routed_moe_kernel(tc, xT, w1, w3, w2, gate, offs, out):
     nc = tc.nc
     xT_view = xT.rearrange("(g p j) n -> g p j n", p=P, j=J)
-    w_views = [w.rearrange("e (g p j) n -> e p g j n", p=P, j=J) for w in (w1, w3)]
-    w2_view = w2.rearrange("e (p j) n -> e p j n", j=J)
+    w_views = [w.rearrange("e (g p j) n -> e g p j n", p=P, j=J) for w in (w1, w3)]
     w2_by_quarter = w2.rearrange("e (m u l v) n -> e l m u (v n)", u=2, l=2, v=2)
 
     def loaded_order(ap):
@@ -56,12 +50,6 @@ def tile_routed_moe_kernel(tc, xT, w1, w3, w2, gate, offs, out):
 
     def interleaved_by_quarter(ap):
         return ap.rearrange("p (u v m l j) -> p u m j l v", u=2, v=2, l=2, j=J)
-
-    def sums_by_word(ap):
-        return ap.rearrange("s (w u b) -> s u w b", u=2, b=2)
-
-    def stored_by_word(ap):
-        return ap.rearrange("s (u w b) -> s u w b", u=2, b=2)
 
     def sums_by_slot_pair(ap):
         return ap.rearrange("p t (c r) -> p c t r", r=2)
@@ -81,6 +69,9 @@ def tile_routed_moe_kernel(tc, xT, w1, w3, w2, gate, offs, out):
         def staging(shape, dtype, name):
             return stage.tile(shape, dtype, name=name, tag="staging", align_bytes=64, bufs=STAGING_BUFS)
 
+        def codes_ring(shape, dtype, name):
+            return stage.tile(shape, dtype, name=name, tag="codes", align_bytes=64)
+
         def last_ring(shape, dtype, name):
             return small.tile(shape, dtype, name=name, tag="last", align_bytes=64, bufs=LAST_BUFS)
 
@@ -89,23 +80,26 @@ def tile_routed_moe_kernel(tc, xT, w1, w3, w2, gate, offs, out):
 
         offsets = keep.tile([P, SLOTS // LIST_COLUMN], U16, name="offsets")
         window = keep.tile([P, T], F32, name="window")
-        identity = keep.tile([P, P], F32, name="identity")
         nc.vector.memset(window[:], 0.0)
-        make_identity(nc, identity[:])
 
         x_raw = {}
         w_raw = {}
         w2_raw = {}
         gates = {}
 
-        def load_passes(e, m, first, last):
+        def load_chunk(e, m, g):
             if (e, m) == (LAST, W3):
-                tile = stage.tile([P, last - first, J, H], F32, name="w_raw", tag="raw", bufs=PASSES)
+                tile = stage.tile([P, J, H], F32, name="w_raw", tag="raw", bufs=PASSES)
             else:
-                tile = keep.tile([P, last - first, J, H], F32, name=f"w_raw{e}{m}{first}")
-            nc.sync.dma_start(out=tile[:], in_=w_views[m][e, :, first:last])
-            for g in range(first, last):
-                w_raw[e, m, g, ALL_COLUMNS] = tile[:, g - first]
+                tile = keep.tile([P, J, H], F32, name=f"w_raw{e}{m}{g}")
+            nc.sync.dma_start(out=tile[:], in_=w_views[m][e, g])
+            w_raw[e, m, g] = tile
+
+        def load_w2(e):
+            w2_raw[e] = keep.tile([P, J, N], F32, name=f"w2_raw{e}")
+            for l in range(2):
+                rows = w2_raw[e][l::2].rearrange("p (u v) n -> p u (v n)", v=2)
+                nc.sync.dma_start(out=rows, in_=w2_by_quarter[e, l])
 
         def load_gate(e):
             gates[e] = keep.tile([P, C], F32, name=f"gates{e}")
@@ -116,26 +110,21 @@ def tile_routed_moe_kernel(tc, xT, w1, w3, w2, gate, offs, out):
             nc.sync.dma_start(out=x_raw[g][:], in_=xT_view[g])
             if g == 0:
                 nc.sync.dma_start(offsets[:], offs)
-        load_passes(FIRST, W1, 0, PASSES - 1)
-        load_passes(FIRST, W1, PASSES - 1, PASSES)
-        for g in range(PASSES):
-            load_passes(FIRST, W3, g, g + 1)
-        load_passes(LAST, W1, 0, 1)
-        w2_raw[FIRST] = keep.tile([P, J, N], F32, name="w2_raw_first")
-        nc.sync.dma_start(out=w2_raw[FIRST][:], in_=w2_view[FIRST])
+        for m in (W1, W3):
+            for g in range(PASSES):
+                load_chunk(FIRST, m, g)
+        load_chunk(LAST, W1, 0)
+        load_w2(FIRST)
         for g in range(1, PASSES):
-            load_passes(LAST, W1, g, g + 1)
+            load_chunk(LAST, W1, g)
         for g in range(PASSES - 1):
-            load_passes(LAST, W3, g, g + 1)
+            load_chunk(LAST, W3, g)
         row_pairs = []
         for first, last in ROW_PAIRS:
             tile = keep.tile([P, last - first, H], F32, name=f"w_rows{first}")
-            nc.sync.dma_start(out=tile[:], in_=w_views[W3][LAST, :, PASSES - 1, first:last])
+            nc.sync.dma_start(out=tile[:], in_=w_views[W3][LAST, PASSES - 1, :, first:last])
             row_pairs.append(loaded_by_quarter(tile[:]))
-        w2_raw[LAST] = keep.tile([P, J, N], F32, name="w2_raw_last")
-        for l in range(2):
-            rows = w2_raw[LAST][l::2].rearrange("p (u v) n -> p u (v n)", v=2)
-            nc.sync.dma_start(out=rows, in_=w2_by_quarter[LAST, l])
+        load_w2(LAST)
         load_gate(FIRST)
         load_gate(LAST)
 
@@ -164,14 +153,9 @@ def tile_routed_moe_kernel(tc, xT, w1, w3, w2, gate, offs, out):
         def quantise(words, scales, interleaved):
             nc.vector.quantize_mx(out=words.bitcast(FP8X4), scales=scales, in_=interleaved)
 
-        def chunk_codes():
-            words = stage.tile([P, H], U32, name="w_words", align_bytes=64)
-            scales = stage.tile([P, H], U8, name="w_bytes", align_bytes=64)
-            return words, scales
-
-        def round_w2(e, ring, copy):
+        def round_w2(e, ring):
             tile = ring([P, N * J], BF16, "w2_interleaved")
-            copy(interleaved_order(tile[:]), loaded_order(w2_raw[e][:]))
+            nc.scalar.copy(interleaved_order(tile[:]), loaded_order(w2_raw[e][:]))
             return tile
 
         def quantise_w2(e, words, interleaved):
@@ -201,176 +185,148 @@ def tile_routed_moe_kernel(tc, xT, w1, w3, w2, gate, offs, out):
             entries = offsets[:, (e * C + first) // LIST_COLUMN : (e * C + last) // LIST_COLUMN]
             nc.scalar.activation(window[:].indirect(entries), weighed[:], COPY)
 
-        def chunk_of_first(m, g, share):
+        def round_quarters(copy, target, source, first, last):
+            for u in range(2):
+                own = [t % 2 for t in range(first, last) if t // 2 == u]
+                if len(own) == 2:
+                    copy(target[:, u], source[:, u])
+                elif own:
+                    copy(target[:, u, :, :, :, own[0]], source[:, u, :, :, :, own[0]])
+
+        def round_chunk(e, m, g, on_vector):
             tile = staging([P, H * J], BF16, "w_interleaved")
-            target = interleaved_order(tile[:])
-            source = loaded_order(w_raw[FIRST, m, g, ALL_COLUMNS])
-            cut = H * share // 64 // RUN
-            nc.scalar.copy(target[:, :cut], source[:, :cut])
-            nc.vector.tensor_copy(target[:, cut:], source[:, cut:])
-            words, scales = chunk_codes()
-            quantise(words[:], scales[:], tile[:])
-            for s in range(GROUPS):
-                slots = slice(s * P, (s + 1) * P)
-                if g == 0:
-                    sums[FIRST, m, s] = psum.tile([P, H], F32, name="sums", bufs=SUM_BANKS)
-                nc.tensor.matmul_mx(
-                    out=sums[FIRST, m, s][:],
-                    lhsT=slot_words[g][:, slots].bitcast(FP8X4),
-                    lhsT_scale=slot_bytes[4 * g :, slots],
-                    rhs=words[:].bitcast(FP8X4),
-                    rhs_scale=scales[:],
-                    start=(g == 0),
-                    stop=(g == PASSES - 1),
-                )
-
-        def rectify_first():
-            tile = staging([P, GROUPS, H], F32, "rectified")
-            for s in range(GROUPS):
-                nc.scalar.activation(stored_by_word(tile[:, s, :]), sums_by_word(sums[FIRST, W1, s][:]), RELU)
-            return tile
-
-        def multiply_first(rectified):
-            rows = small.tile([P, GROUPS, H], BF16, name="hidden_rows", align_bytes=64, bufs=1)
-            for s in range(GROUPS):
-                nc.vector.tensor_tensor(
-                    stored_by_word(rows[:, s, :]),
-                    sums_by_word(sums[FIRST, W3, s][:]),
-                    stored_by_word(rectified[:, s, :]),
-                    MULT,
-                )
-            return rows
-
-        def turn_hidden(rows):
-            tile = small.tile([P, GROUPS * H], BF16, name="hidden_first", align_bytes=64, bufs=1)
-            for s in range(GROUPS):
-                turned = short_bank([P, 2, P])
-                pairs = rows[:, s, :].bitcast(F32)
-                for u in range(2):
-                    nc.tensor.transpose(turned[:, u, :], pairs[:, u * P : (u + 1) * P], identity[:])
-                nc.scalar.copy(
-                    tile[:, s * H : (s + 1) * H].bitcast(F32).rearrange("p (n u) -> p n u", u=2),
-                    turned[:].rearrange("p u n -> p n u"),
-                )
-            return tile
-
-        def round_last(m, g, columns):
-            tile = staging([P, (columns[1] - columns[0]) * J], BF16, "w_interleaved")
             target = interleaved_by_quarter(tile[:])
-            source = loaded_by_quarter(w_raw[LAST, m, g, columns])
-            for u, copy in enumerate((nc.vector.tensor_copy, nc.scalar.copy)):
-                copy(target[:, u], source[:, u])
+            source = loaded_by_quarter(w_raw[e, m, g][:])
+            round_quarters(nc.vector.tensor_copy, target, source, 0, on_vector)
+            round_quarters(nc.scalar.copy, target, source, on_vector, J)
             return tile
 
-        def pass_of_last(m, g, s, t, quarter, stop):
-            slots = slice(C + s * P, C + (s + 1) * P)
-            if g == 0 and t == 0:
-                sums[LAST, m, s] = psum.tile([P, J, P], F32, name="sums", bufs=SUM_BANKS)
+        def quantise_quarters(tile, ring, first, last):
+            words = ring([P, (last - first) * P], U32, "w_words")
+            scales = stage.tile([P, (last - first) * P], U8, name="w_bytes", align_bytes=64, bufs=8)
+            quantise(words[:], scales[:], tile[:, first * H : last * H])
+            return [(words[:, n : n + P], scales[:, n : n + P]) for n in range(0, (last - first) * P, P)]
+
+        def one_pass(result, quarter, g, slots, start, stop):
             nc.tensor.matmul_mx(
-                out=sums[LAST, m, s][:, t, :],
+                out=result,
                 lhsT=quarter[0].bitcast(FP8X4),
                 lhsT_scale=quarter[1],
                 rhs=slot_words[g][:, slots].bitcast(FP8X4),
                 rhs_scale=slot_bytes[4 * g :, slots],
-                start=(g == 0 and t == 0),
+                start=start,
                 stop=stop,
             )
 
-        def first_layer_of_last(m, g, quarters):
+        def passes_of_w1(e, g, quarters):
+            for u in range(2):
+                if g == 0:
+                    sums[e, W1, u] = psum.tile([P, 2, C], F32, name="sums", bufs=SUM_BANKS)
+                for v in range(2):
+                    one_pass(
+                        sums[e, W1, u][:, v, :],
+                        quarters[2 * u + v],
+                        g,
+                        slice(e * C, (e + 1) * C),
+                        g == 0 and v == 0,
+                        g == PASSES - 1 and v == 1,
+                    )
+
+        def passes_of_w3(e, g, quarters):
             for s in range(GROUPS):
+                if g == 0:
+                    sums[e, W3, s] = psum.tile([P, J, P], F32, name="sums", bufs=SUM_BANKS)
                 for t in range(J):
-                    pass_of_last(m, g, s, t, quarters[t], g == PASSES - 1 and t == J - 1)
+                    one_pass(
+                        sums[e, W3, s][:, t, :],
+                        quarters[t],
+                        g,
+                        slice(e * C + s * P, e * C + (s + 1) * P),
+                        g == 0 and t == 0,
+                        g == PASSES - 1 and t == J - 1,
+                    )
 
-        def quarters_of(words, scales):
-            return [(words[:, n : n + P], scales[:, n : n + P]) for n in range(0, words.shape[1], P)]
+        def finish_chunk(e, m, g, tile):
+            quarters = quantise_quarters(tile, codes_ring, 0, J)
+            (passes_of_w1, passes_of_w3)[m](e, g, quarters)
 
-        def chunk_of_last(m, g):
-            tile = round_last(m, g, ALL_COLUMNS)
-            words, scales = chunk_codes()
-            quantise(words[:], scales[:], tile[:])
-            first_layer_of_last(m, g, quarters_of(words, scales))
+        def finish_by_halves(e, g, tile):
+            quarters = quantise_quarters(tile, staging, 0, 2) + quantise_quarters(tile, staging, 2, J)
+            passes_of_w3(e, g, quarters)
 
-        def rectify_last(s):
-            tile = staging([P, H], F32, "rectified")
+        def rectify(e):
+            tile = staging([P, C * J], F32, "rectified")
             target = stored_by_slot_pair(tile[:])
-            source = sums_by_slot_pair(sums[LAST, W1, s][:])
-            if s == 0:
-                nc.vector.tensor_scalar_max(target, source, 0.0)
-            else:
-                nc.scalar.activation(target, source, RELU)
+            for u in range(2):
+                nc.scalar.activation(target[:, :, 2 * u : 2 * u + 2], sums_by_slot_pair(sums[e, W1, u][:]), RELU)
             return tile
+
+        def multiply(e, s, target, rectified, first, last):
+            nc.vector.tensor_tensor(
+                interleaved_by_slot_pair(target),
+                sums_by_slot_pair(sums[e, W3, s][:, :, first:last]),
+                stored_by_slot_pair(rectified[:, (s * P + first) * J : (s * P + last) * J]),
+                MULT,
+            )
 
         def multiply_last(s, rectified, first, last):
             tile = last_ring([P, (last - first) * J], BF16, "hidden_last")
-            nc.vector.tensor_tensor(
-                interleaved_by_slot_pair(tile[:]),
-                sums_by_slot_pair(sums[LAST, W3, s][:, :, first:last]),
-                stored_by_slot_pair(rectified[:, first * J : last * J]),
-                MULT,
-            )
+            multiply(LAST, s, tile[:], rectified, first, last)
             return tile
 
         for g in range(PASSES):
-            chunk_of_first(W1, g, SHARE_BESIDE_GATHERS if g < PASSES - 1 else SHARE_PLAIN)
-        chunk_of_first(W3, 0, SHARE_PLAIN)
-        rectified_first = rectify_first()
-        chunk_of_first(W3, 1, SHARE_PLAIN)
-        chunk_of_first(W3, 2, SHARE_PLAIN)
+            finish_chunk(FIRST, W1, g, round_chunk(FIRST, W1, g, 1 if g < PASSES - 1 else 2))
+        finish_chunk(FIRST, W3, 0, round_chunk(FIRST, W3, 0, 2))
+        tile = round_chunk(FIRST, W3, 1, 3)
+        rectified_first = rectify(FIRST)
+        finish_chunk(FIRST, W3, 1, tile)
+        finish_chunk(FIRST, W3, 2, round_chunk(FIRST, W3, 2, 2))
 
-        chunk_of_last(W1, 0)
-        hidden_rows = multiply_first(rectified_first)
-        hidden_first = turn_hidden(hidden_rows)
-        w2_first = round_w2(FIRST, staging, nc.scalar.copy)
-        chunk_of_last(W1, 1)
+        finish_chunk(LAST, W1, 0, round_chunk(LAST, W1, 0, 2))
+        w2_first = round_w2(FIRST, staging)
+        tile = round_chunk(LAST, W1, 1, 1)
+        hidden_first = staging([P, C * J], BF16, "hidden_first")
+        for s in range(GROUPS):
+            multiply(FIRST, s, hidden_first[:, s * H : (s + 1) * H], rectified_first, 0, P)
         quantise_w2(FIRST, keep.tile([P, N], U32, name="w2_words", align_bytes=64), w2_first)
         codes_first = quantise_hidden(keep.tile([P, C], U32, name="h_words", align_bytes=64), hidden_first)
         bank_first = short_bank([P, C])
         second_layer(FIRST, bank_first[:], *codes_first)
-        chunk_of_last(W1, 2)
+        finish_chunk(LAST, W1, 1, tile)
+        finish_chunk(LAST, W1, 2, round_chunk(LAST, W1, 2, 2))
 
-        tile = round_last(W3, 0, ALL_COLUMNS)
-        rectified_last = [rectify_last(s) for s in range(GROUPS)]
-        words, scales = chunk_codes()
-        quantise(words[:], scales[:], tile[:])
-        first_layer_of_last(W3, 0, quarters_of(words, scales))
-        before = round_last(W3, 1, ALL_COLUMNS)
+        tile = round_chunk(LAST, W3, 0, 3)
+        rectified_last = rectify(LAST)
+        finish_by_halves(LAST, 0, tile)
+        finish_by_halves(LAST, 1, round_chunk(LAST, W3, 1, 2))
 
         tile = staging([P, H * J], BF16, "w_interleaved")
         target = interleaved_by_quarter(tile[:])
         early, late = (slice(*pair) for pair in ROW_PAIRS)
         nc.vector.tensor_copy(target[:, 0, :, early], row_pairs[0][:, 0])
         nc.scalar.copy(target[:, 1, :, early], row_pairs[0][:, 1])
-        words, scales = chunk_codes()
-        quantise(words[:], scales[:], before[:])
-        first_layer_of_last(W3, 1, quarters_of(words, scales))
         middle = target.shape[2] // 2
         for v in range(2):
             nc.vector.tensor_copy(target[:, 0, :, late, :, v], row_pairs[1][:, 0, :, :, :, v])
         nc.scalar.copy(target[:, 1, :, late, :, 0], row_pairs[1][:, 1, :, :, :, 0])
         nc.vector.tensor_copy(target[:, 1, :middle, late, :, 1], row_pairs[1][:, 1, :middle, :, :, 1])
         nc.scalar.copy(target[:, 1, middle:, late, :, 1], row_pairs[1][:, 1, middle:, :, :, 1])
-        quarters = {}
-        for first, last in ((0, 1), (1, 2), (2, 3), (3, 4)):
-            words = last_ring([P, (last - first) * P], U32, "w_words_last")
-            scales = stage.tile([P, (last - first) * P], U8, name="w_bytes_last", align_bytes=64, bufs=4)
-            quantise(words[:], scales[:], tile[:, first * H : last * H])
-            for t, quarter in enumerate(quarters_of(words, scales), first):
-                quarters[t] = quarter
-        for s in range(GROUPS):
-            for t in quarters:
-                pass_of_last(W3, PASSES - 1, s, t, quarters[t], t == J - 1)
-        w2_last = round_w2(LAST, last_ring, nc.scalar.copy)
+        quarters = []
+        for t in range(J):
+            quarters.extend(quantise_quarters(tile, last_ring, t, t + 1))
+        passes_of_w3(LAST, PASSES - 1, quarters)
+        w2_last = round_w2(LAST, last_ring)
         put_back(FIRST, bank_first[:], 0, C)
 
-        early = multiply_last(0, rectified_last[0], 0, P // 2)
-        late = multiply_last(0, rectified_last[0], P // 2, P)
+        early = multiply_last(0, rectified_last, 0, P // 2)
+        late = multiply_last(0, rectified_last, P // 2, P)
         codes_early = quantise_hidden(last_ring([P, P // 2], U32, "h_words_last"), early)
         quantise_w2(LAST, last_ring([P, N], U32, "w2_words_last"), w2_last)
         codes_late = quantise_hidden(last_ring([P, P // 2], U32, "h_words_last"), late)
         bank = short_bank([P, P])
         second_layer(LAST, bank[:, : P // 2], *codes_early)
         second_layer(LAST, bank[:, P // 2 :], *codes_late)
-        hidden = multiply_last(1, rectified_last[1], 0, P)
+        hidden = multiply_last(1, rectified_last, 0, P)
         put_back(LAST, bank[:], 0, P)
         codes = quantise_hidden(last_ring([P, P], U32, "h_words_last"), hidden)
         bank = short_bank([P, P])

@@ -232,19 +232,22 @@ def tile_routed_moe_kernel(tc, xT, w1, w3, w2, gate, offs, out):
                         g == PASSES - 1 and v == 1,
                     )
 
+        def pass_of_w3(e, g, s, t, quarter):
+            if g == 0 and t == 0:
+                sums[e, W3, s] = psum.tile([P, J, P], F32, name="sums", bufs=SUM_BANKS)
+            one_pass(
+                sums[e, W3, s][:, t, :],
+                quarter,
+                g,
+                slice(e * C + s * P, e * C + (s + 1) * P),
+                g == 0 and t == 0,
+                g == PASSES - 1 and t == J - 1,
+            )
+
         def passes_of_w3(e, g, quarters):
-            for s in range(GROUPS):
-                if g == 0:
-                    sums[e, W3, s] = psum.tile([P, J, P], F32, name="sums", bufs=SUM_BANKS)
-                for t in range(J):
-                    one_pass(
-                        sums[e, W3, s][:, t, :],
-                        quarters[t],
-                        g,
-                        slice(e * C + s * P, e * C + (s + 1) * P),
-                        g == 0 and t == 0,
-                        g == PASSES - 1 and t == J - 1,
-                    )
+            for t in range(J):
+                for s in range(GROUPS):
+                    pass_of_w3(e, g, s, t, quarters[t])
 
         def finish_chunk(e, m, g, tile):
             quarters = quantise_quarters(tile, codes_ring, 0, J)
@@ -314,7 +317,9 @@ def tile_routed_moe_kernel(tc, xT, w1, w3, w2, gate, offs, out):
         quarters = []
         for t in range(J):
             quarters.extend(quantise_quarters(tile, last_ring, t, t + 1))
-        passes_of_w3(LAST, PASSES - 1, quarters)
+        for s in range(GROUPS):
+            for t in range(J):
+                pass_of_w3(LAST, PASSES - 1, s, t, quarters[t])
         w2_last = round_w2(LAST, last_ring)
         put_back(FIRST, bank_first[:], 0, C)
 

@@ -26,6 +26,7 @@ W1, W3 = 0, 1
 FIRST, LAST = 0, 1
 ROW_PAIRS = ((0, 2), (2, 4))
 
+DMA_ALIGN = 512
 STAGING_BUFS = 9
 LAST_BUFS = 16
 CODES_BUFS = 5
@@ -78,8 +79,8 @@ def tile_routed_moe_kernel(tc, xT, w1, w3, w2, gate, offs, out):
         def short_bank(shape):
             return psum.tile(shape, F32, name="short", bufs=SHORT_BANKS)
 
-        offsets = keep.tile([P, SLOTS // LIST_COLUMN], U16, name="offsets")
-        window = keep.tile([P, T], F32, name="window")
+        offsets = keep.tile([P, SLOTS // LIST_COLUMN], U16, name="offsets", align_bytes=DMA_ALIGN)
+        window = keep.tile([P, T], F32, name="window", align_bytes=DMA_ALIGN)
         nc.vector.memset(window[:], 0.0)
 
         x_raw = {}
@@ -89,24 +90,24 @@ def tile_routed_moe_kernel(tc, xT, w1, w3, w2, gate, offs, out):
 
         def load_chunk(e, m, g):
             if (e, m) == (LAST, W3):
-                tile = stage.tile([P, J, H], F32, name="w_raw", tag="raw", bufs=PASSES)
+                tile = stage.tile([P, J, H], F32, name="w_raw", tag="raw", bufs=PASSES, align_bytes=DMA_ALIGN)
             else:
-                tile = keep.tile([P, J, H], F32, name=f"w_raw{e}{m}{g}")
+                tile = keep.tile([P, J, H], F32, name=f"w_raw{e}{m}{g}", align_bytes=DMA_ALIGN)
             nc.sync.dma_start(out=tile[:], in_=w_views[m][e, g])
             w_raw[e, m, g] = tile
 
         def load_w2(e):
-            w2_raw[e] = keep.tile([P, J, N], F32, name=f"w2_raw{e}")
+            w2_raw[e] = keep.tile([P, J, N], F32, name=f"w2_raw{e}", align_bytes=DMA_ALIGN)
             for l in range(2):
                 rows = w2_raw[e][l::2].rearrange("p (u v) n -> p u (v n)", v=2)
                 nc.sync.dma_start(out=rows, in_=w2_by_quarter[e, l])
 
         def load_gate(e):
-            gates[e] = keep.tile([P, C], F32, name=f"gates{e}")
+            gates[e] = keep.tile([P, C], F32, name=f"gates{e}", align_bytes=DMA_ALIGN)
             nc.sync.dma_start(out=gates[e][:], in_=gate[:, e * C : (e + 1) * C])
 
         for g in range(PASSES):
-            x_raw[g] = stage.tile([P, J, T], F32, name="x_raw", tag="raw", bufs=PASSES)
+            x_raw[g] = stage.tile([P, J, T], F32, name="x_raw", tag="raw", bufs=PASSES, align_bytes=DMA_ALIGN)
             nc.sync.dma_start(out=x_raw[g][:], in_=xT_view[g])
             if g == 0:
                 nc.sync.dma_start(offsets[:], offs)
@@ -121,7 +122,7 @@ def tile_routed_moe_kernel(tc, xT, w1, w3, w2, gate, offs, out):
             load_chunk(LAST, W3, g)
         row_pairs = []
         for first, last in ROW_PAIRS:
-            tile = keep.tile([P, last - first, H], F32, name=f"w_rows{first}")
+            tile = keep.tile([P, last - first, H], F32, name=f"w_rows{first}", align_bytes=DMA_ALIGN)
             nc.sync.dma_start(out=tile[:], in_=w_views[W3][LAST, PASSES - 1, :, first:last])
             row_pairs.append(loaded_by_quarter(tile[:]))
         load_w2(LAST)

@@ -24,7 +24,7 @@ RUN = 4
 LIST_COLUMN = 16
 W1, W3 = 0, 1
 FIRST, LAST = 0, 1
-ROW_PAIRS = ((0, 2), (2, 4))
+QUARTER_ORDER = (0, 2, 1, 3)
 
 DMA_ALIGN = 512
 STAGING_BUFS = 9
@@ -120,11 +120,11 @@ def tile_routed_moe_kernel(tc, xT, w1, w3, w2, gate, offs, out):
             load_chunk(LAST, W1, g)
         for g in range(PASSES - 1):
             load_chunk(LAST, W3, g)
-        row_pairs = []
-        for first, last in ROW_PAIRS:
-            tile = keep.tile([P, last - first, H], F32, name=f"w_rows{first}", align_bytes=DMA_ALIGN)
-            nc.sync.dma_start(out=tile[:], in_=w_views[W3][LAST, PASSES - 1, :, first:last])
-            row_pairs.append(loaded_by_quarter(tile[:]))
+        halves = []
+        for left in (0, H // 2):
+            tile = keep.tile([P, J, H // 2], F32, name=f"w_half{left}", align_bytes=DMA_ALIGN)
+            nc.sync.dma_start(out=tile[:], in_=w_views[W3][LAST, PASSES - 1, :, :, left : left + H // 2])
+            halves.append(loaded_by_quarter(tile[:]))
         load_w2(LAST)
         load_gate(FIRST)
         load_gate(LAST)
@@ -154,9 +154,9 @@ def tile_routed_moe_kernel(tc, xT, w1, w3, w2, gate, offs, out):
         def quantise(words, scales, interleaved):
             nc.vector.quantize_mx(out=words.bitcast(FP8X4), scales=scales, in_=interleaved)
 
-        def round_w2(e, ring):
+        def round_w2(e, ring, copy):
             tile = ring([P, N * J], BF16, "w2_interleaved")
-            nc.scalar.copy(interleaved_order(tile[:]), loaded_order(w2_raw[e][:]))
+            copy(interleaved_order(tile[:]), loaded_order(w2_raw[e][:]))
             return tile
 
         def quantise_w2(e, words, interleaved):
@@ -287,7 +287,7 @@ def tile_routed_moe_kernel(tc, xT, w1, w3, w2, gate, offs, out):
         finish_chunk(FIRST, W3, 2, round_chunk(FIRST, W3, 2, 2))
 
         finish_chunk(LAST, W1, 0, round_chunk(LAST, W1, 0, 2))
-        w2_first = round_w2(FIRST, staging)
+        w2_first = round_w2(FIRST, staging, nc.scalar.copy)
         tile = round_chunk(LAST, W1, 1, 1)
         hidden_first = staging([P, C * J], BF16, "hidden_first")
         for s in range(GROUPS):
@@ -302,26 +302,32 @@ def tile_routed_moe_kernel(tc, xT, w1, w3, w2, gate, offs, out):
         tile = round_chunk(LAST, W3, 0, 3)
         rectified_last = rectify(LAST)
         finish_by_halves(LAST, 0, tile)
-        finish_by_halves(LAST, 1, round_chunk(LAST, W3, 1, 2))
+        before = round_chunk(LAST, W3, 1, 2)
+        quarters_before = quantise_quarters(before, staging, 0, 2)
 
-        tile = staging([P, H * J], BF16, "w_interleaved")
+        width = P // 2
+        tile = staging([P, H // 2 * J], BF16, "w_interleaved")
         target = interleaved_by_quarter(tile[:])
-        early, late = (slice(*pair) for pair in ROW_PAIRS)
-        nc.vector.tensor_copy(target[:, 0, :, early], row_pairs[0][:, 0])
-        nc.scalar.copy(target[:, 1, :, early], row_pairs[0][:, 1])
-        middle = target.shape[2] // 2
-        for v in range(2):
-            nc.vector.tensor_copy(target[:, 0, :, late, :, v], row_pairs[1][:, 0, :, :, :, v])
-        nc.scalar.copy(target[:, 1, :, late, :, 0], row_pairs[1][:, 1, :, :, :, 0])
-        nc.vector.tensor_copy(target[:, 1, :middle, late, :, 1], row_pairs[1][:, 1, :middle, :, :, 1])
-        nc.scalar.copy(target[:, 1, middle:, late, :, 1], row_pairs[1][:, 1, middle:, :, :, 1])
+        round_quarters(nc.vector.tensor_copy, target, halves[0], 0, 2)
+        round_quarters(nc.scalar.copy, target, halves[0], 2, J)
+        passes_of_w3(LAST, 1, quarters_before + quantise_quarters(before, staging, 2, J))
         quarters = []
         for t in range(J):
-            quarters.extend(quantise_quarters(tile, last_ring, t, t + 1))
+            words = last_ring([P, P], U32, "w_words")
+            scales = stage.tile([P, P], U8, name="w_bytes", align_bytes=64, bufs=8)
+            quantise(words[:, :width], scales[:, :width], tile[:, t * width * J : (t + 1) * width * J])
+            quarters.append((words[:], scales[:]))
+        tile = staging([P, H // 2 * J], BF16, "w_interleaved")
+        target = interleaved_by_quarter(tile[:])
+        for t in range(J):
+            round_quarters(nc.vector.tensor_copy if t < 2 else nc.scalar.copy, target, halves[1], t, t + 1)
+        for t in QUARTER_ORDER:
+            words, scales = quarters[t]
+            quantise(words[:, width:], scales[:, width:], tile[:, t * width * J : (t + 1) * width * J])
         for s in range(GROUPS):
-            for t in range(J):
+            for t in QUARTER_ORDER:
                 pass_of_w3(LAST, PASSES - 1, s, t, quarters[t])
-        w2_last = round_w2(LAST, last_ring)
+        w2_last = round_w2(LAST, last_ring, nc.scalar.copy)
         put_back(FIRST, bank_first[:], 0, C)
 
         early = multiply_last(0, rectified_last, 0, P // 2)

@@ -30,7 +30,7 @@ DMA_ALIGN = 512
 STAGING_BUFS = 9
 LAST_BUFS = 16
 CODES_BUFS = 5
-SUM_BANKS = 6
+SUM_BANKS = (4, 2)
 SHORT_BANKS = 2
 
 
@@ -65,7 +65,7 @@ def tile_routed_moe_kernel(tc, xT, w1, w3, w2, gate, offs, out):
         keep = ctx.enter_context(tc.tile_pool(name="keep", bufs=1))
         stage = ctx.enter_context(tc.tile_pool(name="stage", bufs=CODES_BUFS))
         small = ctx.enter_context(tc.tile_pool(name="small", bufs=E))
-        psum = ctx.enter_context(tc.psum_pool(name="psum", bufs=SUM_BANKS + SHORT_BANKS))
+        psum = ctx.enter_context(tc.psum_pool(name="psum", bufs=sum(SUM_BANKS) + SHORT_BANKS))
 
         def staging(shape, dtype, name):
             return stage.tile(shape, dtype, name=name, tag="staging", align_bytes=64, bufs=STAGING_BUFS)
@@ -222,7 +222,7 @@ def tile_routed_moe_kernel(tc, xT, w1, w3, w2, gate, offs, out):
         def passes_of_w1(e, g, quarters):
             for u in range(2):
                 if g == 0:
-                    sums[e, W1, u] = psum.tile([P, 2, C], F32, name="sums", bufs=SUM_BANKS)
+                    sums[e, W1, u] = psum.tile([P, 2, C], F32, name=f"sums{e}", bufs=SUM_BANKS[e])
                 for v in range(2):
                     one_pass(
                         sums[e, W1, u][:, v, :],
@@ -235,7 +235,7 @@ def tile_routed_moe_kernel(tc, xT, w1, w3, w2, gate, offs, out):
 
         def pass_of_w3(e, g, s, t, quarter):
             if g == 0 and t == 0:
-                sums[e, W3, s] = psum.tile([P, J, P], F32, name="sums", bufs=SUM_BANKS)
+                sums[e, W3, s] = psum.tile([P, J, P], F32, name=f"sums{e}", bufs=SUM_BANKS[e])
             one_pass(
                 sums[e, W3, s][:, t, :],
                 quarter,
@@ -256,7 +256,9 @@ def tile_routed_moe_kernel(tc, xT, w1, w3, w2, gate, offs, out):
 
         def finish_by_halves(e, g, tile):
             quarters = quantise_quarters(tile, staging, 0, 2) + quantise_quarters(tile, staging, 2, J)
-            passes_of_w3(e, g, quarters)
+            for s in range(GROUPS):
+                for t in range(J):
+                    pass_of_w3(e, g, s, t, quarters[t])
 
         def rectify(e):
             tile = staging([P, C * J], F32, "rectified")

@@ -94,7 +94,7 @@ def tile_routed_moe_kernel(tc, xT, w1, w3, w2, gate, offs, out):
             else:
                 tile = keep.tile([P, J, H], F32, name=f"w_raw{e}{m}{g}", align_bytes=DMA_ALIGN)
             nc.sync.dma_start(out=tile[:], in_=w_views[m][e, g])
-            w_raw[e, m, g] = tile
+            w_raw[e, m, g] = tile[:]
 
         def load_w2(e):
             w2_raw[e] = keep.tile([P, J, N], F32, name=f"w2_raw{e}", align_bytes=DMA_ALIGN)
@@ -111,9 +111,12 @@ def tile_routed_moe_kernel(tc, xT, w1, w3, w2, gate, offs, out):
             nc.sync.dma_start(out=x_raw[g][:], in_=xT_view[g])
             if g == 0:
                 nc.sync.dma_start(offsets[:], offs)
-        for m in (W1, W3):
-            for g in range(PASSES):
-                load_chunk(FIRST, m, g)
+        pair = keep.tile([P, 2, J, H], F32, name="w_pair", align_bytes=DMA_ALIGN)
+        nc.sync.dma_start(out=pair[:], in_=w1.rearrange("e (g p j) n -> e p g j n", p=P, j=J)[FIRST, :, 0:2])
+        w_raw[FIRST, W1, 0], w_raw[FIRST, W1, 1] = pair[:, 0], pair[:, 1]
+        load_chunk(FIRST, W1, 2)
+        for g in range(PASSES):
+            load_chunk(FIRST, W3, g)
         load_chunk(LAST, W1, 0)
         load_w2(FIRST)
         for g in range(1, PASSES):
@@ -121,9 +124,9 @@ def tile_routed_moe_kernel(tc, xT, w1, w3, w2, gate, offs, out):
         for g in range(PASSES - 1):
             load_chunk(LAST, W3, g)
         halves = []
-        for left in (0, H // 2):
-            tile = keep.tile([P, J, H // 2], F32, name=f"w_half{left}", align_bytes=DMA_ALIGN)
-            nc.sync.dma_start(out=tile[:], in_=w_views[W3][LAST, PASSES - 1, :, :, left : left + H // 2])
+        for left, top, bottom in ((0, 0, J), (H // 2, 0, 2), (H // 2, 2, J)):
+            tile = keep.tile([P, bottom - top, H // 2], F32, name=f"w_half{left}{top}", align_bytes=DMA_ALIGN)
+            nc.sync.dma_start(out=tile[:], in_=w_views[W3][LAST, PASSES - 1, :, top:bottom, left : left + H // 2])
             halves.append(loaded_by_quarter(tile[:]))
         load_w2(LAST)
         load_gate(FIRST)
@@ -197,7 +200,7 @@ def tile_routed_moe_kernel(tc, xT, w1, w3, w2, gate, offs, out):
         def round_chunk(e, m, g, on_vector):
             tile = staging([P, H * J], BF16, "w_interleaved")
             target = interleaved_by_quarter(tile[:])
-            source = loaded_by_quarter(w_raw[e, m, g][:])
+            source = loaded_by_quarter(w_raw[e, m, g])
             round_quarters(nc.vector.tensor_copy, target, source, 0, on_vector)
             round_quarters(nc.scalar.copy, target, source, on_vector, J)
             return tile
@@ -313,16 +316,19 @@ def tile_routed_moe_kernel(tc, xT, w1, w3, w2, gate, offs, out):
         round_quarters(nc.vector.tensor_copy, target, halves[0], 0, 2)
         round_quarters(nc.scalar.copy, target, halves[0], 2, J)
         passes_of_w3(LAST, 1, quarters_before + quantise_quarters(before, staging, 2, J))
+        late = staging([P, H // 2 * J], BF16, "w_interleaved")
+        target = interleaved_by_quarter(late[:])
+        round_quarters(nc.vector.tensor_copy, target[:, :, :, 0:2], halves[1], 0, 2)
+        round_quarters(nc.scalar.copy, target[:, :, :, 0:2], halves[1], 2, J)
         quarters = []
         for t in range(J):
             words = last_ring([P, P], U32, "w_words")
             scales = stage.tile([P, P], U8, name="w_bytes", align_bytes=64, bufs=8)
             quantise(words[:, :width], scales[:, :width], tile[:, t * width * J : (t + 1) * width * J])
             quarters.append((words[:], scales[:]))
-        tile = staging([P, H // 2 * J], BF16, "w_interleaved")
-        target = interleaved_by_quarter(tile[:])
+        tile = late
         for t in range(J):
-            round_quarters(nc.vector.tensor_copy if t < 2 else nc.scalar.copy, target, halves[1], t, t + 1)
+            round_quarters(nc.vector.tensor_copy if t < 2 else nc.scalar.copy, target[:, :, :, 2:J], halves[2], t, t + 1)
         for t in QUARTER_ORDER:
             words, scales = quarters[t]
             quantise(words[:, width:], scales[:, width:], tile[:, t * width * J : (t + 1) * width * J])

@@ -24,7 +24,7 @@ RUN = 4
 LIST_COLUMN = 16
 W1, W3 = 0, 1
 FIRST, LAST = 0, 1
-QUARTER_ORDER = (0, 2, 1, 3)
+QUARTER_ORDER = (0, 1, 3, 2)
 
 DMA_ALIGN = 512
 STAGING_BUFS = 9
@@ -245,7 +245,7 @@ def tile_routed_moe_kernel(tc, xT, w1, w3, w2, gate, offs, out):
                 g,
                 slice(e * C + s * P, e * C + (s + 1) * P),
                 g == 0 and t == 0,
-                g == PASSES - 1 and t == J - 1,
+                g == PASSES - 1 and t == (QUARTER_ORDER[-1] if e == LAST else J - 1),
             )
 
         def passes_of_w3(e, g, quarters):
@@ -328,7 +328,7 @@ def tile_routed_moe_kernel(tc, xT, w1, w3, w2, gate, offs, out):
             quarters.append((words[:], scales[:]))
         tile = late
         for t in range(J):
-            round_quarters(nc.vector.tensor_copy if t < 2 else nc.scalar.copy, target[:, :, :, 2:J], halves[2], t, t + 1)
+            round_quarters(nc.vector.tensor_copy if t < 3 else nc.scalar.copy, target[:, :, :, 2:J], halves[2], t, t + 1)
         for t in QUARTER_ORDER:
             words, scales = quarters[t]
             quantise(words[:, width:], scales[:, width:], tile[:, t * width * J : (t + 1) * width * J])

@@ -27,6 +27,7 @@ FIRST, LAST = 0, 1
 QUARTER_ORDER = (0, 1, 3, 2)
 
 DMA_ALIGN = 512
+MX_ALIGN = 256
 STAGING_BUFS = 9
 LAST_BUFS = 16
 CODES_BUFS = 5
@@ -68,13 +69,13 @@ def tile_routed_moe_kernel(tc, xT, w1, w3, w2, gate, offs, out):
         psum = ctx.enter_context(tc.psum_pool(name="psum", bufs=sum(SUM_BANKS) + SHORT_BANKS))
 
         def staging(shape, dtype, name):
-            return stage.tile(shape, dtype, name=name, tag="staging", align_bytes=64, bufs=STAGING_BUFS)
+            return stage.tile(shape, dtype, name=name, tag="staging", align_bytes=MX_ALIGN, bufs=STAGING_BUFS)
 
         def codes_ring(shape, dtype, name):
-            return stage.tile(shape, dtype, name=name, tag="codes", align_bytes=64)
+            return stage.tile(shape, dtype, name=name, tag="codes", align_bytes=MX_ALIGN)
 
         def last_ring(shape, dtype, name):
-            return small.tile(shape, dtype, name=name, tag="last", align_bytes=64, bufs=LAST_BUFS)
+            return small.tile(shape, dtype, name=name, tag="last", align_bytes=MX_ALIGN, bufs=LAST_BUFS)
 
         def short_bank(shape):
             return psum.tile(shape, F32, name="short", bufs=SHORT_BANKS)
@@ -133,11 +134,11 @@ def tile_routed_moe_kernel(tc, xT, w1, w3, w2, gate, offs, out):
         load_gate(LAST)
 
         slot_words = {}
-        token_bytes = keep.tile([P, T], U8, name="token_bytes", align_bytes=64)
-        slot_bytes = keep.tile([P, SLOTS], U8, name="slot_bytes", align_bytes=64)
+        token_bytes = keep.tile([P, T], U8, name="token_bytes", align_bytes=MX_ALIGN)
+        slot_bytes = keep.tile([P, SLOTS], U8, name="slot_bytes", align_bytes=MX_ALIGN)
         for g in range(PASSES):
-            token_words = keep.tile([P, T], U32, name=f"token_words{g}", align_bytes=64)
-            slot_words[g] = keep.tile([P, SLOTS], U32, name=f"slot_words{g}", align_bytes=64)
+            token_words = keep.tile([P, T], U32, name=f"token_words{g}", align_bytes=MX_ALIGN)
+            slot_words[g] = keep.tile([P, SLOTS], U32, name=f"slot_words{g}", align_bytes=MX_ALIGN)
             for half, copy in enumerate((nc.vector.tensor_copy, nc.scalar.copy)):
                 tokens = slice(half * T // 2, (half + 1) * T // 2)
                 interleaved = staging([P, T // 2 * J], BF16, "x_interleaved")
@@ -163,12 +164,12 @@ def tile_routed_moe_kernel(tc, xT, w1, w3, w2, gate, offs, out):
             return tile
 
         def quantise_w2(e, words, interleaved):
-            scales = small.tile([P, N], U8, name="w2_bytes", align_bytes=64)
+            scales = small.tile([P, N], U8, name="w2_bytes", align_bytes=MX_ALIGN)
             quantise(words[:], scales[:], interleaved[:])
             w2_codes[e] = (words, scales)
 
         def quantise_hidden(words, interleaved):
-            scales = small.tile(list(words.shape), U8, name="h_bytes", align_bytes=64, bufs=2 + GROUPS)
+            scales = small.tile(list(words.shape), U8, name="h_bytes", align_bytes=MX_ALIGN, bufs=2 + GROUPS)
             quantise(words[:], scales[:], interleaved[:])
             return words, scales
 
@@ -207,7 +208,7 @@ def tile_routed_moe_kernel(tc, xT, w1, w3, w2, gate, offs, out):
 
         def quantise_quarters(tile, ring, first, last):
             words = ring([P, (last - first) * P], U32, "w_words")
-            scales = stage.tile([P, (last - first) * P], U8, name="w_bytes", align_bytes=64, bufs=8)
+            scales = stage.tile([P, (last - first) * P], U8, name="w_bytes", align_bytes=MX_ALIGN, bufs=8)
             quantise(words[:], scales[:], tile[:, first * H : last * H])
             return [(words[:, n : n + P], scales[:, n : n + P]) for n in range(0, (last - first) * P, P)]
 
@@ -297,8 +298,8 @@ def tile_routed_moe_kernel(tc, xT, w1, w3, w2, gate, offs, out):
         hidden_first = staging([P, C * J], BF16, "hidden_first")
         for s in range(GROUPS):
             multiply(FIRST, s, hidden_first[:, s * H : (s + 1) * H], rectified_first, 0, P)
-        quantise_w2(FIRST, keep.tile([P, N], U32, name="w2_words", align_bytes=64), w2_first)
-        codes_first = quantise_hidden(keep.tile([P, C], U32, name="h_words", align_bytes=64), hidden_first)
+        quantise_w2(FIRST, keep.tile([P, N], U32, name="w2_words", align_bytes=MX_ALIGN), w2_first)
+        codes_first = quantise_hidden(keep.tile([P, C], U32, name="h_words", align_bytes=MX_ALIGN), hidden_first)
         bank_first = short_bank([P, C])
         second_layer(FIRST, bank_first[:], *codes_first)
         finish_chunk(LAST, W1, 1, tile)
@@ -323,7 +324,7 @@ def tile_routed_moe_kernel(tc, xT, w1, w3, w2, gate, offs, out):
         quarters = []
         for t in range(J):
             words = last_ring([P, P], U32, "w_words")
-            scales = stage.tile([P, P], U8, name="w_bytes", align_bytes=64, bufs=8)
+            scales = stage.tile([P, P], U8, name="w_bytes", align_bytes=MX_ALIGN, bufs=8)
             quantise(words[:, :width], scales[:, :width], tile[:, t * width * J : (t + 1) * width * J])
             quarters.append((words[:], scales[:]))
         tile = late

from contextlib import ExitStack

import concourse.mybir as mybir

K, T, E, C, H, N = 1536, 1024, 2, 256, 512, 128
FLOPS = 2 * E * C * (2 * K * H + H * N)

F32 = mybir.dt.float32
BF16 = mybir.dt.bfloat16
U32 = mybir.dt.uint32
U16 = mybir.dt.uint16
U8 = mybir.dt.uint8
FP8X4 = mybir.dt.float8_e4m3fn_x4
MULT = mybir.AluOpType.mult
RELU = mybir.ActivationFunctionType.Relu
COPY = mybir.ActivationFunctionType.Copy

P = 128
J = 4
PASSES = K // (P * J)
SLOTS = E * C
GROUPS = C // P
RUN = 4
LIST_COLUMN = 16
W1, W3 = 0, 1
FIRST, LAST = 0, 1
QUARTER_ORDER = (0, 1, 3, 2)

DMA_ALIGN = 512
MX_ALIGN = 256
STAGING_BUFS = 9
LAST_BUFS = 16
CODES_BUFS = 5
SUM_BANKS = (4, 2)
SHORT_BANKS = 2


def tile_routed_moe_kernel(tc, xT, w1, w3, w2, gate, offs, out):
    nc = tc.nc
    xT_view = xT.rearrange("(g p j) n -> g p j n", p=P, j=J)
    w_views = [w.rearrange("e (g p j) n -> e g p j n", p=P, j=J) for w in (w1, w3)]
    w2_by_quarter = w2.rearrange("e (m u l v) n -> e l m u (v n)", u=2, l=2, v=2)

    def loaded_order(ap):
        return ap.rearrange("p j (c r) -> p c j r", r=RUN)

    def interleaved_order(ap):
        return ap.rearrange("p (c r j) -> p c j r", r=RUN, j=J)

    def loaded_by_quarter(ap):
        return ap.rearrange("p j (m u l v) -> p u m j l v", u=2, l=2, v=2)

    def interleaved_by_quarter(ap):
        return ap.rearrange("p (u v m l j) -> p u m j l v", u=2, v=2, l=2, j=J)

    def sums_by_slot_pair(ap):
        return ap.rearrange("p t (c r) -> p c t r", r=2)

    def stored_by_slot_pair(ap):
        return ap.rearrange("p (c t r) -> p c t r", t=J, r=2)

    def interleaved_by_slot_pair(ap):
        return ap.rearrange("p (c r t) -> p c t r", t=J, r=2)

    with ExitStack() as ctx:
        keep = ctx.enter_context(tc.tile_pool(name="keep", bufs=1))
        stage = ctx.enter_context(tc.tile_pool(name="stage", bufs=CODES_BUFS))
        small = ctx.enter_context(tc.tile_pool(name="small", bufs=E))
        psum = ctx.enter_context(tc.psum_pool(name="psum", bufs=sum(SUM_BANKS) + SHORT_BANKS))

        def staging(shape, dtype, name):
            return stage.tile(shape, dtype, name=name, tag="staging", align_bytes=MX_ALIGN, bufs=STAGING_BUFS)

        def codes_ring(shape, dtype, name):
            return stage.tile(shape, dtype, name=name, tag="codes", align_bytes=MX_ALIGN)

        def last_ring(shape, dtype, name):
            return small.tile(shape, dtype, name=name, tag="last", align_bytes=MX_ALIGN, bufs=LAST_BUFS)

        def short_bank(shape):
            return psum.tile(shape, F32, name="short", bufs=SHORT_BANKS)

        offsets = keep.tile([P, SLOTS // LIST_COLUMN], U16, name="offsets", align_bytes=DMA_ALIGN)
        window = keep.tile([P, T], F32, name="window", align_bytes=DMA_ALIGN)
        nc.vector.memset(window[:], 0.0)

        x_raw = {}
        w_raw = {}
        w2_raw = {}
        gates = {}

        def load_chunk(e, m, g):
            if (e, m) == (LAST, W3):
                tile = stage.tile([P, J, H], F32, name="w_raw", tag="raw", bufs=PASSES, align_bytes=DMA_ALIGN)
            else:
                tile = keep.tile([P, J, H], F32, name=f"w_raw{e}{m}{g}", align_bytes=DMA_ALIGN)
            nc.sync.dma_start(out=tile[:], in_=w_views[m][e, g])
            w_raw[e, m, g] = tile[:]

        def load_w2(e):
            w2_raw[e] = keep.tile([P, J, N], F32, name=f"w2_raw{e}", align_bytes=DMA_ALIGN)
            for l in range(2):
                rows = w2_raw[e][l::2].rearrange("p (u v) n -> p u (v n)", v=2)
                nc.sync.dma_start(out=rows, in_=w2_by_quarter[e, l])

        def load_gate(e):
            gates[e] = keep.tile([P, C], F32, name=f"gates{e}", align_bytes=DMA_ALIGN)
            nc.sync.dma_start(out=gates[e][:], in_=gate[:, e * C : (e + 1) * C])

        for g in range(PASSES):
            x_raw[g] = stage.tile([P, J, T], F32, name="x_raw", tag="raw", bufs=PASSES, align_bytes=DMA_ALIGN)
            nc.sync.dma_start(out=x_raw[g][:], in_=xT_view[g])
            if g == 0:
                nc.sync.dma_start(offsets[:], offs)
        pair = keep.tile([P, 2, J, H], F32, name="w_pair", align_bytes=DMA_ALIGN)
        nc.sync.dma_start(out=pair[:], in_=w1.rearrange("e (g p j) n -> e p g j n", p=P, j=J)[FIRST, :, 0:2])
        w_raw[FIRST, W1, 0], w_raw[FIRST, W1, 1] = pair[:, 0], pair[:, 1]
        load_chunk(FIRST, W1, 2)
        for g in range(PASSES):
            load_chunk(FIRST, W3, g)
        load_chunk(LAST, W1, 0)
        load_w2(FIRST)
        for g in range(1, PASSES):
            load_chunk(LAST, W1, g)
        for g in range(PASSES - 1):
            load_chunk(LAST, W3, g)
        halves = []
        for left, top, bottom in ((0, 0, J), (H // 2, 0, 2), (H // 2, 2, J)):
            tile = keep.tile([P, bottom - top, H // 2], F32, name=f"w_half{left}{top}", align_bytes=DMA_ALIGN)
            nc.sync.dma_start(out=tile[:], in_=w_views[W3][LAST, PASSES - 1, :, top:bottom, left : left + H // 2])
            halves.append(loaded_by_quarter(tile[:]))
        load_w2(LAST)
        load_gate(FIRST)
        load_gate(LAST)

        slot_words = {}
        token_bytes = keep.tile([P, T], U8, name="token_bytes", align_bytes=MX_ALIGN)
        slot_bytes = keep.tile([P, SLOTS], U8, name="slot_bytes", align_bytes=MX_ALIGN)
        for g in range(PASSES):
            token_words = keep.tile([P, T], U32, name=f"token_words{g}", align_bytes=MX_ALIGN)
            slot_words[g] = keep.tile([P, SLOTS], U32, name=f"slot_words{g}", align_bytes=MX_ALIGN)
            for half, copy in enumerate((nc.vector.tensor_copy, nc.scalar.copy)):
                tokens = slice(half * T // 2, (half + 1) * T // 2)
                interleaved = staging([P, T // 2 * J], BF16, "x_interleaved")
                copy(interleaved_order(interleaved[:]), loaded_order(x_raw[g][:, :, tokens]))
                nc.vector.quantize_mx(
                    out=token_words[:, tokens].bitcast(FP8X4),
                    scales=token_bytes[4 * g :, tokens],
                    in_=interleaved[:],
                )
            if g == PASSES - 1:
                nc.vector.tensor_copy(slot_bytes[:], token_bytes[:].indirect(offsets[:]))
            nc.vector.tensor_copy(slot_words[g][:], token_words[:].indirect(offsets[:]))

        sums = {}
        w2_codes = {}

        def quantise(words, scales, interleaved):
            nc.vector.quantize_mx(out=words.bitcast(FP8X4), scales=scales, in_=interleaved)

        def round_w2(e, ring, copy):
            tile = ring([P, N * J], BF16, "w2_interleaved")
            copy(interleaved_order(tile[:]), loaded_order(w2_raw[e][:]))
            return tile

        def quantise_w2(e, words, interleaved):
            scales = small.tile([P, N], U8, name="w2_bytes", align_bytes=MX_ALIGN)
            quantise(words[:], scales[:], interleaved[:])
            w2_codes[e] = (words, scales)

        def quantise_hidden(words, interleaved):
            scales = small.tile(list(words.shape), U8, name="h_bytes", align_bytes=MX_ALIGN, bufs=2 + GROUPS)
            quantise(words[:], scales[:], interleaved[:])
            return words, scales

        def second_layer(e, y, words, scales):
            nc.tensor.matmul_mx(
                out=y,
                lhsT=w2_codes[e][0][:].bitcast(FP8X4),
                lhsT_scale=w2_codes[e][1][:],
                rhs=words[:].bitcast(FP8X4),
                rhs_scale=scales[:],
                start=True,
                stop=True,
            )

        def put_back(e, y, first, last):
            weighed = last_ring([P, last - first], F32, "weighed")
            nc.vector.tensor_tensor(weighed[:], y, gates[e][:, first:last], MULT)
            entries = offsets[:, (e * C + first) // LIST_COLUMN : (e * C + last) // LIST_COLUMN]
            nc.scalar.activation(window[:].indirect(entries), weighed[:], COPY)

        def round_quarters(copy, target, source, first, last):
            for u in range(2):
                own = [t % 2 for t in range(first, last) if t // 2 == u]
                if len(own) == 2:
                    copy(target[:, u], source[:, u])
                elif own:
                    copy(target[:, u, :, :, :, own[0]], source[:, u, :, :, :, own[0]])

        def round_chunk(e, m, g, on_vector):
            tile = staging([P, H * J], BF16, "w_interleaved")
            target = interleaved_by_quarter(tile[:])
            source = loaded_by_quarter(w_raw[e, m, g])
            round_quarters(nc.vector.tensor_copy, target, source, 0, on_vector)
            round_quarters(nc.scalar.copy, target, source, on_vector, J)
            return tile

        def quantise_quarters(tile, ring, first, last):
            words = ring([P, (last - first) * P], U32, "w_words")
            scales = stage.tile([P, (last - first) * P], U8, name="w_bytes", align_bytes=MX_ALIGN, bufs=8)
            quantise(words[:], scales[:], tile[:, first * H : last * H])
            return [(words[:, n : n + P], scales[:, n : n + P]) for n in range(0, (last - first) * P, P)]

        def one_pass(result, quarter, g, slots, start, stop):
            nc.tensor.matmul_mx(
                out=result,
                lhsT=quarter[0].bitcast(FP8X4),
                lhsT_scale=quarter[1],
                rhs=slot_words[g][:, slots].bitcast(FP8X4),
                rhs_scale=slot_bytes[4 * g :, slots],
                start=start,
                stop=stop,
            )

        def passes_of_w1(e, g, quarters):
            for u in range(2):
                if g == 0:
                    sums[e, W1, u] = psum.tile([P, 2, C], F32, name=f"sums{e}", bufs=SUM_BANKS[e])
                for v in range(2):
                    one_pass(
                        sums[e, W1, u][:, v, :],
                        quarters[2 * u + v],
                        g,
                        slice(e * C, (e + 1) * C),
                        g == 0 and v == 0,
                        g == PASSES - 1 and v == 1,
                    )

        def pass_of_w3(e, g, s, t, quarter):
            if g == 0 and t == 0:
                sums[e, W3, s] = psum.tile([P, J, P], F32, name=f"sums{e}", bufs=SUM_BANKS[e])
            one_pass(
                sums[e, W3, s][:, t, :],
                quarter,
                g,
                slice(e * C + s * P, e * C + (s + 1) * P),
                g == 0 and t == 0,
                g == PASSES - 1 and t == (QUARTER_ORDER[-1] if e == LAST else J - 1),
            )

        def passes_of_w3(e, g, quarters):
            for t in range(J):
                for s in range(GROUPS):
                    pass_of_w3(e, g, s, t, quarters[t])

        def finish_chunk(e, m, g, tile):
            quarters = quantise_quarters(tile, codes_ring, 0, J)
            (passes_of_w1, passes_of_w3)[m](e, g, quarters)

        def finish_by_halves(e, g, tile):
            quarters = quantise_quarters(tile, staging, 0, 2) + quantise_quarters(tile, staging, 2, J)
            for s in range(GROUPS):
                for t in range(J):
                    pass_of_w3(e, g, s, t, quarters[t])

        def rectify(e):
            tile = staging([P, C * J], F32, "rectified")
            target = stored_by_slot_pair(tile[:])
            for u in range(2):
                nc.scalar.activation(target[:, :, 2 * u : 2 * u + 2], sums_by_slot_pair(sums[e, W1, u][:]), RELU)
            return tile

        def multiply(e, s, target, rectified, first, last):
            nc.vector.tensor_tensor(
                interleaved_by_slot_pair(target),
                sums_by_slot_pair(sums[e, W3, s][:, :, first:last]),
                stored_by_slot_pair(rectified[:, (s * P + first) * J : (s * P + last) * J]),
                MULT,
            )

        def multiply_last(s, rectified, first, last):
            tile = last_ring([P, (last - first) * J], BF16, "hidden_last")
            multiply(LAST, s, tile[:], rectified, first, last)
            return tile

        for g in range(PASSES):
            finish_chunk(FIRST, W1, g, round_chunk(FIRST, W1, g, 1 if g < PASSES - 1 else 2))
        finish_chunk(FIRST, W3, 0, round_chunk(FIRST, W3, 0, 2))
        tile = round_chunk(FIRST, W3, 1, 3)
        rectified_first = rectify(FIRST)
        finish_chunk(FIRST, W3, 1, tile)
        finish_chunk(FIRST, W3, 2, round_chunk(FIRST, W3, 2, 2))

        finish_chunk(LAST, W1, 0, round_chunk(LAST, W1, 0, 2))
        w2_first = round_w2(FIRST, staging, nc.scalar.copy)
        tile = round_chunk(LAST, W1, 1, 1)
        hidden_first = staging([P, C * J], BF16, "hidden_first")
        for s in range(GROUPS):
            multiply(FIRST, s, hidden_first[:, s * H : (s + 1) * H], rectified_first, 0, P)
        quantise_w2(FIRST, keep.tile([P, N], U32, name="w2_words", align_bytes=MX_ALIGN), w2_first)
        codes_first = quantise_hidden(keep.tile([P, C], U32, name="h_words", align_bytes=MX_ALIGN), hidden_first)
        bank_first = short_bank([P, C])
        second_layer(FIRST, bank_first[:], *codes_first)
        finish_chunk(LAST, W1, 1, tile)
        finish_chunk(LAST, W1, 2, round_chunk(LAST, W1, 2, 2))

        tile = round_chunk(LAST, W3, 0, 3)
        rectified_last = rectify(LAST)
        finish_by_halves(LAST, 0, tile)
        before = round_chunk(LAST, W3, 1, 2)
        quarters_before = quantise_quarters(before, staging, 0, 2)

        width = P // 2
        tile = staging([P, H // 2 * J], BF16, "w_interleaved")
        target = interleaved_by_quarter(tile[:])
        round_quarters(nc.vector.tensor_copy, target, halves[0], 0, 2)
        round_quarters(nc.scalar.copy, target, halves[0], 2, J)
        passes_of_w3(LAST, 1, quarters_before + quantise_quarters(before, staging, 2, J))
        late = staging([P, H // 2 * J], BF16, "w_interleaved")
        target = interleaved_by_quarter(late[:])
        round_quarters(nc.vector.tensor_copy, target[:, :, :, 0:2], halves[1], 0, 2)
        round_quarters(nc.scalar.copy, target[:, :, :, 0:2], halves[1], 2, J)
        quarters = []
        for t in range(J):
            words = last_ring([P, P], U32, "w_words")
            scales = stage.tile([P, P], U8, name="w_bytes", align_bytes=MX_ALIGN, bufs=8)
            quantise(words[:, :width], scales[:, :width], tile[:, t * width * J : (t + 1) * width * J])
            quarters.append((words[:], scales[:]))
        tile = late
        for t in range(J):
            round_quarters(nc.vector.tensor_copy if t < 3 else nc.scalar.copy, target[:, :, :, 2:J], halves[2], t, t + 1)
        for t in QUARTER_ORDER:
            words, scales = quarters[t]
            quantise(words[:, width:], scales[:, width:], tile[:, t * width * J : (t + 1) * width * J])
        for s in range(GROUPS):
            for t in QUARTER_ORDER:
                pass_of_w3(LAST, PASSES - 1, s, t, quarters[t])
        w2_last = round_w2(LAST, last_ring, nc.scalar.copy)
        put_back(FIRST, bank_first[:], 0, C)

        early = multiply_last(0, rectified_last, 0, P // 2)
        late = multiply_last(0, rectified_last, P // 2, P)
        codes_early = quantise_hidden(last_ring([P, P // 2], U32, "h_words_last"), early)
        quantise_w2(LAST, last_ring([P, N], U32, "w2_words_last"), w2_last)
        codes_late = quantise_hidden(last_ring([P, P // 2], U32, "h_words_last"), late)
        bank = short_bank([P, P])
        second_layer(LAST, bank[:, : P // 2], *codes_early)
        second_layer(LAST, bank[:, P // 2 :], *codes_late)
        hidden = multiply_last(1, rectified_last, 0, P)
        put_back(LAST, bank[:], 0, P)
        codes = quantise_hidden(last_ring([P, P], U32, "h_words_last"), hidden)
        bank = short_bank([P, P])
        second_layer(LAST, bank[:], *codes)
        put_back(LAST, bank[:], P, C)
        nc.sync.dma_start(out=out, in_=window[:])
